import numpy as np
import ml_dtypes


def mxq(x, axis, fmt="e4m3"):
    dtype, down = {"e4m3": (ml_dtypes.float8_e4m3fn, 7), "e5m2": (ml_dtypes.float8_e5m2, 14)}[fmt]
    v = np.moveaxis(np.asarray(x, np.float32).astype(ml_dtypes.bfloat16).astype(np.float64), axis, -1)
    blocks = v.reshape(v.shape[:-1] + (-1, 32))
    amax = np.abs(blocks).max(-1, keepdims=True)
    byte = np.maximum(np.where(amax > 0, np.frexp(amax)[1] - 1 + 127, 0) - down, 1)
    scale = np.exp2(byte - 127.0)
    codes = (blocks / scale).astype(np.float32).astype(dtype).astype(np.float64)
    return np.moveaxis((codes * scale).reshape(v.shape), -1, axis)


WIDE = False


def mx_kscale(k):
    if not WIDE:
        return np.ones(k)
    levels = np.array([10, -10, 5, -5, 0])
    if k % 512:
        return np.exp2(np.random.permutation(np.resize(levels, k // 32))).repeat(32)
    a = np.empty((k // 512, 16))
    for p in range(k // 512):
        a[p, :8] = np.random.permutation(np.resize(levels, 8))
        for g in range(8):
            far = levels[np.abs(levels - a[p, g]) >= 10]
            a[p, g + 8] = far[np.random.randint(len(far))]
    return np.exp2(a.ravel()).repeat(32)


def f64(x):
    return np.asarray(x).astype(np.float64)


def striped(idx):
    return np.tile(idx.reshape(-1, 16).T, (8, 1)).astype(np.uint16)


def unstriped(offs):
    return offs[:16].T.reshape(-1).astype(np.int64)


E2M1 = np.array([0.0, 0.5, 1.0, 1.5, 2.0, 3.0, 4.0, 6.0, -0.0, -0.5, -1.0, -1.5, -2.0, -3.0, -4.0, -6.0])


def pack_weight(w, fmt):
    k, n = w.shape
    w = f64(np.asarray(w, np.float32).astype(ml_dtypes.bfloat16)).reshape(k // 32, 32, n)
    amax = np.abs(w).max(1)
    if fmt == "e4m3":
        byte = np.frexp(amax)[1] - 1 + 127 - 7
    else:
        mant, ex = np.frexp(amax / 6.0)
        byte = np.where(mant > 0.5, ex, ex - 1) + 127
    byte = np.clip(np.where(amax > 0, byte, 1), 1, 254)
    scaled = (w * np.exp2(127.0 - byte)[:, None, :]).reshape(k, n).astype(np.float32)
    by_word = np.ascontiguousarray(scaled.reshape(k // 512, 128, 4, n).transpose(0, 1, 3, 2))
    if fmt == "e4m3":
        words = by_word.astype(ml_dtypes.float8_e4m3fn).view(np.uint8)
    else:
        c = by_word.astype(ml_dtypes.float4_e2m1fn).view(np.uint8) & 0xF
        words = (c[..., 0::2] | (c[..., 1::2] << 4)).reshape(k // 512, 128, 2 * n)
    return np.ascontiguousarray(words), np.ascontiguousarray(byte.astype(np.uint8).reshape(k // 512, 16, n))


def unpack_weight(words, scales, fmt):
    g, _, n = scales.shape
    words = np.ascontiguousarray(words).reshape(g, 128, n, -1)
    if fmt == "e4m3":
        vals = words.view(ml_dtypes.float8_e4m3fn).astype(np.float64)
    else:
        nib = np.empty((g, 128, n, 4), np.uint8)
        nib[..., 0::2] = words & 0xF
        nib[..., 1::2] = words >> 4
        vals = E2M1[nib]
    vals = vals * np.repeat(np.exp2(scales.astype(np.float64) - 127.0), 8, axis=1)[..., None]
    return vals.transpose(0, 1, 3, 2).reshape(g * 512, n)


def gelu(v):
    return 0.5 * v * (1.0 + np.tanh(np.sqrt(2.0 / np.pi) * (v + 0.044715 * v**3)))


K, T, E, C, H, N = 512, 640, 8, 128, 512, 256
TOP = 4
PAD = 64


def by_expert(wq, xq):
    return np.concatenate([wq[e].T @ xq[:, e * C:(e + 1) * C] for e in range(E)], axis=1)


def setup_inputs():
    n = np.random.standard_normal
    s = mx_kscale(K)[:, None]
    u = mx_kscale(H)
    slot_token = np.empty(E * C, np.int64); pos = np.tile(E * C + np.arange(T) % PAD, (TOP, 1)); taken = np.zeros(T, np.int64)
    liked = np.random.randn(T)
    for e in np.random.permutation(E):
        free = np.flatnonzero(taken < TOP); pick = np.random.permutation(free[np.argsort(-(liked[free] + np.random.gumbel(size=free.size)))[:C]]); slot_token[e * C:(e + 1) * C] = pick
        pos[taken[pick], pick] = e * C + np.arange(C); taken[pick] += 1
    g = np.random.uniform(0.2, 0.8, (TOP, T))
    w1 = [pack_weight(m, "e2m1") for m in n((E, K, H)) / np.sqrt(K) / s[None] * u[None, None, :]]
    w2 = [pack_weight(m, "e2m1") for m in n((E, H, N)) / np.sqrt(H) / u[None, :, None]]
    return {
        "xT": (n((K, T)) * s).astype(np.float32),
        "w1_words": np.stack([m[0] for m in w1]),
        "w1_scales": np.stack([m[1] for m in w1]),
        "w2_words": np.stack([m[0] for m in w2]),
        "w2_scales": np.stack([m[1] for m in w2]),
        "gate": np.stack([np.tile(r, (N, 1)) for r in g]).astype(np.float32),
        "offs": striped(slot_token),
        "pos1": striped(pos[0]),
        "pos2": striped(pos[1]),
        "pos3": striped(pos[2]),
        "pos4": striped(pos[3]),
    }


def reference(xT, w1_words, w1_scales, w2_words, w2_scales, gate, offs, pos1, pos2, pos3, pos4):
    idx = unstriped(offs)
    w1 = np.stack([unpack_weight(w1_words[e], w1_scales[e], "e2m1") for e in range(E)])
    w2 = np.stack([unpack_weight(w2_words[e], w2_scales[e], "e2m1") for e in range(E)])
    xq = mxq(f64(xT)[:, idx], 0, "e4m3")
    h = gelu(by_expert(w1, xq))
    y = by_expert(w2, mxq(h, 0, "e4m3"))
    y = np.concatenate([y, np.zeros((N, PAD))], axis=1)
    return sum(f64(gate[r]) * y[:, unstriped(p)] for r, p in enumerate((pos1, pos2, pos3, pos4)))

@@ -1,0 +1,210 @@
+from contextlib import ExitStack
+
+import concourse.mybir as mybir
+from concourse.masks import make_identity
+
+K, T, E, C, H, N = 512, 640, 8, 128, 512, 256
+TOP, PAD = 4, 64
+S = E * C
+P = 128
+FLOPS = 2 * S * (K * H + H * N)
+
+F32 = mybir.dt.float32
+BF16 = mybir.dt.bfloat16
+I32 = mybir.dt.int32
+U32 = mybir.dt.uint32
+U16 = mybir.dt.uint16
+U8 = mybir.dt.uint8
+FP8X4 = mybir.dt.float8_e4m3fn_x4
+FP4X4 = mybir.dt.float4_e2m1fn_x4
+GELU = mybir.ActivationFunctionType.Gelu_apprx_tanh
+MULT = mybir.AluOpType.mult
+ADD = mybir.AluOpType.add
+
+X_CHUNKS = [(0, 256), (256, 512), (512, 640)]
+GATHERS = [(0, 128), (128, 256), (256, 512), (512, 768), (768, 896), (896, 1024)]
+T_PARTS = [(0, 384), (384, 640)]
+
+
+def tile_moe_ecr_mlp_gelu_kernel(
+    tc, xT, w1_words, w1_scales, w2_words, w2_scales, gate, offs, pos1, pos2, pos3, pos4, out
+):
+    nc = tc.nc
+    with ExitStack() as ctx:
+        keep = ctx.enter_context(tc.tile_pool(name="keep", bufs=1))
+        psum = ctx.enter_context(tc.psum_pool(name="psum", bufs=8))
+
+        def bank():
+            return psum.tile([P, 512], F32, name="bank")
+
+        def sb(name, shape, dtype):
+            return keep.tile(shape, dtype, name=name, align_bytes=64)
+
+        offs_sb = keep.tile([P, S // 16], U16, name="offs_sb")
+        nc.sync.dma_start(offs_sb[:], offs)
+        x_rows = xT.rearrange("(p j) t -> p j t", j=4)
+        x_raw = []
+        for c, (a, b) in enumerate(X_CHUNKS):
+            raw = sb(f"x_raw{c}", [P, 4, b - a], F32)
+            nc.sync.dma_start(raw[:], x_rows[:, :, a:b])
+            x_raw.append(raw)
+
+        w1_plane = sb("w1_plane", [P, E * H], U8)
+        w2_plane = sb("w2_plane", [P, E * N], U8)
+        x_bytes = sb("x_bytes", [P, T], U8)
+        nc.vector.memset(w1_plane[:].bitcast(I32), 0)
+        nc.vector.memset(w2_plane[:].bitcast(I32), 0)
+        nc.vector.memset(x_bytes[:].bitcast(I32), 0)
+        y = [sb(f"y{h}", [P, S + PAD], F32) for h in range(2)]
+        nc.vector.memset(y[1][:, S:], 0.0)
+        nc.scalar.activation(y[0][:, S:], y[1][:, S:], GELU)
+        ident = sb("ident", [P, P], F32)
+        make_identity(nc, ident[:])
+
+        def load_plane(plane, scales):
+            for r in range(4):
+                nc.sync.dma_start(
+                    plane[r:P:32, :].bitcast(I32).rearrange("q (e w) -> q e w", e=E),
+                    scales[:, 0, r:16:4, :].bitcast(I32).rearrange("e q w -> q e w"),
+                )
+
+        def load_words(name, words, e0, e1):
+            tile = sb(name, [P, e1 - e0, words.shape[3]], U8)
+            nc.sync.dma_start(
+                tile[:].bitcast(I32), words[e0:e1, 0].bitcast(I32).rearrange("e p w -> p e w")
+            )
+            return [tile[:, e, :] for e in range(e1 - e0)]
+
+        load_plane(w1_plane, w1_scales)
+        w1 = []
+        for e0 in range(0, E, 2):
+            w1.extend(load_words(f"w1_{e0}", w1_words, e0, e0 + 2))
+        load_plane(w2_plane, w2_scales)
+        w2 = load_words("w2_0", w2_words, 0, 4) + load_words("w2_4", w2_words, 4, 8)
+        pos = []
+        for r, src in enumerate((pos1, pos2, pos3, pos4)):
+            tile = keep.tile([P, T // 16], U16, name=f"pos_sb{r}")
+            nc.sync.dma_start(tile[:], src)
+            pos.append(tile)
+        gates = {}
+        for h in range(2):
+            for r0 in (0, 2):
+                tile = sb(f"gate{h}{r0}", [P, 2, T], F32)
+                nc.sync.dma_start(
+                    tile[:], gate[r0 : r0 + 2, h * P : (h + 1) * P, :].rearrange("r p t -> p r t")
+                )
+                gates[h, r0] = tile[:, 0, :]
+                gates[h, r0 + 1] = tile[:, 1, :]
+
+        x_words = sb("x_words", [P, T], U32)
+        for c, (a, b) in enumerate(X_CHUNKS):
+            grouped = sb(f"x_bf{c}", [P, b - a, 4], BF16)
+            nc.vector.tensor_copy(
+                grouped[:].rearrange("p (c i) j -> p c j i", i=4),
+                x_raw[c][:].rearrange("p j (c i) -> p c j i", i=4),
+            )
+            nc.vector.quantize_mx(
+                out=x_words[:, a:b].bitcast(FP8X4),
+                scales=x_bytes[:, a:b],
+                in_=grouped[:].rearrange("p t j -> p (t j)"),
+            )
+        slot_words = sb("slot_words", [P, S], U32)
+        slot_bytes = sb("slot_bytes", [P, S], U8)
+        for a, b in GATHERS:
+            nc.vector.tensor_copy(slot_words[:, a:b], x_words[:].indirect(offs_sb[:, a // 16 : b // 16]))
+            nc.vector.tensor_copy(slot_bytes[:, a:b], x_bytes[:].indirect(offs_sb[:, a // 16 : b // 16]))
+
+        turned = []
+        for e in range(E):
+            slots = slice(e * C, (e + 1) * C)
+            acc = bank()
+            nc.tensor.matmul_mx(
+                out=acc[:],
+                lhsT=slot_words[:, slots].bitcast(FP8X4),
+                lhsT_scale=slot_bytes[:, slots],
+                rhs=w1[e].bitcast(FP4X4),
+                rhs_scale=w1_plane[:, e * H : (e + 1) * H],
+                start=True,
+                stop=True,
+            )
+            h_bf = sb(f"h_bf{e}", [P, H], BF16)
+            nc.scalar.activation(
+                h_bf[:].rearrange("s (u p d) -> s u p d", u=2, d=2),
+                acc[:].rearrange("s (p u d) -> s u p d", u=2, d=2),
+                GELU,
+            )
+            if e % 2 == 0:
+                turned.append(bank())
+            pairs = h_bf[:].bitcast(F32)
+            for u in range(2):
+                col = (2 * (e % 2) + u) * P
+                nc.tensor.transpose(turned[-1][:, col : col + P], pairs[:, u * P : (u + 1) * P], ident[:])
+
+        h_words = sb("h_words", [P, S], U32)
+        h_bytes = sb("h_bytes", [P, S], U8)
+        y_acc = []
+        for g in range(E // 2):
+            slots = slice(g * 2 * C, (g + 1) * 2 * C)
+            grouped = sb(f"h_grouped{g}", [P, 2 * C * 4], BF16)
+            dst = grouped[:].bitcast(F32).rearrange("p (e s u) -> p e s u", e=2, u=2)
+            src = turned[g][:].rearrange("p (e u s) -> p e s u", e=2, u=2)
+            if g < 2:
+                nc.vector.tensor_copy(dst, src)
+            else:
+                nc.scalar.copy(dst, src)
+            nc.vector.quantize_mx(out=h_words[:, slots].bitcast(FP8X4), scales=h_bytes[:, slots], in_=grouped[:])
+            acc = bank()
+            for h in range(2):
+                for i in range(2):
+                    e = 2 * g + i
+                    mine = slice(e * C, (e + 1) * C)
+                    nc.tensor.matmul_mx(
+                        out=acc[:, (2 * h + i) * C : (2 * h + i + 1) * C],
+                        lhsT=w2[e][:, 2 * h * P : 2 * (h + 1) * P].bitcast(FP4X4),
+                        lhsT_scale=w2_plane[:, e * N + h * P : e * N + (h + 1) * P],
+                        rhs=h_words[:, mine].bitcast(FP8X4),
+                        rhs_scale=h_bytes[:, mine],
+                        start=True,
+                        stop=True,
+                    )
+            if g < 3:
+                nc.scalar.copy(y[0][:, slots], acc[:, : 2 * C])
+            else:
+                nc.vector.tensor_copy(y[0][:, slots], acc[:, : 2 * C])
+            y_acc.append(acc)
+        for g in range(E // 2):
+            nc.scalar.copy(y[1][:, g * 2 * C : (g + 1) * 2 * C], y_acc[g][:, 2 * C :])
+
+        def fetch(h, r):
+            prod = sb(f"prod{h}{r}", [P, T], F32)
+            nc.vector.tensor_tensor(prod[:], y[h][:].indirect(pos[r][:]), gates[h, r], MULT)
+            return prod
+
+        partial = {}
+        for h in range(2):
+            sums = [bank() for part in T_PARTS]
+            for r in range(TOP - 1):
+                prod = fetch(h, r)
+                for part, (a, b) in enumerate(T_PARTS):
+                    for t0 in range(a, b, P):
+                        nc.tensor.matmul(
+                            sums[part][:, t0 - a : t0 - a + P],
+                            prod[:, t0 : t0 + P],
+                            ident[:],
+                            start=(r == 0 and t0 == a),
+                            stop=(r == TOP - 2 and t0 == b - P),
+                            is_transpose=True,
+                        )
+            for part, (a, b) in enumerate(T_PARTS):
+                flipped = sb(f"flipped{h}{part}", [P, b - a], F32)
+                nc.scalar.copy(flipped[:], sums[part][:, : b - a])
+                back = bank()
+                for t0 in range(0, b - a, P):
+                    nc.tensor.transpose(back[:, t0 : t0 + P], flipped[:, t0 : t0 + P], ident[:])
+                partial[h, part] = back
+        for h in range(2):
+            prod = fetch(h, TOP - 1)
+            for part, (a, b) in enumerate(T_PARTS):
+                res = sb(f"res{h}{part}", [P, b - a], F32)
+                nc.vector.tensor_tensor(res[:], partial[h, part][:, : b - a], prod[:, a:b], ADD)
+                nc.sync.dma_start(out[h * P : (h + 1) * P, a:b], res[:])

@@ -23,7 +23,9 @@ ADD = mybir.AluOpType.add
 
 X_CHUNKS = [(0, 256), (256, 512), (512, 640)]
 GATHERS = [(0, 128), (128, 256), (256, 512), (512, 768), (768, 896), (896, 1024)]
-T_PARTS = [(0, 384), (384, 640)]
+T_PARTS = [(0, 512), (512, 640)]
+H_GROUPS = [(0, 2), (2, 4), (4, 6), (6, 7), (7, 8)]
+COPY = mybir.ActivationFunctionType.Copy
 
 
 def tile_moe_ecr_mlp_gelu_kernel(
@@ -37,17 +39,27 @@ def tile_moe_ecr_mlp_gelu_kernel(
         def bank():
             return psum.tile([P, 512], F32, name="bank")
 
-        def sb(name, shape, dtype):
-            return keep.tile(shape, dtype, name=name, align_bytes=64)
+        def sb(name, shape, dtype, tag=None):
+            return keep.tile(shape, dtype, name=name, tag=tag or name, align_bytes=64)
 
-        offs_sb = keep.tile([P, S // 16], U16, name="offs_sb")
-        nc.sync.dma_start(offs_sb[:], offs)
         x_rows = xT.rearrange("(p j) t -> p j t", j=4)
         x_raw = []
-        for c, (a, b) in enumerate(X_CHUNKS):
-            raw = sb(f"x_raw{c}", [P, 4, b - a], F32)
-            nc.sync.dma_start(raw[:], x_rows[:, :, a:b])
-            x_raw.append(raw)
+
+        def load_x(c):
+            a, b = X_CHUNKS[c]
+            x_raw.append(sb(f"x_raw{c}", [P, 4, b - a], F32))
+            nc.sync.dma_start(x_raw[c][:], x_rows[:, :, a:b])
+
+        load_x(0)
+        pos = []
+        for r, src in enumerate((pos1, pos2, pos3, pos4)):
+            tile = keep.tile([P, T // 16], U16, name=f"pos_sb{r}")
+            nc.sync.dma_start(tile[:], src)
+            pos.append(tile)
+        offs_sb = keep.tile([P, S // 16], U16, name="offs_sb")
+        nc.sync.dma_start(offs_sb[:], offs)
+        load_x(1)
+        load_x(2)
 
         w1_plane = sb("w1_plane", [P, E * H], U8)
         w2_plane = sb("w2_plane", [P, E * N], U8)
@@ -68,54 +80,69 @@ def tile_moe_ecr_mlp_gelu_kernel(
                     scales[:, 0, r:16:4, :].bitcast(I32).rearrange("e q w -> q e w"),
                 )
 
-        def load_words(name, words, e0, e1):
-            tile = sb(name, [P, e1 - e0, words.shape[3]], U8)
+        def load_words(name, words, e0, e1, tag=None):
+            tile = sb(name, [P, e1 - e0, words.shape[3]], U8, tag)
             nc.sync.dma_start(
                 tile[:].bitcast(I32), words[e0:e1, 0].bitcast(I32).rearrange("e p w -> p e w")
             )
             return [tile[:, e, :] for e in range(e1 - e0)]
 
-        load_plane(w1_plane, w1_scales)
-        w1 = []
-        for e0 in range(0, E, 2):
-            w1.extend(load_words(f"w1_{e0}", w1_words, e0, e0 + 2))
-        load_plane(w2_plane, w2_scales)
-        w2 = load_words("w2_0", w2_words, 0, 4) + load_words("w2_4", w2_words, 4, 8)
-        pos = []
-        for r, src in enumerate((pos1, pos2, pos3, pos4)):
-            tile = keep.tile([P, T // 16], U16, name=f"pos_sb{r}")
-            nc.sync.dma_start(tile[:], src)
-            pos.append(tile)
         gates = {}
-        for h in range(2):
-            for r0 in (0, 2):
-                tile = sb(f"gate{h}{r0}", [P, 2, T], F32)
-                nc.sync.dma_start(
-                    tile[:], gate[r0 : r0 + 2, h * P : (h + 1) * P, :].rearrange("r p t -> p r t")
-                )
-                gates[h, r0] = tile[:, 0, :]
-                gates[h, r0 + 1] = tile[:, 1, :]
+
+        def load_gates(h, r0, tag):
+            tile = sb(f"gate{h}{r0}", [P, 2, T], F32, tag)
+            nc.sync.dma_start(
+                tile[:], gate[r0 : r0 + 2, h * P : (h + 1) * P, :].rearrange("r p t -> p r t")
+            )
+            gates[h, r0] = tile[:, 0, :]
+            gates[h, r0 + 1] = tile[:, 1, :]
+
+        w1 = load_words("w1_first", w1_words, 0, 2)
+        load_plane(w1_plane, w1_scales)
+        load_plane(w2_plane, w2_scales)
 
         x_words = sb("x_words", [P, T], U32)
-        for c, (a, b) in enumerate(X_CHUNKS):
-            grouped = sb(f"x_bf{c}", [P, b - a, 4], BF16)
-            nc.vector.tensor_copy(
-                grouped[:].rearrange("p (c i) j -> p c j i", i=4),
-                x_raw[c][:].rearrange("p j (c i) -> p c j i", i=4),
-            )
+        x_bf = [sb(f"x_bf{c}", [P, b - a, 4], BF16) for c, (a, b) in enumerate(X_CHUNKS)]
+
+        def round_x(c):
+            width = X_CHUNKS[c][1] - X_CHUNKS[c][0]
+            cut = width * 5 // 8
+            dst = x_bf[c][:].rearrange("p (c i) j -> p c j i", i=4)
+            src = x_raw[c][:].rearrange("p j (c i) -> p c j i", i=4)
+            nc.vector.tensor_copy(dst[:, : cut // 4], src[:, : cut // 4])
+            nc.scalar.activation(dst[:, cut // 4 :], src[:, cut // 4 :], COPY)
+
+        def quantise_x(c):
+            a, b = X_CHUNKS[c]
             nc.vector.quantize_mx(
                 out=x_words[:, a:b].bitcast(FP8X4),
                 scales=x_bytes[:, a:b],
-                in_=grouped[:].rearrange("p t j -> p (t j)"),
+                in_=x_bf[c][:].rearrange("p t j -> p (t j)"),
             )
+
+        round_x(0)
+        quantise_x(0)
+        round_x(1)
+        round_x(2)
+        quantise_x(1)
+        quantise_x(2)
+        w1.extend(load_words("w1_second", w1_words, 2, 5, "x_raw0"))
+        w1.extend(load_words("w1_third", w1_words, 5, 8, "x_bf0"))
+        w2 = load_words("w2_all", w2_words, 0, 8, "x_raw1")
+        load_gates(0, 0, "x_raw2")
+        load_gates(0, 2, "x_bf1")
+        load_gates(1, 0, "x_bf2")
         slot_words = sb("slot_words", [P, S], U32)
         slot_bytes = sb("slot_bytes", [P, S], U8)
         for a, b in GATHERS:
             nc.vector.tensor_copy(slot_words[:, a:b], x_words[:].indirect(offs_sb[:, a // 16 : b // 16]))
             nc.vector.tensor_copy(slot_bytes[:, a:b], x_bytes[:].indirect(offs_sb[:, a // 16 : b // 16]))
 
-        turned = []
-        for e in range(E):
+        h_bf, turned, grouped, y_acc = {}, {}, {}, {}
+        h_words = sb("h_words", [P, S], U32)
+        h_bytes = sb("h_bytes", [P, S], U8)
+
+        def first_layer(e):
             slots = slice(e * C, (e + 1) * C)
             acc = bank()
             nc.tensor.matmul_mx(
@@ -127,69 +154,101 @@ def tile_moe_ecr_mlp_gelu_kernel(
                 start=True,
                 stop=True,
             )
-            h_bf = sb(f"h_bf{e}", [P, H], BF16)
+            h_bf[e] = sb(f"h_bf{e}", [P, H], BF16)
             nc.scalar.activation(
-                h_bf[:].rearrange("s (u p d) -> s u p d", u=2, d=2),
+                h_bf[e][:].rearrange("s (u p d) -> s u p d", u=2, d=2),
                 acc[:].rearrange("s (p u d) -> s u p d", u=2, d=2),
                 GELU,
             )
+
+        def turn(g):
+            e0, e1 = H_GROUPS[g]
+            turned[g] = bank()
+            for e in range(e0, e1):
+                pairs = h_bf[e][:].bitcast(F32)
+                for u in range(2):
+                    col = (2 * (e - e0) + u) * P
+                    nc.tensor.transpose(turned[g][:, col : col + P], pairs[:, u * P : (u + 1) * P], ident[:])
+
+        def interleave(g, copy):
+            n = H_GROUPS[g][1] - H_GROUPS[g][0]
+            grouped[g] = sb(f"h_grouped{g}", [P, n * C * 4], BF16)
+            copy(
+                grouped[g][:].bitcast(F32).rearrange("p (e s u) -> p e s u", e=n, u=2),
+                turned[g][:, : n * 2 * C].rearrange("p (e u s) -> p e s u", e=n, u=2),
+            )
+
+        def quantise_h(g):
+            slots = slice(H_GROUPS[g][0] * C, H_GROUPS[g][1] * C)
+            nc.vector.quantize_mx(out=h_words[:, slots].bitcast(FP8X4), scales=h_bytes[:, slots], in_=grouped[g][:])
+
+        def second_layer(e):
             if e % 2 == 0:
-                turned.append(bank())
-            pairs = h_bf[:].bitcast(F32)
-            for u in range(2):
-                col = (2 * (e % 2) + u) * P
-                nc.tensor.transpose(turned[-1][:, col : col + P], pairs[:, u * P : (u + 1) * P], ident[:])
-
-        h_words = sb("h_words", [P, S], U32)
-        h_bytes = sb("h_bytes", [P, S], U8)
-        y_acc = []
-        for g in range(E // 2):
-            slots = slice(g * 2 * C, (g + 1) * 2 * C)
-            grouped = sb(f"h_grouped{g}", [P, 2 * C * 4], BF16)
-            dst = grouped[:].bitcast(F32).rearrange("p (e s u) -> p e s u", e=2, u=2)
-            src = turned[g][:].rearrange("p (e u s) -> p e s u", e=2, u=2)
-            if g < 2:
-                nc.vector.tensor_copy(dst, src)
-            else:
-                nc.scalar.copy(dst, src)
-            nc.vector.quantize_mx(out=h_words[:, slots].bitcast(FP8X4), scales=h_bytes[:, slots], in_=grouped[:])
-            acc = bank()
+                y_acc[e // 2] = bank()
+            mine = slice(e * C, (e + 1) * C)
             for h in range(2):
-                for i in range(2):
-                    e = 2 * g + i
-                    mine = slice(e * C, (e + 1) * C)
-                    nc.tensor.matmul_mx(
-                        out=acc[:, (2 * h + i) * C : (2 * h + i + 1) * C],
-                        lhsT=w2[e][:, 2 * h * P : 2 * (h + 1) * P].bitcast(FP4X4),
-                        lhsT_scale=w2_plane[:, e * N + h * P : e * N + (h + 1) * P],
-                        rhs=h_words[:, mine].bitcast(FP8X4),
-                        rhs_scale=h_bytes[:, mine],
-                        start=True,
-                        stop=True,
-                    )
-            if g < 3:
-                nc.scalar.copy(y[0][:, slots], acc[:, : 2 * C])
-            else:
-                nc.vector.tensor_copy(y[0][:, slots], acc[:, : 2 * C])
-            y_acc.append(acc)
-        for g in range(E // 2):
-            nc.scalar.copy(y[1][:, g * 2 * C : (g + 1) * 2 * C], y_acc[g][:, 2 * C :])
+                col = (2 * h + e % 2) * C
+                nc.tensor.matmul_mx(
+                    out=y_acc[e // 2][:, col : col + C],
+                    lhsT=w2[e][:, 2 * h * P : 2 * (h + 1) * P].bitcast(FP4X4),
+                    lhsT_scale=w2_plane[:, e * N + h * P : e * N + (h + 1) * P],
+                    rhs=h_words[:, mine].bitcast(FP8X4),
+                    rhs_scale=h_bytes[:, mine],
+                    start=True,
+                    stop=True,
+                )
 
-        def fetch(h, r):
-            prod = sb(f"prod{h}{r}", [P, T], F32)
-            nc.vector.tensor_tensor(prod[:], y[h][:].indirect(pos[r][:]), gates[h, r], MULT)
-            return prod
+        def unload(h, pair):
+            nc.scalar.copy(
+                y[h][:, pair * 2 * C : (pair + 1) * 2 * C], y_acc[pair][:, h * 2 * C : (h + 1) * 2 * C]
+            )
+
+        for e in range(4):
+            first_layer(e)
+        load_gates(1, 2, "w1_first")
+        turn(0)
+        first_layer(4)
+        first_layer(5)
+        turn(1)
+        first_layer(6)
+        first_layer(7)
+        turn(2)
+        turn(3)
+        turn(4)
+        interleave(0, nc.vector.tensor_copy)
+        interleave(1, nc.vector.tensor_copy)
+        interleave(2, nc.scalar.copy)
+        quantise_h(0)
+        quantise_h(1)
+        interleave(3, nc.vector.tensor_copy)
+        interleave(4, nc.scalar.copy)
+        for g in range(2, 5):
+            quantise_h(g)
+        for e in range(E):
+            second_layer(e)
+        for h in range(2):
+            for pair in range(E // 2):
+                unload(h, pair)
+
+        prods = {}
+
+        def fetch(h, r, a, b):
+            if (h, r) not in prods:
+                prods[h, r] = sb(f"prod{h}{r}", [P, T], F32)
+            nc.vector.tensor_tensor(
+                prods[h, r][:, a:b], y[h][:].indirect(pos[r][:, a // 16 : b // 16]), gates[h, r][:, a:b], MULT
+            )
 
         partial = {}
         for h in range(2):
             sums = [bank() for part in T_PARTS]
             for r in range(TOP - 1):
-                prod = fetch(h, r)
+                fetch(h, r, 0, T)
                 for part, (a, b) in enumerate(T_PARTS):
                     for t0 in range(a, b, P):
                         nc.tensor.matmul(
                             sums[part][:, t0 - a : t0 - a + P],
-                            prod[:, t0 : t0 + P],
+                            prods[h, r][:, t0 : t0 + P],
                             ident[:],
                             start=(r == 0 and t0 == a),
                             stop=(r == TOP - 2 and t0 == b - P),
@@ -202,9 +261,17 @@ def tile_moe_ecr_mlp_gelu_kernel(
                 for t0 in range(0, b - a, P):
                     nc.tensor.transpose(back[:, t0 : t0 + P], flipped[:, t0 : t0 + P], ident[:])
                 partial[h, part] = back
-        for h in range(2):
-            prod = fetch(h, TOP - 1)
-            for part, (a, b) in enumerate(T_PARTS):
-                res = sb(f"res{h}{part}", [P, b - a], F32)
-                nc.vector.tensor_tensor(res[:], partial[h, part][:, : b - a], prod[:, a:b], ADD)
-                nc.sync.dma_start(out[h * P : (h + 1) * P, a:b], res[:])
+
+        def finish(h, part):
+            a, b = T_PARTS[part]
+            res = sb(f"res{h}{part}", [P, b - a], F32)
+            nc.vector.tensor_tensor(res[:], partial[h, part][:, : b - a], prods[h, TOP - 1][:, a:b], ADD)
+            nc.sync.dma_start(out[h * P : (h + 1) * P, a:b], res[:])
+
+        fetch(0, TOP - 1, 0, T)
+        fetch(1, TOP - 1, *T_PARTS[0])
+        finish(0, 0)
+        finish(1, 0)
+        fetch(1, TOP - 1, *T_PARTS[1])
+        finish(0, 1)
+        finish(1, 1)

@@ -7,6 +7,9 @@ K, T, E, C, H, N = 512, 640, 8, 128, 512, 256
 TOP, PAD = 4, 64
 S = E * C
 P = 128
+BANK = 512
+PACK = 4
+PER_COLUMN = 16
 FLOPS = 2 * S * (K * H + H * N)
 
 F32 = mybir.dt.float32
@@ -18,14 +21,15 @@ U8 = mybir.dt.uint8
 FP8X4 = mybir.dt.float8_e4m3fn_x4
 FP4X4 = mybir.dt.float4_e2m1fn_x4
 GELU = mybir.ActivationFunctionType.Gelu_apprx_tanh
+COPY = mybir.ActivationFunctionType.Copy
 MULT = mybir.AluOpType.mult
 ADD = mybir.AluOpType.add
 
 X_CHUNKS = [(0, 256), (256, 512), (512, 640)]
-GATHERS = [(0, 128), (128, 256), (256, 512), (512, 768), (768, 896), (896, 1024)]
-T_PARTS = [(0, 512), (512, 640)]
-H_GROUPS = [(0, 2), (2, 4), (4, 6), (6, 7), (7, 8)]
-COPY = mybir.ActivationFunctionType.Copy
+X_EIGHTHS_ON_VECTOR = 5
+SLOT_PIECES = [(0, 128), (128, 384), (384, 640), (640, 896), (896, 1024)]
+TOKEN_PARTS = [(0, BANK), (BANK, T)]
+SPARE_COLUMNS = E * N - 2 * H
 
 
 def tile_moe_ecr_mlp_gelu_kernel(
@@ -37,87 +41,81 @@ def tile_moe_ecr_mlp_gelu_kernel(
         psum = ctx.enter_context(tc.psum_pool(name="psum", bufs=8))
 
         def bank():
-            return psum.tile([P, 512], F32, name="bank")
+            return psum.tile([P, BANK], F32, name="bank")
 
-        def sb(name, shape, dtype, tag=None):
-            return keep.tile(shape, dtype, name=name, tag=tag or name, align_bytes=64)
+        def sb(name, shape, dtype, place=None):
+            return keep.tile(shape, dtype, name=name, tag=place or name, align_bytes=64)
 
-        x_rows = xT.rearrange("(p j) t -> p j t", j=4)
+        x_rows = xT.rearrange("(p j) t -> p j t", j=PACK)
         x_raw = []
 
-        def load_x(c):
-            a, b = X_CHUNKS[c]
-            x_raw.append(sb(f"x_raw{c}", [P, 4, b - a], F32))
-            nc.sync.dma_start(x_raw[c][:], x_rows[:, :, a:b])
+        def load_x(chunk):
+            a, b = X_CHUNKS[chunk]
+            x_raw.append(sb(f"x_raw{chunk}", [P, PACK, b - a], F32))
+            nc.sync.dma_start(x_raw[chunk][:], x_rows[:, :, a:b])
 
         load_x(0)
         pos = []
-        for r, src in enumerate((pos1, pos2, pos3, pos4)):
-            tile = keep.tile([P, T // 16], U16, name=f"pos_sb{r}")
-            nc.sync.dma_start(tile[:], src)
-            pos.append(tile)
-        offs_sb = keep.tile([P, S // 16], U16, name="offs_sb")
+        for r, source in enumerate((pos1, pos2, pos3, pos4)):
+            pos.append(keep.tile([P, T // PER_COLUMN], U16, name=f"pos_sb{r}"))
+            nc.sync.dma_start(pos[r][:], source)
+        offs_sb = keep.tile([P, S // PER_COLUMN], U16, name="offs_sb")
         nc.sync.dma_start(offs_sb[:], offs)
         load_x(1)
         load_x(2)
 
-        w1_plane = sb("w1_plane", [P, E * H], U8)
-        w2_plane = sb("w2_plane", [P, E * N], U8)
+        planes = sb("planes", [P, SPARE_COLUMNS + E * H], U8)
+        w1_plane, w2_plane = planes[:, SPARE_COLUMNS:], planes[:, : E * N]
         x_bytes = sb("x_bytes", [P, T], U8)
-        nc.vector.memset(w1_plane[:].bitcast(I32), 0)
-        nc.vector.memset(w2_plane[:].bitcast(I32), 0)
+        nc.vector.memset(planes[:].bitcast(I32), 0)
         nc.vector.memset(x_bytes[:].bitcast(I32), 0)
-        y = [sb(f"y{h}", [P, S + PAD], F32) for h in range(2)]
+        y = [sb(f"y{half}", [P, S + PAD], F32) for half in range(2)]
         nc.vector.memset(y[1][:, S:], 0.0)
         nc.scalar.activation(y[0][:, S:], y[1][:, S:], GELU)
         ident = sb("ident", [P, P], F32)
         make_identity(nc, ident[:])
 
-        def load_plane(plane, scales):
-            for r in range(4):
-                nc.sync.dma_start(
-                    plane[r:P:32, :].bitcast(I32).rearrange("q (e w) -> q e w", e=E),
-                    scales[:, 0, r:16:4, :].bitcast(I32).rearrange("e q w -> q e w"),
-                )
-
-        def load_words(name, words, e0, e1, tag=None):
-            tile = sb(name, [P, e1 - e0, words.shape[3]], U8, tag)
+        def load_words(name, source, e0, e1, place=None):
+            tile = sb(name, [P, e1 - e0, source.shape[3]], U8, place)
             nc.sync.dma_start(
-                tile[:].bitcast(I32), words[e0:e1, 0].bitcast(I32).rearrange("e p w -> p e w")
+                tile[:].bitcast(I32), source[e0:e1, 0].bitcast(I32).rearrange("e p w -> p e w")
             )
             return [tile[:, e, :] for e in range(e1 - e0)]
 
         gates = {}
 
-        def load_gates(h, r0, tag):
-            tile = sb(f"gate{h}{r0}", [P, 2, T], F32, tag)
+        def load_gates(half, r0, place):
+            tile = sb(f"gate{half}{r0}", [P, 2, T], F32, place)
             nc.sync.dma_start(
-                tile[:], gate[r0 : r0 + 2, h * P : (h + 1) * P, :].rearrange("r p t -> p r t")
+                tile[:], gate[r0 : r0 + 2, half * P : (half + 1) * P, :].rearrange("r p t -> p r t")
             )
-            gates[h, r0] = tile[:, 0, :]
-            gates[h, r0 + 1] = tile[:, 1, :]
+            gates[half, r0] = tile[:, 0, :]
+            gates[half, r0 + 1] = tile[:, 1, :]
 
         w1 = load_words("w1_first", w1_words, 0, 2)
-        load_plane(w1_plane, w1_scales)
-        load_plane(w2_plane, w2_scales)
+        for row in range(4):
+            nc.sync.dma_start(
+                w1_plane[row:P:32, :].bitcast(I32).rearrange("q (e w) -> q e w", e=E),
+                w1_scales[:, 0, row:16:4, :].bitcast(I32).rearrange("e q w -> q e w"),
+            )
 
         x_words = sb("x_words", [P, T], U32)
-        x_bf = [sb(f"x_bf{c}", [P, b - a, 4], BF16) for c, (a, b) in enumerate(X_CHUNKS)]
+        x_bf = [sb(f"x_bf{chunk}", [P, b - a, PACK], BF16) for chunk, (a, b) in enumerate(X_CHUNKS)]
 
-        def round_x(c):
-            width = X_CHUNKS[c][1] - X_CHUNKS[c][0]
-            cut = width * 5 // 8
-            dst = x_bf[c][:].rearrange("p (c i) j -> p c j i", i=4)
-            src = x_raw[c][:].rearrange("p j (c i) -> p c j i", i=4)
-            nc.vector.tensor_copy(dst[:, : cut // 4], src[:, : cut // 4])
-            nc.scalar.activation(dst[:, cut // 4 :], src[:, cut // 4 :], COPY)
+        def round_x(chunk):
+            a, b = X_CHUNKS[chunk]
+            runs_on_vector = (b - a) * X_EIGHTHS_ON_VECTOR // 8 // 4
+            dst = x_bf[chunk][:].rearrange("p (c i) j -> p c j i", i=4)
+            src = x_raw[chunk][:].rearrange("p j (c i) -> p c j i", i=4)
+            nc.vector.tensor_copy(dst[:, :runs_on_vector], src[:, :runs_on_vector])
+            nc.scalar.activation(dst[:, runs_on_vector:], src[:, runs_on_vector:], COPY)
 
-        def quantise_x(c):
-            a, b = X_CHUNKS[c]
+        def quantise_x(chunk):
+            a, b = X_CHUNKS[chunk]
             nc.vector.quantize_mx(
                 out=x_words[:, a:b].bitcast(FP8X4),
                 scales=x_bytes[:, a:b],
-                in_=x_bf[c][:].rearrange("p t j -> p (t j)"),
+                in_=x_bf[chunk][:].rearrange("p t j -> p (t j)"),
             )
 
         round_x(0)
@@ -127,18 +125,18 @@ def tile_moe_ecr_mlp_gelu_kernel(
         quantise_x(1)
         quantise_x(2)
         w1.extend(load_words("w1_second", w1_words, 2, 5, "x_raw0"))
-        w1.extend(load_words("w1_third", w1_words, 5, 8, "x_bf0"))
-        w2 = load_words("w2_all", w2_words, 0, 8, "x_raw1")
-        load_gates(0, 0, "x_raw2")
-        load_gates(0, 2, "x_bf1")
-        load_gates(1, 0, "x_bf2")
+        w1.extend(load_words("w1_third", w1_words, 5, E, "x_bf0"))
+        w2 = load_words("w2_all", w2_words, 0, E, "x_raw1")
+        load_gates(0, 0, "x_bf2")
         slot_words = sb("slot_words", [P, S], U32)
         slot_bytes = sb("slot_bytes", [P, S], U8)
-        for a, b in GATHERS:
-            nc.vector.tensor_copy(slot_words[:, a:b], x_words[:].indirect(offs_sb[:, a // 16 : b // 16]))
-            nc.vector.tensor_copy(slot_bytes[:, a:b], x_bytes[:].indirect(offs_sb[:, a // 16 : b // 16]))
+        for a, b in SLOT_PIECES:
+            entries = offs_sb[:, a // PER_COLUMN : b // PER_COLUMN]
+            nc.vector.tensor_copy(slot_words[:, a:b], x_words[:].indirect(entries))
+            nc.vector.tensor_copy(slot_bytes[:, a:b], x_bytes[:].indirect(entries))
 
-        h_bf, turned, grouped, y_acc = {}, {}, {}, {}
+        h_bf, turned = {}, {}
+        h_grouped = [sb(f"h_grouped{pair}", [P, 2 * C * PACK], BF16) for pair in range(E // 2)]
         h_words = sb("h_words", [P, S], U32)
         h_bytes = sb("h_bytes", [P, S], U8)
 
@@ -161,117 +159,120 @@ def tile_moe_ecr_mlp_gelu_kernel(
                 GELU,
             )
 
-        def turn(g):
-            e0, e1 = H_GROUPS[g]
-            turned[g] = bank()
+        def turn(e0, e1):
+            turned[e0] = bank()
             for e in range(e0, e1):
                 pairs = h_bf[e][:].bitcast(F32)
                 for u in range(2):
-                    col = (2 * (e - e0) + u) * P
-                    nc.tensor.transpose(turned[g][:, col : col + P], pairs[:, u * P : (u + 1) * P], ident[:])
+                    col = (2 * (e - e0) + u) * C
+                    nc.tensor.transpose(turned[e0][:, col : col + C], pairs[:, u * P : (u + 1) * P], ident[:])
 
-        def interleave(g, copy):
-            n = H_GROUPS[g][1] - H_GROUPS[g][0]
-            grouped[g] = sb(f"h_grouped{g}", [P, n * C * 4], BF16)
+        def interleave(e0, e1, copy):
+            dst = h_grouped[e0 // 2][:].bitcast(F32).rearrange("p (e s u) -> p e s u", e=2, u=2)
             copy(
-                grouped[g][:].bitcast(F32).rearrange("p (e s u) -> p e s u", e=n, u=2),
-                turned[g][:, : n * 2 * C].rearrange("p (e u s) -> p e s u", e=n, u=2),
+                dst[:, e0 % 2 : e0 % 2 + e1 - e0],
+                turned[e0][:, : (e1 - e0) * 2 * C].rearrange("p (e u s) -> p e s u", s=C, u=2),
             )
 
-        def quantise_h(g):
-            slots = slice(H_GROUPS[g][0] * C, H_GROUPS[g][1] * C)
-            nc.vector.quantize_mx(out=h_words[:, slots].bitcast(FP8X4), scales=h_bytes[:, slots], in_=grouped[g][:])
+        def quantise_h(pair):
+            slots = slice(pair * 2 * C, (pair + 1) * 2 * C)
+            nc.vector.quantize_mx(
+                out=h_words[:, slots].bitcast(FP8X4), scales=h_bytes[:, slots], in_=h_grouped[pair][:]
+            )
 
-        def second_layer(e):
-            if e % 2 == 0:
-                y_acc[e // 2] = bank()
-            mine = slice(e * C, (e + 1) * C)
-            for h in range(2):
-                col = (2 * h + e % 2) * C
+        def second_layer(half, e0, e1):
+            acc = bank()
+            for e in range(e0, e1):
+                slots = slice(e * C, (e + 1) * C)
                 nc.tensor.matmul_mx(
-                    out=y_acc[e // 2][:, col : col + C],
-                    lhsT=w2[e][:, 2 * h * P : 2 * (h + 1) * P].bitcast(FP4X4),
-                    lhsT_scale=w2_plane[:, e * N + h * P : e * N + (h + 1) * P],
-                    rhs=h_words[:, mine].bitcast(FP8X4),
-                    rhs_scale=h_bytes[:, mine],
+                    out=acc[:, (e - e0) * C : (e - e0 + 1) * C],
+                    lhsT=w2[e][:, 2 * half * P : 2 * (half + 1) * P].bitcast(FP4X4),
+                    lhsT_scale=w2_plane[:, e * N + half * P : e * N + (half + 1) * P],
+                    rhs=h_words[:, slots].bitcast(FP8X4),
+                    rhs_scale=h_bytes[:, slots],
                     start=True,
                     stop=True,
                 )
+            nc.scalar.copy(y[half][:, e0 * C : e1 * C], acc[:, : (e1 - e0) * C])
 
-        def unload(h, pair):
-            nc.scalar.copy(
-                y[h][:, pair * 2 * C : (pair + 1) * 2 * C], y_acc[pair][:, h * 2 * C : (h + 1) * 2 * C]
-            )
-
-        for e in range(4):
+        for e in range(5):
             first_layer(e)
-        load_gates(1, 2, "w1_first")
-        turn(0)
-        first_layer(4)
+        for quadrant in (0, 2, 1, 3):
+            nc.sync.dma_start(
+                w2_plane[32 * quadrant : 32 * quadrant + 4, :].bitcast(I32).rearrange("r (e w) -> r e w", e=E),
+                w2_scales[:, 0, 4 * quadrant : 4 * quadrant + 4, :].bitcast(I32).rearrange("e r w -> r e w"),
+            )
+        load_gates(0, 2, "w1_first")
+        load_gates(1, 0, "x_raw0")
+        turn(0, 2)
         first_layer(5)
-        turn(1)
         first_layer(6)
+        turn(2, 4)
         first_layer(7)
-        turn(2)
-        turn(3)
-        turn(4)
-        interleave(0, nc.vector.tensor_copy)
-        interleave(1, nc.vector.tensor_copy)
-        interleave(2, nc.scalar.copy)
+        load_gates(1, 2, "x_bf0")
+        turn(4, 6)
+        turn(6, 7)
+        turn(7, 8)
+        interleave(0, 2, nc.vector.tensor_copy)
+        interleave(2, 4, nc.vector.tensor_copy)
+        interleave(4, 6, nc.scalar.copy)
         quantise_h(0)
         quantise_h(1)
-        interleave(3, nc.vector.tensor_copy)
-        interleave(4, nc.scalar.copy)
-        for g in range(2, 5):
-            quantise_h(g)
-        for e in range(E):
-            second_layer(e)
-        for h in range(2):
-            for pair in range(E // 2):
-                unload(h, pair)
+        interleave(6, 7, nc.vector.tensor_copy)
+        interleave(7, 8, nc.scalar.copy)
+        quantise_h(2)
+        quantise_h(3)
+        second_layer(0, 0, 4)
+        second_layer(0, 4, 6)
+        second_layer(0, 6, 8)
+        second_layer(1, 0, 4)
+        second_layer(1, 4, 8)
 
-        prods = {}
+        last = TOP - 1
+        products = {}
 
-        def fetch(h, r, a, b):
-            if (h, r) not in prods:
-                prods[h, r] = sb(f"prod{h}{r}", [P, T], F32)
+        def fetch(half, r, a, b):
+            if (half, r) not in products:
+                products[half, r] = sb(f"product{half}{r}", [P, T], F32)
             nc.vector.tensor_tensor(
-                prods[h, r][:, a:b], y[h][:].indirect(pos[r][:, a // 16 : b // 16]), gates[h, r][:, a:b], MULT
+                products[half, r][:, a:b],
+                y[half][:].indirect(pos[r][:, a // PER_COLUMN : b // PER_COLUMN]),
+                gates[half, r][:, a:b],
+                MULT,
             )
 
         partial = {}
-        for h in range(2):
-            sums = [bank() for part in T_PARTS]
-            for r in range(TOP - 1):
-                fetch(h, r, 0, T)
-                for part, (a, b) in enumerate(T_PARTS):
+        for half in range(2):
+            sums = [bank() for part in TOKEN_PARTS]
+            for r in range(last):
+                fetch(half, r, 0, T)
+                for part, (a, b) in enumerate(TOKEN_PARTS):
                     for t0 in range(a, b, P):
                         nc.tensor.matmul(
                             sums[part][:, t0 - a : t0 - a + P],
-                            prods[h, r][:, t0 : t0 + P],
+                            products[half, r][:, t0 : t0 + P],
                             ident[:],
                             start=(r == 0 and t0 == a),
-                            stop=(r == TOP - 2 and t0 == b - P),
+                            stop=(r == last - 1 and t0 == b - P),
                             is_transpose=True,
                         )
-            for part, (a, b) in enumerate(T_PARTS):
-                flipped = sb(f"flipped{h}{part}", [P, b - a], F32)
+            for part, (a, b) in enumerate(TOKEN_PARTS):
+                flipped = sb(f"flipped{half}{part}", [P, b - a], F32)
                 nc.scalar.copy(flipped[:], sums[part][:, : b - a])
-                back = bank()
+                partial[half, part] = bank()
                 for t0 in range(0, b - a, P):
-                    nc.tensor.transpose(back[:, t0 : t0 + P], flipped[:, t0 : t0 + P], ident[:])
-                partial[h, part] = back
+                    nc.tensor.transpose(partial[half, part][:, t0 : t0 + P], flipped[:, t0 : t0 + P], ident[:])
 
-        def finish(h, part):
-            a, b = T_PARTS[part]
-            res = sb(f"res{h}{part}", [P, b - a], F32)
-            nc.vector.tensor_tensor(res[:], partial[h, part][:, : b - a], prods[h, TOP - 1][:, a:b], ADD)
-            nc.sync.dma_start(out[h * P : (h + 1) * P, a:b], res[:])
+        def finish(half, part):
+            a, b = TOKEN_PARTS[part]
+            result = sb(f"result{half}{part}", [P, b - a], F32)
+            nc.vector.tensor_tensor(result[:], partial[half, part][:, : b - a], products[half, last][:, a:b], ADD)
+            nc.sync.dma_start(out[half * P : (half + 1) * P, a:b], result[:])
 
-        fetch(0, TOP - 1, 0, T)
-        fetch(1, TOP - 1, *T_PARTS[0])
+        fetch(0, last, 0, T)
+        fetch(1, last, *TOKEN_PARTS[0])
         finish(0, 0)
         finish(1, 0)
-        fetch(1, TOP - 1, *T_PARTS[1])
+        fetch(1, last, *TOKEN_PARTS[1])
         finish(0, 1)
         finish(1, 1)

@@ -27,9 +27,8 @@ ADD = mybir.AluOpType.add
 
 X_CHUNKS = [(0, 256), (256, 512), (512, 640)]
 X_EIGHTHS_ON_VECTOR = 5
-SLOT_PIECES = [(0, 128), (128, 384), (384, 640), (640, 896), (896, 1024)]
-TOKEN_PARTS = [(0, BANK), (BANK, T)]
-SPARE_COLUMNS = E * N - 2 * H
+SLOT_PIECES = [(e * C, (e + 1) * C) for e in range(E)]
+TOKEN_PARTS = [[(0, 3 * P), (3 * P, T)], [(0, 2 * P), (2 * P, 4 * P), (4 * P, T)]]
 
 
 def tile_moe_ecr_mlp_gelu_kernel(
@@ -54,50 +53,52 @@ def tile_moe_ecr_mlp_gelu_kernel(
             x_raw.append(sb(f"x_raw{chunk}", [P, PACK, b - a], F32))
             nc.sync.dma_start(x_raw[chunk][:], x_rows[:, :, a:b])
 
-        load_x(0)
+        for chunk in range(len(X_CHUNKS)):
+            load_x(chunk)
+        offs_sb = keep.tile([P, S // PER_COLUMN], U16, name="offs_sb")
+        nc.sync.dma_start(offs_sb[:], offs)
+
+        def load_plane(name, source, e0, e1):
+            tile = sb(name, [P, e1 - e0, source.shape[3]], U8)
+            nc.vector.memset(tile[:].bitcast(I32), 0)
+            for row in range(4):
+                nc.sync.dma_start(
+                    tile[row:P:32].bitcast(I32),
+                    source[e0:e1, 0, row:16:4, :].bitcast(I32).rearrange("e q w -> q e w"),
+                )
+            return [tile[:, e, :] for e in range(e1 - e0)]
+
+        def load_words(name, source, e0, e1):
+            tile = sb(name, [P, e1 - e0, source.shape[3]], U8)
+            nc.sync.dma_start(
+                tile[:].bitcast(I32), source[e0:e1, 0].bitcast(I32).rearrange("e p w -> p e w")
+            )
+            return [tile[:, e, :] for e in range(e1 - e0)]
+
+        w1_plane = load_plane("w1_plane_first", w1_scales, 0, 2)
+        w1 = load_words("w1_first", w1_words, 0, 2)
+        w1.extend(load_words("w1_second", w1_words, 2, 5))
+        w1_plane.extend(load_plane("w1_plane_rest", w1_scales, 2, E))
+        w1.extend(load_words("w1_third", w1_words, 5, E))
+        w2_plane = load_plane("w2_plane", w2_scales, 0, E)
+        w2 = load_words("w2_all", w2_words, 0, E)
         pos = []
         for r, source in enumerate((pos1, pos2, pos3, pos4)):
             pos.append(keep.tile([P, T // PER_COLUMN], U16, name=f"pos_sb{r}"))
             nc.sync.dma_start(pos[r][:], source)
-        offs_sb = keep.tile([P, S // PER_COLUMN], U16, name="offs_sb")
-        nc.sync.dma_start(offs_sb[:], offs)
-        load_x(1)
-        load_x(2)
+        gates = []
+        for r0 in (0, 2):
+            tile = sb(f"gate{r0}", [P, 2, T], F32)
+            nc.sync.dma_start(tile[:], gate[r0 : r0 + 2, :P, :].rearrange("r p t -> p r t"))
+            gates.extend([tile[:, 0, :], tile[:, 1, :]])
 
-        planes = sb("planes", [P, SPARE_COLUMNS + E * H], U8)
-        w1_plane, w2_plane = planes[:, SPARE_COLUMNS:], planes[:, : E * N]
         x_bytes = sb("x_bytes", [P, T], U8)
-        nc.vector.memset(planes[:].bitcast(I32), 0)
         nc.vector.memset(x_bytes[:].bitcast(I32), 0)
         y = [sb(f"y{half}", [P, S + PAD], F32) for half in range(2)]
         nc.vector.memset(y[1][:, S:], 0.0)
         nc.scalar.activation(y[0][:, S:], y[1][:, S:], GELU)
         ident = sb("ident", [P, P], F32)
         make_identity(nc, ident[:])
-
-        def load_words(name, source, e0, e1, place=None):
-            tile = sb(name, [P, e1 - e0, source.shape[3]], U8, place)
-            nc.sync.dma_start(
-                tile[:].bitcast(I32), source[e0:e1, 0].bitcast(I32).rearrange("e p w -> p e w")
-            )
-            return [tile[:, e, :] for e in range(e1 - e0)]
-
-        gates = {}
-
-        def load_gates(half, r0, place):
-            tile = sb(f"gate{half}{r0}", [P, 2, T], F32, place)
-            nc.sync.dma_start(
-                tile[:], gate[r0 : r0 + 2, half * P : (half + 1) * P, :].rearrange("r p t -> p r t")
-            )
-            gates[half, r0] = tile[:, 0, :]
-            gates[half, r0 + 1] = tile[:, 1, :]
-
-        w1 = load_words("w1_first", w1_words, 0, 2)
-        for row in range(4):
-            nc.sync.dma_start(
-                w1_plane[row:P:32, :].bitcast(I32).rearrange("q (e w) -> q e w", e=E),
-                w1_scales[:, 0, row:16:4, :].bitcast(I32).rearrange("e q w -> q e w"),
-            )
 
         x_words = sb("x_words", [P, T], U32)
         x_bf = [sb(f"x_bf{chunk}", [P, b - a, PACK], BF16) for chunk, (a, b) in enumerate(X_CHUNKS)]
@@ -124,10 +125,6 @@ def tile_moe_ecr_mlp_gelu_kernel(
         round_x(2)
         quantise_x(1)
         quantise_x(2)
-        w1.extend(load_words("w1_second", w1_words, 2, 5, "x_raw0"))
-        w1.extend(load_words("w1_third", w1_words, 5, E, "x_bf0"))
-        w2 = load_words("w2_all", w2_words, 0, E, "x_raw1")
-        load_gates(0, 0, "x_bf2")
         slot_words = sb("slot_words", [P, S], U32)
         slot_bytes = sb("slot_bytes", [P, S], U8)
         for a, b in SLOT_PIECES:
@@ -148,7 +145,7 @@ def tile_moe_ecr_mlp_gelu_kernel(
                 lhsT=slot_words[:, slots].bitcast(FP8X4),
                 lhsT_scale=slot_bytes[:, slots],
                 rhs=w1[e].bitcast(FP4X4),
-                rhs_scale=w1_plane[:, e * H : (e + 1) * H],
+                rhs_scale=w1_plane[e],
                 start=True,
                 stop=True,
             )
@@ -187,7 +184,7 @@ def tile_moe_ecr_mlp_gelu_kernel(
                 nc.tensor.matmul_mx(
                     out=acc[:, (e - e0) * C : (e - e0 + 1) * C],
                     lhsT=w2[e][:, 2 * half * P : 2 * (half + 1) * P].bitcast(FP4X4),
-                    lhsT_scale=w2_plane[:, e * N + half * P : e * N + (half + 1) * P],
+                    lhsT_scale=w2_plane[e][:, half * P : (half + 1) * P],
                     rhs=h_words[:, slots].bitcast(FP8X4),
                     rhs_scale=h_bytes[:, slots],
                     start=True,
@@ -197,19 +194,11 @@ def tile_moe_ecr_mlp_gelu_kernel(
 
         for e in range(5):
             first_layer(e)
-        for quadrant in (0, 2, 1, 3):
-            nc.sync.dma_start(
-                w2_plane[32 * quadrant : 32 * quadrant + 4, :].bitcast(I32).rearrange("r (e w) -> r e w", e=E),
-                w2_scales[:, 0, 4 * quadrant : 4 * quadrant + 4, :].bitcast(I32).rearrange("e r w -> r e w"),
-            )
-        load_gates(0, 2, "w1_first")
-        load_gates(1, 0, "x_raw0")
         turn(0, 2)
         first_layer(5)
         first_layer(6)
         turn(2, 4)
         first_layer(7)
-        load_gates(1, 2, "x_bf0")
         turn(4, 6)
         turn(6, 7)
         turn(7, 8)
@@ -229,50 +218,57 @@ def tile_moe_ecr_mlp_gelu_kernel(
         second_layer(1, 4, 8)
 
         last = TOP - 1
-        products = {}
+        products = [sb("products0", [P, TOP, T], F32), sb("products1", [P, TOP, T], F32, "y0")]
 
         def fetch(half, r, a, b):
-            if (half, r) not in products:
-                products[half, r] = sb(f"product{half}{r}", [P, T], F32)
             nc.vector.tensor_tensor(
-                products[half, r][:, a:b],
+                products[half][:, r, a:b],
                 y[half][:].indirect(pos[r][:, a // PER_COLUMN : b // PER_COLUMN]),
-                gates[half, r][:, a:b],
+                gates[r][:, a:b],
                 MULT,
             )
 
-        partial = {}
-        for half in range(2):
-            sums = [bank() for part in TOKEN_PARTS]
-            for r in range(last):
-                fetch(half, r, 0, T)
-                for part, (a, b) in enumerate(TOKEN_PARTS):
-                    for t0 in range(a, b, P):
-                        nc.tensor.matmul(
-                            sums[part][:, t0 - a : t0 - a + P],
-                            products[half, r][:, t0 : t0 + P],
-                            ident[:],
-                            start=(r == 0 and t0 == a),
-                            stop=(r == last - 1 and t0 == b - P),
-                            is_transpose=True,
-                        )
-            for part, (a, b) in enumerate(TOKEN_PARTS):
-                flipped = sb(f"flipped{half}{part}", [P, b - a], F32)
-                nc.scalar.copy(flipped[:], sums[part][:, : b - a])
-                partial[half, part] = bank()
-                for t0 in range(0, b - a, P):
-                    nc.tensor.transpose(partial[half, part][:, t0 : t0 + P], flipped[:, t0 : t0 + P], ident[:])
+        def add_up(sums, half, r, a, b, final):
+            for t0 in range(a, b, P):
+                nc.tensor.matmul(
+                    sums[:, t0 - a : t0 - a + P],
+                    products[half][:, r, t0 : t0 + P],
+                    ident[:],
+                    start=(r == 0 and t0 == a),
+                    stop=(final and t0 == b - P),
+                    is_transpose=True,
+                )
 
-        def finish(half, part):
-            a, b = TOKEN_PARTS[part]
-            result = sb(f"result{half}{part}", [P, b - a], F32)
-            nc.vector.tensor_tensor(result[:], partial[half, part][:, : b - a], products[half, last][:, a:b], ADD)
-            nc.sync.dma_start(out[half * P : (half + 1) * P, a:b], result[:])
+        def turn_back(sums, half, a, b):
+            flipped = sb(f"flipped{half}_{a}", [P, b - a], F32)
+            nc.scalar.copy(flipped[:], sums[:, : b - a])
+            back = bank()
+            for t0 in range(0, b - a, P):
+                nc.tensor.transpose(back[:, t0 : t0 + P], flipped[:, t0 : t0 + P], ident[:])
+            return back
 
-        fetch(0, last, 0, T)
-        fetch(1, last, *TOKEN_PARTS[0])
-        finish(0, 0)
-        finish(1, 0)
-        fetch(1, last, *TOKEN_PARTS[1])
-        finish(0, 1)
-        finish(1, 1)
+        sums = [bank() for part in TOKEN_PARTS[0]]
+        for r in range(TOP):
+            fetch(0, r, 0, T)
+            for part, (a, b) in enumerate(TOKEN_PARTS[0]):
+                add_up(sums[part], 0, r, a, b, r == last)
+        for part, (a, b) in enumerate(TOKEN_PARTS[0]):
+            back = turn_back(sums[part], 0, a, b)
+            result = sb(f"result0{part}", [P, b - a], F32)
+            nc.scalar.copy(result[:], back[:, : b - a])
+            nc.sync.dma_start(out[:P, a:b], result[:])
+        sums = [bank() for part in TOKEN_PARTS[1]]
+        for r in range(last - 1):
+            fetch(1, r, 0, T)
+            for part, (a, b) in enumerate(TOKEN_PARTS[1]):
+                add_up(sums[part], 1, r, a, b, False)
+        for part, (a, b) in enumerate(TOKEN_PARTS[1]):
+            fetch(1, last - 1, a, b)
+            add_up(sums[part], 1, last - 1, a, b, True)
+        backs = [turn_back(sums[part], 1, a, b) for part, (a, b) in enumerate(TOKEN_PARTS[1])]
+        for a, b in TOKEN_PARTS[1]:
+            fetch(1, last, a, b)
+        for part, (a, b) in enumerate(TOKEN_PARTS[1]):
+            result = sb(f"result1{part}", [P, b - a], F32)
+            nc.vector.tensor_tensor(result[:], backs[part][:, : b - a], products[1][:, last, a:b], ADD)
+            nc.sync.dma_start(out[P:, a:b], result[:])

@@ -10,6 +10,7 @@ P = 128
 BANK = 512
 PACK = 4
 PER_COLUMN = 16
+TURNED = 6
 FLOPS = 2 * S * (K * H + H * N)
 
 F32 = mybir.dt.float32
@@ -27,7 +28,6 @@ ADD = mybir.AluOpType.add
 
 X_CHUNKS = [(0, 256), (256, 512), (512, 640)]
 X_EIGHTHS_ON_VECTOR = 5
-SLOT_PIECES = [(e * C, (e + 1) * C) for e in range(E)]
 TOKEN_PARTS = [[(0, 3 * P), (3 * P, T)], [(0, 2 * P), (2 * P, 4 * P), (4 * P, T)]]
 
 
@@ -58,6 +58,8 @@ def tile_moe_ecr_mlp_gelu_kernel(
         offs_sb = keep.tile([P, S // PER_COLUMN], U16, name="offs_sb")
         nc.sync.dma_start(offs_sb[:], offs)
 
+        whole = {}
+
         def load_plane(name, source, e0, e1):
             tile = sb(name, [P, e1 - e0, source.shape[3]], U8)
             nc.vector.memset(tile[:].bitcast(I32), 0)
@@ -66,6 +68,7 @@ def tile_moe_ecr_mlp_gelu_kernel(
                     tile[row:P:32].bitcast(I32),
                     source[e0:e1, 0, row:16:4, :].bitcast(I32).rearrange("e q w -> q e w"),
                 )
+            whole[name] = tile
             return [tile[:, e, :] for e in range(e1 - e0)]
 
         def load_words(name, source, e0, e1):
@@ -73,13 +76,13 @@ def tile_moe_ecr_mlp_gelu_kernel(
             nc.sync.dma_start(
                 tile[:].bitcast(I32), source[e0:e1, 0].bitcast(I32).rearrange("e p w -> p e w")
             )
+            whole[name] = tile
             return [tile[:, e, :] for e in range(e1 - e0)]
 
-        w1_plane = load_plane("w1_plane_first", w1_scales, 0, 2)
-        w1 = load_words("w1_first", w1_words, 0, 2)
-        w1.extend(load_words("w1_second", w1_words, 2, 5))
-        w1_plane.extend(load_plane("w1_plane_rest", w1_scales, 2, E))
-        w1.extend(load_words("w1_third", w1_words, 5, E))
+        w1_plane = load_plane("w1_plane", w1_scales, 0, E)
+        w1 = []
+        for e0, e1 in ((0, 1), (1, 3), (3, TURNED), (TURNED, E)):
+            w1.extend(load_words(f"w1_from{e0}", w1_words, e0, e1))
         w2_plane = load_plane("w2_plane", w2_scales, 0, E)
         w2 = load_words("w2_all", w2_words, 0, E)
         pos = []
@@ -99,6 +102,17 @@ def tile_moe_ecr_mlp_gelu_kernel(
         nc.scalar.activation(y[0][:, S:], y[1][:, S:], GELU)
         ident = sb("ident", [P, P], F32)
         make_identity(nc, ident[:])
+
+        w1_sorted = sb("w1_sorted", [P, E - TURNED, H], U16)
+        plane_sorted = sb("plane_sorted", [P, E - TURNED, H], U8)
+        nc.gpsimd.tensor_copy(
+            plane_sorted[:].rearrange("p e (t m) -> p e t m", t=PACK),
+            whole["w1_plane"][:, TURNED:].rearrange("p e (m t) -> p e t m", t=PACK),
+        )
+        nc.gpsimd.tensor_copy(
+            w1_sorted[:].rearrange("p e (t m) -> p e t m", t=PACK),
+            whole[f"w1_from{TURNED}"][:].bitcast(U16).rearrange("p e (m t) -> p e t m", t=PACK),
+        )
 
         x_words = sb("x_words", [P, T], U32)
         x_bf = [sb(f"x_bf{chunk}", [P, b - a, PACK], BF16) for chunk, (a, b) in enumerate(X_CHUNKS)]
@@ -127,14 +141,18 @@ def tile_moe_ecr_mlp_gelu_kernel(
         quantise_x(2)
         slot_words = sb("slot_words", [P, S], U32)
         slot_bytes = sb("slot_bytes", [P, S], U8)
-        for a, b in SLOT_PIECES:
-            entries = offs_sb[:, a // PER_COLUMN : b // PER_COLUMN]
-            nc.vector.tensor_copy(slot_words[:, a:b], x_words[:].indirect(entries))
-            nc.vector.tensor_copy(slot_bytes[:, a:b], x_bytes[:].indirect(entries))
+
+        def gather(slots, tokens, e0, e1):
+            entries = offs_sb[:, e0 * C // PER_COLUMN : e1 * C // PER_COLUMN]
+            nc.vector.tensor_copy(slots[:, e0 * C : e1 * C], tokens[:].indirect(entries))
+
+        for e in range(E):
+            gather(slot_bytes, x_bytes, e, e + 1)
+            gather(slot_words, x_words, e, e + 1)
 
         h_bf, turned = {}, {}
-        h_grouped = [sb(f"h_grouped{pair}", [P, 2 * C * PACK], BF16) for pair in range(E // 2)]
-        h_words = sb("h_words", [P, S], U32)
+        h_grouped = {}
+        h_words = {}
         h_bytes = sb("h_bytes", [P, S], U8)
 
         def first_layer(e):
@@ -156,28 +174,50 @@ def tile_moe_ecr_mlp_gelu_kernel(
                 GELU,
             )
 
-        def turn(e0, e1):
-            turned[e0] = bank()
-            for e in range(e0, e1):
-                pairs = h_bf[e][:].bitcast(F32)
-                for u in range(2):
-                    col = (2 * (e - e0) + u) * C
-                    nc.tensor.transpose(turned[e0][:, col : col + C], pairs[:, u * P : (u + 1) * P], ident[:])
+        def first_layer_sorted(e):
+            slots = slice(e * C, (e + 1) * C)
+            acc = bank()
+            for t in range(PACK):
+                nc.tensor.matmul_mx(
+                    out=acc[:, t * C : (t + 1) * C],
+                    lhsT=w1_sorted[:, e - TURNED, t * P : (t + 1) * P].bitcast(FP4X4),
+                    lhsT_scale=plane_sorted[:, e - TURNED, t * P : (t + 1) * P],
+                    rhs=slot_words[:, slots].bitcast(FP8X4),
+                    rhs_scale=slot_bytes[:, slots],
+                    start=True,
+                    stop=True,
+                )
+            if e == TURNED:
+                h_grouped[e] = sb("h_grouped_sorted", [P, (E - TURNED) * C * PACK], BF16)
+            part = h_grouped[TURNED][:, (e - TURNED) * C * PACK : (e - TURNED + 1) * C * PACK]
+            nc.scalar.activation(
+                part.rearrange("p (s t) -> p s t", t=PACK), acc[:].rearrange("p (t s) -> p s t", t=PACK), GELU
+            )
+
+        def turn(e, e0):
+            if e == e0:
+                turned[e0] = bank()
+            pairs = h_bf[e][:].bitcast(F32)
+            for u in range(2):
+                col = (2 * (e - e0) + u) * C
+                nc.tensor.transpose(turned[e0][:, col : col + C], pairs[:, u * P : (u + 1) * P], ident[:])
 
         def interleave(e0, e1, copy):
-            dst = h_grouped[e0 // 2][:].bitcast(F32).rearrange("p (e s u) -> p e s u", e=2, u=2)
+            h_grouped[e0] = sb(f"h_grouped{e0}", [P, (e1 - e0) * C * PACK], BF16)
             copy(
-                dst[:, e0 % 2 : e0 % 2 + e1 - e0],
+                h_grouped[e0][:].bitcast(F32).rearrange("p (e s u) -> p e s u", s=C, u=2),
                 turned[e0][:, : (e1 - e0) * 2 * C].rearrange("p (e u s) -> p e s u", s=C, u=2),
             )
 
-        def quantise_h(pair):
-            slots = slice(pair * 2 * C, (pair + 1) * 2 * C)
+        def quantise_h(e0, e1, place=None):
+            words = sb(f"h_words{e0}", [P, (e1 - e0) * C], U32, place)
             nc.vector.quantize_mx(
-                out=h_words[:, slots].bitcast(FP8X4), scales=h_bytes[:, slots], in_=h_grouped[pair][:]
+                out=words[:].bitcast(FP8X4), scales=h_bytes[:, e0 * C : e1 * C], in_=h_grouped[e0][:]
             )
+            for e in range(e0, e1):
+                h_words[e] = words[:, (e - e0) * C : (e - e0 + 1) * C]
 
-        def second_layer(half, e0, e1):
+        def second_layer(half, e0, e1, copy):
             acc = bank()
             for e in range(e0, e1):
                 slots = slice(e * C, (e + 1) * C)
@@ -185,37 +225,37 @@ def tile_moe_ecr_mlp_gelu_kernel(
                     out=acc[:, (e - e0) * C : (e - e0 + 1) * C],
                     lhsT=w2[e][:, 2 * half * P : 2 * (half + 1) * P].bitcast(FP4X4),
                     lhsT_scale=w2_plane[e][:, half * P : (half + 1) * P],
-                    rhs=h_words[:, slots].bitcast(FP8X4),
+                    rhs=h_words[e].bitcast(FP8X4),
                     rhs_scale=h_bytes[:, slots],
                     start=True,
                     stop=True,
                 )
-            nc.scalar.copy(y[half][:, e0 * C : e1 * C], acc[:, : (e1 - e0) * C])
+            copy(y[half][:, e0 * C : e1 * C], acc[:, : (e1 - e0) * C])
 
+        on_vector, on_scalar = nc.vector.tensor_copy, nc.scalar.copy
         for e in range(5):
             first_layer(e)
-        turn(0, 2)
+        turn(0, 0)
         first_layer(5)
-        first_layer(6)
-        turn(2, 4)
-        first_layer(7)
-        turn(4, 6)
-        turn(6, 7)
-        turn(7, 8)
-        interleave(0, 2, nc.vector.tensor_copy)
-        interleave(2, 4, nc.vector.tensor_copy)
-        interleave(4, 6, nc.scalar.copy)
-        quantise_h(0)
-        quantise_h(1)
-        interleave(6, 7, nc.vector.tensor_copy)
-        interleave(7, 8, nc.scalar.copy)
-        quantise_h(2)
-        quantise_h(3)
-        second_layer(0, 0, 4)
-        second_layer(0, 4, 6)
-        second_layer(0, 6, 8)
-        second_layer(1, 0, 4)
-        second_layer(1, 4, 8)
+        turn(1, 0)
+        first_layer_sorted(6)
+        turn(2, 2)
+        turn(3, 2)
+        first_layer_sorted(7)
+        turn(4, 4)
+        turn(5, 4)
+        interleave(0, 2, on_vector)
+        interleave(2, 4, on_vector)
+        interleave(4, 6, on_scalar)
+        quantise_h(0, 2, "h_bf3")
+        quantise_h(2, 4)
+        quantise_h(6, 8)
+        quantise_h(4, 6)
+        second_layer(0, 0, 4, on_scalar)
+        second_layer(0, 6, 8, on_vector)
+        second_layer(0, 4, 6, on_scalar)
+        second_layer(1, 0, 4, on_scalar)
+        second_layer(1, 4, 8, on_scalar)
 
         last = TOP - 1
         products = [sb("products0", [P, TOP, T], F32), sb("products1", [P, TOP, T], F32, "y0")]

@@ -10,7 +10,7 @@ P = 128
 BANK = 512
 PACK = 4
 PER_COLUMN = 16
-TURNED = 6
+SORTED = 2
 FLOPS = 2 * S * (K * H + H * N)
 
 F32 = mybir.dt.float32
@@ -79,10 +79,10 @@ def tile_moe_ecr_mlp_gelu_kernel(
             whole[name] = tile
             return [tile[:, e, :] for e in range(e1 - e0)]
 
-        w1_plane = load_plane("w1_plane", w1_scales, 0, E)
-        w1 = []
-        for e0, e1 in ((0, 1), (1, 3), (3, TURNED), (TURNED, E)):
-            w1.extend(load_words(f"w1_from{e0}", w1_words, e0, e1))
+        w1_plane = load_plane("w1_plane", w1_scales, 0, E // 2)
+        w1 = load_words("w1_from2", w1_words, 2, 4) + load_words("w1_from4", w1_words, 4, 6)
+        w1_plane.extend(load_plane("w1_plane_rest", w1_scales, E // 2, E))
+        w1 = load_words("w1_from0", w1_words, 0, 2) + w1 + load_words("w1_from6", w1_words, 6, E)
         w2_plane = load_plane("w2_plane", w2_scales, 0, E)
         w2 = load_words("w2_all", w2_words, 0, E)
         pos = []
@@ -103,15 +103,15 @@ def tile_moe_ecr_mlp_gelu_kernel(
         ident = sb("ident", [P, P], F32)
         make_identity(nc, ident[:])
 
-        w1_sorted = sb("w1_sorted", [P, E - TURNED, H], U16)
-        plane_sorted = sb("plane_sorted", [P, E - TURNED, H], U8)
+        w1_sorted = sb("w1_sorted", [P, SORTED, H], U16)
+        plane_sorted = sb("plane_sorted", [P, SORTED, H], U8)
         nc.gpsimd.tensor_copy(
             plane_sorted[:].rearrange("p e (t m) -> p e t m", t=PACK),
-            whole["w1_plane"][:, TURNED:].rearrange("p e (m t) -> p e t m", t=PACK),
+            whole["w1_plane"][:, :SORTED].rearrange("p e (m t) -> p e t m", t=PACK),
         )
         nc.gpsimd.tensor_copy(
             w1_sorted[:].rearrange("p e (t m) -> p e t m", t=PACK),
-            whole[f"w1_from{TURNED}"][:].bitcast(U16).rearrange("p e (m t) -> p e t m", t=PACK),
+            whole["w1_from0"][:].bitcast(U16).rearrange("p e (m t) -> p e t m", t=PACK),
         )
 
         x_words = sb("x_words", [P, T], U32)
@@ -146,9 +146,13 @@ def tile_moe_ecr_mlp_gelu_kernel(
             entries = offs_sb[:, e0 * C // PER_COLUMN : e1 * C // PER_COLUMN]
             nc.vector.tensor_copy(slots[:, e0 * C : e1 * C], tokens[:].indirect(entries))
 
-        for e in range(E):
+        for e in (2, 3):
             gather(slot_bytes, x_bytes, e, e + 1)
             gather(slot_words, x_words, e, e + 1)
+        for e in (4, 6, 0):
+            gather(slot_bytes, x_bytes, e, e + 2)
+            gather(slot_words, x_words, e, e + 1)
+            gather(slot_words, x_words, e + 1, e + 2)
 
         h_bf, turned = {}, {}
         h_grouped = {}
@@ -180,16 +184,16 @@ def tile_moe_ecr_mlp_gelu_kernel(
             for t in range(PACK):
                 nc.tensor.matmul_mx(
                     out=acc[:, t * C : (t + 1) * C],
-                    lhsT=w1_sorted[:, e - TURNED, t * P : (t + 1) * P].bitcast(FP4X4),
-                    lhsT_scale=plane_sorted[:, e - TURNED, t * P : (t + 1) * P],
+                    lhsT=w1_sorted[:, e, t * P : (t + 1) * P].bitcast(FP4X4),
+                    lhsT_scale=plane_sorted[:, e, t * P : (t + 1) * P],
                     rhs=slot_words[:, slots].bitcast(FP8X4),
                     rhs_scale=slot_bytes[:, slots],
                     start=True,
                     stop=True,
                 )
-            if e == TURNED:
-                h_grouped[e] = sb("h_grouped_sorted", [P, (E - TURNED) * C * PACK], BF16)
-            part = h_grouped[TURNED][:, (e - TURNED) * C * PACK : (e - TURNED + 1) * C * PACK]
+            if e == 0:
+                h_grouped[0] = sb("h_grouped0", [P, SORTED * C * PACK], BF16)
+            part = h_grouped[0][:, e * C * PACK : (e + 1) * C * PACK]
             nc.scalar.activation(
                 part.rearrange("p (s t) -> p s t", t=PACK), acc[:].rearrange("p (t s) -> p s t", t=PACK), GELU
             )
@@ -233,27 +237,31 @@ def tile_moe_ecr_mlp_gelu_kernel(
             copy(y[half][:, e0 * C : e1 * C], acc[:, : (e1 - e0) * C])
 
         on_vector, on_scalar = nc.vector.tensor_copy, nc.scalar.copy
-        for e in range(5):
+        for e in range(2, 6):
             first_layer(e)
-        turn(0, 0)
-        first_layer(5)
-        turn(1, 0)
-        first_layer_sorted(6)
         turn(2, 2)
+        first_layer(6)
+        first_layer(7)
         turn(3, 2)
-        first_layer_sorted(7)
         turn(4, 4)
+        first_layer_sorted(0)
         turn(5, 4)
-        interleave(0, 2, on_vector)
+        first_layer_sorted(1)
+        turn(6, 6)
+        turn(7, 7)
         interleave(2, 4, on_vector)
-        interleave(4, 6, on_scalar)
-        quantise_h(0, 2, "h_bf3")
-        quantise_h(2, 4)
-        quantise_h(6, 8)
+        interleave(4, 6, on_vector)
+        interleave(6, 7, on_scalar)
+        interleave(7, 8, on_scalar)
+        quantise_h(2, 4, "h_bf5")
         quantise_h(4, 6)
-        second_layer(0, 0, 4, on_scalar)
-        second_layer(0, 6, 8, on_vector)
-        second_layer(0, 4, 6, on_scalar)
+        quantise_h(0, 2)
+        quantise_h(6, 7)
+        quantise_h(7, 8)
+        second_layer(0, 2, 6, on_scalar)
+        second_layer(0, 0, 2, on_vector)
+        second_layer(0, 6, 7, on_scalar)
+        second_layer(0, 7, 8, on_scalar)
         second_layer(1, 0, 4, on_scalar)
         second_layer(1, 4, 8, on_scalar)
 

@@ -11,6 +11,7 @@ BANK = 512
 PACK = 4
 PER_COLUMN = 16
 SORTED = 2
+WARM_UPS = 2
 FLOPS = 2 * S * (K * H + H * N)
 
 F32 = mybir.dt.float32
@@ -113,6 +114,24 @@ def tile_moe_ecr_mlp_gelu_kernel(
             w1_sorted[:].rearrange("p e (t m) -> p e t m", t=PACK),
             whole["w1_from0"][:].bitcast(U16).rearrange("p e (m t) -> p e t m", t=PACK),
         )
+
+        zeros = sb("zeros", [P, PACK * P], BF16)
+        nc.vector.memset(zeros[:].bitcast(I32), 0)
+        zero_words = sb("zero_words", [P, P], U32)
+        zero_bytes = sb("zero_bytes", [P, P], U8)
+        nc.vector.quantize_mx(out=zero_words[:].bitcast(FP8X4), scales=zero_bytes[:], in_=zeros[:])
+        plane_bytes = whole["w1_plane"][:].rearrange("p e w -> p (e w)")
+        unused = bank()
+        for warm_up in range(WARM_UPS):
+            nc.tensor.matmul_mx(
+                out=unused[:],
+                lhsT=zero_words[:].bitcast(FP8X4),
+                lhsT_scale=zero_bytes[:],
+                rhs=plane_bytes[:, : 2 * H].bitcast(FP4X4),
+                rhs_scale=plane_bytes[:, 2 * H : 3 * H],
+                start=True,
+                stop=True,
+            )
 
         x_words = sb("x_words", [P, T], U32)
         x_bf = [sb(f"x_bf{chunk}", [P, b - a, PACK], BF16) for chunk, (a, b) in enumerate(X_CHUNKS)]

@@ -10,7 +10,7 @@ P = 128
 BANK = 512
 PACK = 4
 PER_COLUMN = 16
-SORTED = 2
+SORTED = 3
 WARM_UPS = 2
 FLOPS = 2 * S * (K * H + H * N)
 
@@ -29,6 +29,7 @@ ADD = mybir.AluOpType.add
 
 X_CHUNKS = [(0, 256), (256, 512), (512, 640)]
 X_EIGHTHS_ON_VECTOR = 5
+GATHER_GROUPS = [(3, 4), (4, 5), (5, 7), (7, 8), (0, 1), (1, 3)]
 TOKEN_PARTS = [[(0, 3 * P), (3 * P, T)], [(0, 2 * P), (2 * P, 4 * P), (4 * P, T)]]
 
 
@@ -48,18 +49,11 @@ def tile_moe_ecr_mlp_gelu_kernel(
 
         x_rows = xT.rearrange("(p j) t -> p j t", j=PACK)
         x_raw = []
-
-        def load_x(chunk):
-            a, b = X_CHUNKS[chunk]
+        for chunk, (a, b) in enumerate(X_CHUNKS):
             x_raw.append(sb(f"x_raw{chunk}", [P, PACK, b - a], F32))
             nc.sync.dma_start(x_raw[chunk][:], x_rows[:, :, a:b])
-
-        for chunk in range(len(X_CHUNKS)):
-            load_x(chunk)
         offs_sb = keep.tile([P, S // PER_COLUMN], U16, name="offs_sb")
         nc.sync.dma_start(offs_sb[:], offs)
-
-        whole = {}
 
         def load_plane(name, source, e0, e1):
             tile = sb(name, [P, e1 - e0, source.shape[3]], U8)
@@ -69,23 +63,28 @@ def tile_moe_ecr_mlp_gelu_kernel(
                     tile[row:P:32].bitcast(I32),
                     source[e0:e1, 0, row:16:4, :].bitcast(I32).rearrange("e q w -> q e w"),
                 )
-            whole[name] = tile
-            return [tile[:, e, :] for e in range(e1 - e0)]
+            return tile
 
         def load_words(name, source, e0, e1):
             tile = sb(name, [P, e1 - e0, source.shape[3]], U8)
             nc.sync.dma_start(
                 tile[:].bitcast(I32), source[e0:e1, 0].bitcast(I32).rearrange("e p w -> p e w")
             )
-            whole[name] = tile
-            return [tile[:, e, :] for e in range(e1 - e0)]
+            return tile
 
-        w1_plane = load_plane("w1_plane", w1_scales, 0, E // 2)
-        w1 = load_words("w1_from2", w1_words, 2, 4) + load_words("w1_from4", w1_words, 4, 6)
-        w1_plane.extend(load_plane("w1_plane_rest", w1_scales, E // 2, E))
-        w1 = load_words("w1_from0", w1_words, 0, 2) + w1 + load_words("w1_from6", w1_words, 6, E)
-        w2_plane = load_plane("w2_plane", w2_scales, 0, E)
-        w2 = load_words("w2_all", w2_words, 0, E)
+        def by_expert(*tiles):
+            return [tile[:, e, :] for tile in tiles for e in range(tile.shape[1])]
+
+        plane_first = load_plane("w1_plane", w1_scales, 0, 5)
+        words_3_4 = load_words("w1_from3", w1_words, 3, 5)
+        words_5_6 = load_words("w1_from5", w1_words, 5, 7)
+        plane_rest = load_plane("w1_plane_rest", w1_scales, 5, E)
+        words_to_sort = load_words("w1_from0", w1_words, 0, SORTED)
+        words_7 = load_words("w1_from7", w1_words, 7, E)
+        w1_plane = by_expert(plane_first, plane_rest)
+        w1 = by_expert(words_to_sort, words_3_4, words_5_6, words_7)
+        w2_plane = by_expert(load_plane("w2_plane", w2_scales, 0, E))
+        w2 = by_expert(load_words("w2_all", w2_words, 0, E))
         pos = []
         for r, source in enumerate((pos1, pos2, pos3, pos4)):
             pos.append(keep.tile([P, T // PER_COLUMN], U16, name=f"pos_sb{r}"))
@@ -108,19 +107,20 @@ def tile_moe_ecr_mlp_gelu_kernel(
         plane_sorted = sb("plane_sorted", [P, SORTED, H], U8)
         nc.gpsimd.tensor_copy(
             plane_sorted[:].rearrange("p e (t m) -> p e t m", t=PACK),
-            whole["w1_plane"][:, :SORTED].rearrange("p e (m t) -> p e t m", t=PACK),
+            plane_first[:, :SORTED].rearrange("p e (m t) -> p e t m", t=PACK),
         )
-        nc.gpsimd.tensor_copy(
-            w1_sorted[:].rearrange("p e (t m) -> p e t m", t=PACK),
-            whole["w1_from0"][:].bitcast(U16).rearrange("p e (m t) -> p e t m", t=PACK),
-        )
+        for e0, e1 in ((0, 1), (1, SORTED)):
+            nc.gpsimd.tensor_copy(
+                w1_sorted[:, e0:e1].rearrange("p e (t m) -> p e t m", t=PACK),
+                words_to_sort[:, e0:e1].bitcast(U16).rearrange("p e (m t) -> p e t m", t=PACK),
+            )
 
         zeros = sb("zeros", [P, PACK * P], BF16)
         nc.vector.memset(zeros[:].bitcast(I32), 0)
         zero_words = sb("zero_words", [P, P], U32)
         zero_bytes = sb("zero_bytes", [P, P], U8)
         nc.vector.quantize_mx(out=zero_words[:].bitcast(FP8X4), scales=zero_bytes[:], in_=zeros[:])
-        plane_bytes = whole["w1_plane"][:].rearrange("p e w -> p (e w)")
+        plane_bytes = plane_first[:].rearrange("p e w -> p (e w)")
         unused = bank()
         for warm_up in range(WARM_UPS):
             nc.tensor.matmul_mx(
@@ -165,18 +165,22 @@ def tile_moe_ecr_mlp_gelu_kernel(
             entries = offs_sb[:, e0 * C // PER_COLUMN : e1 * C // PER_COLUMN]
             nc.vector.tensor_copy(slots[:, e0 * C : e1 * C], tokens[:].indirect(entries))
 
-        for e in (2, 3):
-            gather(slot_bytes, x_bytes, e, e + 1)
-            gather(slot_words, x_words, e, e + 1)
-        for e in (4, 6, 0):
-            gather(slot_bytes, x_bytes, e, e + 2)
-            gather(slot_words, x_words, e, e + 1)
-            gather(slot_words, x_words, e + 1, e + 2)
+        for e0, e1 in GATHER_GROUPS:
+            gather(slot_bytes, x_bytes, e0, e1)
+            for e in range(e0, e1):
+                gather(slot_words, x_words, e, e + 1)
 
-        h_bf, turned = {}, {}
-        h_grouped = {}
-        h_words = {}
+        h_bf, turned, h_grouped, h_words = {}, {}, {}, {}
         h_bytes = sb("h_bytes", [P, S], U8)
+
+        def group(e0, e1, place=None):
+            tile = sb(f"h_grouped{e0}", [P, e1 - e0, C * PACK], BF16, place)
+            for e in range(e0, e1):
+                h_grouped[e] = (tile, e - e0)
+
+        def grouped(e0, e1):
+            tile, first = h_grouped[e0]
+            return tile[:, first : first + e1 - e0].rearrange("p e w -> p (e w)")
 
         def first_layer(e):
             slots = slice(e * C, (e + 1) * C)
@@ -210,11 +214,10 @@ def tile_moe_ecr_mlp_gelu_kernel(
                     start=True,
                     stop=True,
                 )
-            if e == 0:
-                h_grouped[0] = sb("h_grouped0", [P, SORTED * C * PACK], BF16)
-            part = h_grouped[0][:, e * C * PACK : (e + 1) * C * PACK]
             nc.scalar.activation(
-                part.rearrange("p (s t) -> p s t", t=PACK), acc[:].rearrange("p (t s) -> p s t", t=PACK), GELU
+                grouped(e, e + 1).rearrange("p (s t) -> p s t", t=PACK),
+                acc[:].rearrange("p (t s) -> p s t", t=PACK),
+                GELU,
             )
 
         def turn(e, e0):
@@ -226,16 +229,15 @@ def tile_moe_ecr_mlp_gelu_kernel(
                 nc.tensor.transpose(turned[e0][:, col : col + C], pairs[:, u * P : (u + 1) * P], ident[:])
 
         def interleave(e0, e1, copy):
-            h_grouped[e0] = sb(f"h_grouped{e0}", [P, (e1 - e0) * C * PACK], BF16)
             copy(
-                h_grouped[e0][:].bitcast(F32).rearrange("p (e s u) -> p e s u", s=C, u=2),
+                grouped(e0, e1).bitcast(F32).rearrange("p (e s u) -> p e s u", s=C, u=2),
                 turned[e0][:, : (e1 - e0) * 2 * C].rearrange("p (e u s) -> p e s u", s=C, u=2),
             )
 
         def quantise_h(e0, e1, place=None):
             words = sb(f"h_words{e0}", [P, (e1 - e0) * C], U32, place)
             nc.vector.quantize_mx(
-                out=words[:].bitcast(FP8X4), scales=h_bytes[:, e0 * C : e1 * C], in_=h_grouped[e0][:]
+                out=words[:].bitcast(FP8X4), scales=h_bytes[:, e0 * C : e1 * C], in_=grouped(e0, e1)
             )
             for e in range(e0, e1):
                 h_words[e] = words[:, (e - e0) * C : (e - e0 + 1) * C]
@@ -256,31 +258,34 @@ def tile_moe_ecr_mlp_gelu_kernel(
             copy(y[half][:, e0 * C : e1 * C], acc[:, : (e1 - e0) * C])
 
         on_vector, on_scalar = nc.vector.tensor_copy, nc.scalar.copy
-        for e in range(2, 6):
+        for e0, e1 in ((0, 1), (1, 3), (3, 5), (5, 7)):
+            group(e0, e1)
+        for e in range(3, 7):
             first_layer(e)
-        turn(2, 2)
-        first_layer(6)
+        turn(3, 3)
         first_layer(7)
-        turn(3, 2)
         turn(4, 4)
         first_layer_sorted(0)
-        turn(5, 4)
+        interleave(3, 4, on_scalar)
+        turn(5, 5)
+        turn(6, 5)
         first_layer_sorted(1)
-        turn(6, 6)
+        first_layer_sorted(2)
         turn(7, 7)
-        interleave(2, 4, on_vector)
-        interleave(4, 6, on_vector)
-        interleave(6, 7, on_scalar)
+        group(7, 8, "w1_sorted")
+        interleave(4, 5, on_vector)
+        interleave(5, 7, on_vector)
         interleave(7, 8, on_scalar)
-        quantise_h(2, 4, "h_bf5")
-        quantise_h(4, 6)
-        quantise_h(0, 2)
-        quantise_h(6, 7)
+        quantise_h(3, 5, "h_bf6")
+        quantise_h(0, 1)
+        quantise_h(5, 7)
+        quantise_h(1, 3)
         quantise_h(7, 8)
-        second_layer(0, 2, 6, on_scalar)
-        second_layer(0, 0, 2, on_vector)
-        second_layer(0, 6, 7, on_scalar)
-        second_layer(0, 7, 8, on_scalar)
+        second_layer(0, 3, 5, on_scalar)
+        second_layer(0, 0, 1, on_vector)
+        second_layer(0, 5, 7, on_scalar)
+        second_layer(0, 1, 3, on_scalar)
+        second_layer(0, 7, 8, on_vector)
         second_layer(1, 0, 4, on_scalar)
         second_layer(1, 4, 8, on_scalar)
 

@@ -300,13 +300,13 @@ def tile_moe_ecr_mlp_gelu_kernel(
                 MULT,
             )
 
-        def add_up(sums, half, r, a, b, final):
+        def add_up(sums, half, r, a, b, first, final):
             for t0 in range(a, b, P):
                 nc.tensor.matmul(
                     sums[:, t0 - a : t0 - a + P],
                     products[half][:, r, t0 : t0 + P],
                     ident[:],
-                    start=(r == 0 and t0 == a),
+                    start=(first and t0 == a),
                     stop=(final and t0 == b - P),
                     is_transpose=True,
                 )
@@ -319,28 +319,27 @@ def tile_moe_ecr_mlp_gelu_kernel(
                 nc.tensor.transpose(back[:, t0 : t0 + P], flipped[:, t0 : t0 + P], ident[:])
             return back
 
-        sums = [bank() for part in TOKEN_PARTS[0]]
-        for r in range(TOP):
-            fetch(0, r, 0, T)
-            for part, (a, b) in enumerate(TOKEN_PARTS[0]):
-                add_up(sums[part], 0, r, a, b, r == last)
         for part, (a, b) in enumerate(TOKEN_PARTS[0]):
-            back = turn_back(sums[part], 0, a, b)
+            sums = bank()
+            for r in range(TOP):
+                fetch(0, r, a, b)
+                add_up(sums, 0, r, a, b, r == 0, r == last)
+            back = turn_back(sums, 0, a, b)
             result = sb(f"result0{part}", [P, b - a], F32)
             nc.scalar.copy(result[:], back[:, : b - a])
             nc.sync.dma_start(out[:P, a:b], result[:])
         sums = [bank() for part in TOKEN_PARTS[1]]
-        for r in range(last - 1):
+        for r in range(last, 1, -1):
             fetch(1, r, 0, T)
             for part, (a, b) in enumerate(TOKEN_PARTS[1]):
-                add_up(sums[part], 1, r, a, b, False)
+                add_up(sums[part], 1, r, a, b, r == last, False)
         for part, (a, b) in enumerate(TOKEN_PARTS[1]):
-            fetch(1, last - 1, a, b)
-            add_up(sums[part], 1, last - 1, a, b, True)
+            fetch(1, 1, a, b)
+            add_up(sums[part], 1, 1, a, b, False, True)
         backs = [turn_back(sums[part], 1, a, b) for part, (a, b) in enumerate(TOKEN_PARTS[1])]
         for a, b in TOKEN_PARTS[1]:
-            fetch(1, last, a, b)
+            fetch(1, 0, a, b)
         for part, (a, b) in enumerate(TOKEN_PARTS[1]):
             result = sb(f"result1{part}", [P, b - a], F32)
-            nc.vector.tensor_tensor(result[:], backs[part][:, : b - a], products[1][:, last, a:b], ADD)
+            nc.vector.tensor_tensor(result[:], backs[part][:, : b - a], products[1][:, 0, a:b], ADD)
             nc.sync.dma_start(out[P:, a:b], result[:])

@@ -319,12 +319,13 @@ def tile_moe_ecr_mlp_gelu_kernel(
                 nc.tensor.transpose(back[:, t0 : t0 + P], flipped[:, t0 : t0 + P], ident[:])
             return back
 
+        sums = [bank() for part in TOKEN_PARTS[0]]
+        for r in range(TOP):
+            fetch(0, r, 0, T)
+            for part, (a, b) in enumerate(TOKEN_PARTS[0]):
+                add_up(sums[part], 0, r, a, b, r == 0, r == last)
         for part, (a, b) in enumerate(TOKEN_PARTS[0]):
-            sums = bank()
-            for r in range(TOP):
-                fetch(0, r, a, b)
-                add_up(sums, 0, r, a, b, r == 0, r == last)
-            back = turn_back(sums, 0, a, b)
+            back = turn_back(sums[part], 0, a, b)
             result = sb(f"result0{part}", [P, b - a], F32)
             nc.scalar.copy(result[:], back[:, : b - a])
             nc.sync.dma_start(out[:P, a:b], result[:])

@@ -284,17 +284,19 @@ def tile_moe_ecr_mlp_gelu_kernel(
         second_layer(0, 3, 5, on_scalar)
         second_layer(0, 0, 1, on_vector)
         second_layer(0, 5, 7, on_scalar)
-        second_layer(0, 1, 3, on_scalar)
-        second_layer(0, 7, 8, on_vector)
+        second_layer(0, 1, 2, on_vector)
+        second_layer(0, 2, 3, on_scalar)
+        second_layer(0, 7, 8, on_scalar)
         second_layer(1, 0, 4, on_scalar)
         second_layer(1, 4, 8, on_scalar)
 
         last = TOP - 1
-        products = [sb("products0", [P, TOP, T], F32), sb("products1", [P, TOP, T], F32, "y0")]
+        products = [by_expert(sb("products0", [P, TOP, T], F32))]
+        products.append(by_expert(sb("products1_late", [P, 2, T], F32, "y0"), sb("products1", [P, 2, T], F32)))
 
         def fetch(half, r, a, b):
             nc.vector.tensor_tensor(
-                products[half][:, r, a:b],
+                products[half][r][:, a:b],
                 y[half][:].indirect(pos[r][:, a // PER_COLUMN : b // PER_COLUMN]),
                 gates[r][:, a:b],
                 MULT,
@@ -304,7 +306,7 @@ def tile_moe_ecr_mlp_gelu_kernel(
             for t0 in range(a, b, P):
                 nc.tensor.matmul(
                     sums[:, t0 - a : t0 - a + P],
-                    products[half][:, r, t0 : t0 + P],
+                    products[half][r][:, t0 : t0 + P],
                     ident[:],
                     start=(first and t0 == a),
                     stop=(final and t0 == b - P),
@@ -342,5 +344,5 @@ def tile_moe_ecr_mlp_gelu_kernel(
             fetch(1, 0, a, b)
         for part, (a, b) in enumerate(TOKEN_PARTS[1]):
             result = sb(f"result1{part}", [P, b - a], F32)
-            nc.vector.tensor_tensor(result[:], backs[part][:, : b - a], products[1][:, 0, a:b], ADD)
+            nc.vector.tensor_tensor(result[:], backs[part][:, : b - a], products[1][0][:, a:b], ADD)
             nc.sync.dma_start(out[P:, a:b], result[:])

@@ -11,7 +11,6 @@ BANK = 512
 PACK = 4
 PER_COLUMN = 16
 SORTED = 3
-WARM_UPS = 2
 FLOPS = 2 * S * (K * H + H * N)
 
 F32 = mybir.dt.float32
@@ -89,11 +88,11 @@ def tile_moe_ecr_mlp_gelu_kernel(
         for r, source in enumerate((pos1, pos2, pos3, pos4)):
             pos.append(keep.tile([P, T // PER_COLUMN], U16, name=f"pos_sb{r}"))
             nc.sync.dma_start(pos[r][:], source)
-        gates = []
-        for r0 in (0, 2):
+        gates = {}
+        for r0, r1 in ((0, 3), (1, 2)):
             tile = sb(f"gate{r0}", [P, 2, T], F32)
-            nc.sync.dma_start(tile[:], gate[r0 : r0 + 2, :P, :].rearrange("r p t -> p r t"))
-            gates.extend([tile[:, 0, :], tile[:, 1, :]])
+            nc.sync.dma_start(tile[:], gate[r0 : r1 + 1 : r1 - r0, :P, :].rearrange("r p t -> p r t"))
+            gates[r0], gates[r1] = tile[:, 0, :], tile[:, 1, :]
 
         x_bytes = sb("x_bytes", [P, T], U8)
         nc.vector.memset(x_bytes[:].bitcast(I32), 0)
@@ -113,24 +112,6 @@ def tile_moe_ecr_mlp_gelu_kernel(
             nc.gpsimd.tensor_copy(
                 w1_sorted[:, e0:e1].rearrange("p e (t m) -> p e t m", t=PACK),
                 words_to_sort[:, e0:e1].bitcast(U16).rearrange("p e (m t) -> p e t m", t=PACK),
-            )
-
-        zeros = sb("zeros", [P, PACK * P], BF16)
-        nc.vector.memset(zeros[:].bitcast(I32), 0)
-        zero_words = sb("zero_words", [P, P], U32)
-        zero_bytes = sb("zero_bytes", [P, P], U8)
-        nc.vector.quantize_mx(out=zero_words[:].bitcast(FP8X4), scales=zero_bytes[:], in_=zeros[:])
-        plane_bytes = plane_first[:].rearrange("p e w -> p (e w)")
-        unused = bank()
-        for warm_up in range(WARM_UPS):
-            nc.tensor.matmul_mx(
-                out=unused[:],
-                lhsT=zero_words[:].bitcast(FP8X4),
-                lhsT_scale=zero_bytes[:],
-                rhs=plane_bytes[:, : 2 * H].bitcast(FP4X4),
-                rhs_scale=plane_bytes[:, 2 * H : 3 * H],
-                start=True,
-                stop=True,
             )
 
         x_words = sb("x_words", [P, T], U32)
@@ -287,62 +268,91 @@ def tile_moe_ecr_mlp_gelu_kernel(
         second_layer(0, 1, 2, on_vector)
         second_layer(0, 2, 3, on_scalar)
         second_layer(0, 7, 8, on_scalar)
-        second_layer(1, 0, 4, on_scalar)
-        second_layer(1, 4, 8, on_scalar)
 
-        last = TOP - 1
-        products = [by_expert(sb("products0", [P, TOP, T], F32))]
-        products.append(by_expert(sb("products1_late", [P, 2, T], F32, "y0"), sb("products1", [P, 2, T], F32)))
+        products = [by_expert(sb(f"products{half}", [P, TOP, T], F32)) for half in range(2)]
+        fetched = {}
 
-        def fetch(half, r, a, b):
+        def entries(r, a, b):
+            return pos[r][:, a // PER_COLUMN : b // PER_COLUMN]
+
+        def fetch_times_gate(half, r, a=0, b=T):
             nc.vector.tensor_tensor(
-                products[half][r][:, a:b],
-                y[half][:].indirect(pos[r][:, a // PER_COLUMN : b // PER_COLUMN]),
-                gates[r][:, a:b],
-                MULT,
+                products[half][r][:, a:b], y[half][:].indirect(entries(r, a, b)), gates[r][:, a:b], MULT
             )
 
-        def add_up(sums, half, r, a, b, first, final):
-            for t0 in range(a, b, P):
-                nc.tensor.matmul(
-                    sums[:, t0 - a : t0 - a + P],
-                    products[half][r][:, t0 : t0 + P],
-                    ident[:],
-                    start=(first and t0 == a),
-                    stop=(final and t0 == b - P),
-                    is_transpose=True,
-                )
+        def fetch(half, r, a=0, b=T):
+            fetched[half, r, a] = sb(f"fetched{half}{r}_{a}", [P, b - a], F32)
+            nc.scalar.activation(fetched[half, r, a][:], y[half][:].indirect(entries(r, a, b)), COPY)
 
-        def turn_back(sums, half, a, b):
+        def times_gate(half, r, a=0, b=T):
+            nc.vector.tensor_tensor(products[half][r][:, a:b], fetched[half, r, a][:], gates[r][:, a:b], MULT)
+
+        sums = [[bank() for part in TOKEN_PARTS[half]] for half in range(2)]
+
+        def add_up(half, r, first=False, final=False, only=None):
+            for part, (a, b) in enumerate(TOKEN_PARTS[half]):
+                if only is None or part == only:
+                    for t0 in range(a, b, P):
+                        nc.tensor.matmul(
+                            sums[half][part][:, t0 - a : t0 - a + P],
+                            products[half][r][:, t0 : t0 + P],
+                            ident[:],
+                            start=(first and t0 == a),
+                            stop=(final and t0 == b - P),
+                            is_transpose=True,
+                        )
+
+        backs = {}
+
+        def turn_back(half, part):
+            a, b = TOKEN_PARTS[half][part]
             flipped = sb(f"flipped{half}_{a}", [P, b - a], F32)
-            nc.scalar.copy(flipped[:], sums[:, : b - a])
-            back = bank()
+            nc.scalar.copy(flipped[:], sums[half][part][:, : b - a])
+            backs[half, part] = bank()
             for t0 in range(0, b - a, P):
-                nc.tensor.transpose(back[:, t0 : t0 + P], flipped[:, t0 : t0 + P], ident[:])
-            return back
+                nc.tensor.transpose(backs[half, part][:, t0 : t0 + P], flipped[:, t0 : t0 + P], ident[:])
 
-        sums = [bank() for part in TOKEN_PARTS[0]]
-        for r in range(TOP):
-            fetch(0, r, 0, T)
-            for part, (a, b) in enumerate(TOKEN_PARTS[0]):
-                add_up(sums[part], 0, r, a, b, r == 0, r == last)
-        for part, (a, b) in enumerate(TOKEN_PARTS[0]):
-            back = turn_back(sums[part], 0, a, b)
-            result = sb(f"result0{part}", [P, b - a], F32)
-            nc.scalar.copy(result[:], back[:, : b - a])
-            nc.sync.dma_start(out[:P, a:b], result[:])
-        sums = [bank() for part in TOKEN_PARTS[1]]
-        for r in range(last, 1, -1):
-            fetch(1, r, 0, T)
-            for part, (a, b) in enumerate(TOKEN_PARTS[1]):
-                add_up(sums[part], 1, r, a, b, r == last, False)
-        for part, (a, b) in enumerate(TOKEN_PARTS[1]):
-            fetch(1, 1, a, b)
-            add_up(sums[part], 1, 1, a, b, False, True)
-        backs = [turn_back(sums[part], 1, a, b) for part, (a, b) in enumerate(TOKEN_PARTS[1])]
+        def store(half, part):
+            a, b = TOKEN_PARTS[half][part]
+            result = sb(f"result{half}{part}", [P, b - a], F32)
+            if half == 0:
+                nc.scalar.copy(result[:], backs[half, part][:, : b - a])
+            else:
+                nc.vector.tensor_tensor(result[:], backs[half, part][:, : b - a], products[1][0][:, a:b], ADD)
+            nc.sync.dma_start(out[half * P : (half + 1) * P, a:b], result[:])
+
+        fetch(0, 1)
+        second_layer(1, 0, 4, on_scalar)
+        second_layer(1, 4, 8, on_scalar)
+        fetch_times_gate(0, 3)
+        add_up(0, 3, first=True)
+        fetch_times_gate(0, 0)
+        add_up(0, 0)
+        fetch(0, 2)
+        times_gate(0, 1)
+        add_up(0, 1)
+        fetch_times_gate(1, 3)
+        add_up(1, 3, first=True)
+        fetch(1, 1)
+        times_gate(0, 2)
+        add_up(0, 2, final=True)
         for a, b in TOKEN_PARTS[1]:
-            fetch(1, 0, a, b)
-        for part, (a, b) in enumerate(TOKEN_PARTS[1]):
-            result = sb(f"result1{part}", [P, b - a], F32)
-            nc.vector.tensor_tensor(result[:], backs[part][:, : b - a], products[1][0][:, a:b], ADD)
-            nc.sync.dma_start(out[P:, a:b], result[:])
+            fetch(1, 2, a, b)
+        times_gate(1, 1)
+        add_up(1, 1)
+        times_gate(1, 2, *TOKEN_PARTS[1][0])
+        add_up(1, 2, final=True, only=0)
+        turn_back(0, 0)
+        turn_back(0, 1)
+        fetch_times_gate(1, 0, *TOKEN_PARTS[1][0])
+        for part in (1, 2):
+            times_gate(1, 2, *TOKEN_PARTS[1][part])
+            add_up(1, 2, final=True, only=part)
+        for part in range(3):
+            turn_back(1, part)
+        for part in (1, 2):
+            fetch_times_gate(1, 0, *TOKEN_PARTS[1][part])
+        for part in range(2):
+            store(0, part)
+        for part in range(3):
+            store(1, part)

@@ -29,7 +29,8 @@ ADD = mybir.AluOpType.add
 X_CHUNKS = [(0, 256), (256, 512), (512, 640)]
 X_EIGHTHS_ON_VECTOR = 5
 GATHER_GROUPS = [(3, 4), (4, 5), (5, 7), (7, 8), (0, 1), (1, 3)]
-TOKEN_PARTS = [[(0, 3 * P), (3 * P, T)], [(0, 2 * P), (2 * P, 4 * P), (4 * P, T)]]
+TOKEN_PARTS = [[(0, 3 * P), (3 * P, T)], [(0, 3 * P), (3 * P, T)]]
+STORE_PARTS = [(0, 0, 3 * P), (1, 3 * P, 4 * P), (1, 4 * P, T)]
 
 
 def tile_moe_ecr_mlp_gelu_kernel(
@@ -89,7 +90,7 @@ def tile_moe_ecr_mlp_gelu_kernel(
             pos.append(keep.tile([P, T // PER_COLUMN], U16, name=f"pos_sb{r}"))
             nc.sync.dma_start(pos[r][:], source)
         gates = {}
-        for r0, r1 in ((0, 3), (1, 2)):
+        for r0, r1 in ((2, 3), (0, 1)):
             tile = sb(f"gate{r0}", [P, 2, T], F32)
             nc.sync.dma_start(tile[:], gate[r0 : r1 + 1 : r1 - r0, :P, :].rearrange("r p t -> p r t"))
             gates[r0], gates[r1] = tile[:, 0, :], tile[:, 1, :]
@@ -268,6 +269,7 @@ def tile_moe_ecr_mlp_gelu_kernel(
         second_layer(0, 1, 2, on_vector)
         second_layer(0, 2, 3, on_scalar)
         second_layer(0, 7, 8, on_scalar)
+        second_layer(1, 3, 7, on_vector)
 
         products = [by_expert(sb(f"products{half}", [P, TOP, T], F32)) for half in range(2)]
         fetched = {}
@@ -312,47 +314,45 @@ def tile_moe_ecr_mlp_gelu_kernel(
             for t0 in range(0, b - a, P):
                 nc.tensor.transpose(backs[half, part][:, t0 : t0 + P], flipped[:, t0 : t0 + P], ident[:])
 
-        def store(half, part):
-            a, b = TOKEN_PARTS[half][part]
-            result = sb(f"result{half}{part}", [P, b - a], F32)
-            if half == 0:
-                nc.scalar.copy(result[:], backs[half, part][:, : b - a])
-            else:
-                nc.vector.tensor_tensor(result[:], backs[half, part][:, : b - a], products[1][0][:, a:b], ADD)
-            nc.sync.dma_start(out[half * P : (half + 1) * P, a:b], result[:])
+        def store_half0(part):
+            a, b = TOKEN_PARTS[0][part]
+            nc.scalar.copy(result0[:, a:b], backs[0, part][:, : b - a])
 
+        fetch(0, 0)
         fetch(0, 1)
-        second_layer(1, 0, 4, on_scalar)
-        second_layer(1, 4, 8, on_scalar)
+        second_layer(1, 0, 3, on_scalar)
+        second_layer(1, 7, 8, on_scalar)
         fetch_times_gate(0, 3)
         add_up(0, 3, first=True)
-        fetch_times_gate(0, 0)
+        fetch_times_gate(0, 2)
+        add_up(0, 2)
+        times_gate(0, 0)
         add_up(0, 0)
-        fetch(0, 2)
         times_gate(0, 1)
-        add_up(0, 1)
+        add_up(0, 1, final=True)
+        fetch(1, 0)
         fetch_times_gate(1, 3)
         add_up(1, 3, first=True)
-        fetch(1, 1)
-        times_gate(0, 2)
-        add_up(0, 2, final=True)
-        for a, b in TOKEN_PARTS[1]:
-            fetch(1, 2, a, b)
-        times_gate(1, 1)
-        add_up(1, 1)
-        times_gate(1, 2, *TOKEN_PARTS[1][0])
-        add_up(1, 2, final=True, only=0)
+        times_gate(1, 0)
+        add_up(1, 0, final=True)
         turn_back(0, 0)
         turn_back(0, 1)
-        fetch_times_gate(1, 0, *TOKEN_PARTS[1][0])
-        for part in (1, 2):
-            times_gate(1, 2, *TOKEN_PARTS[1][part])
-            add_up(1, 2, final=True, only=part)
-        for part in range(3):
-            turn_back(1, part)
-        for part in (1, 2):
-            fetch_times_gate(1, 0, *TOKEN_PARTS[1][part])
-        for part in range(2):
-            store(0, part)
-        for part in range(3):
-            store(1, part)
+        for a, b in TOKEN_PARTS[1]:
+            fetch(1, 1, a, b)
+        fetch_times_gate(1, 2)
+        turn_back(1, 0)
+        turn_back(1, 1)
+        result0 = sb("result0", [P, T], F32)
+        store_half0(0)
+        store_half0(1)
+        nc.sync.dma_start(out[:P, :], result0[:])
+        pair = sb("pair", [P, T], F32)
+        for a, b in TOKEN_PARTS[1]:
+            times_gate(1, 1, a, b)
+        for a, b in TOKEN_PARTS[1]:
+            nc.vector.tensor_tensor(pair[:, a:b], products[1][1][:, a:b], products[1][2][:, a:b], ADD)
+        for part, a, b in STORE_PARTS:
+            first = TOKEN_PARTS[1][part][0]
+            result = sb(f"result1_{a}", [P, b - a], F32)
+            nc.vector.tensor_tensor(result[:], backs[1, part][:, a - first : b - first], pair[:, a:b], ADD)
+            nc.sync.dma_start(out[P:, a:b], result[:])

@@ -29,8 +29,8 @@ ADD = mybir.AluOpType.add
 X_CHUNKS = [(0, 256), (256, 512), (512, 640)]
 X_EIGHTHS_ON_VECTOR = 5
 GATHER_GROUPS = [(3, 4), (4, 5), (5, 7), (7, 8), (0, 1), (1, 3)]
-TOKEN_PARTS = [[(0, 3 * P), (3 * P, T)], [(0, 3 * P), (3 * P, T)]]
-STORE_PARTS = [(0, 0, 3 * P), (1, 3 * P, 4 * P), (1, 4 * P, T)]
+TOKEN_PARTS = [[(0, 2 * P), (2 * P, 4 * P), (4 * P, T)], [(0, 4 * P), (4 * P, T)]]
+STORE_PARTS = [(0, 0, 2 * P), (0, 2 * P, 4 * P), (1, 4 * P, T)]
 
 
 def tile_moe_ecr_mlp_gelu_kernel(
@@ -90,14 +90,16 @@ def tile_moe_ecr_mlp_gelu_kernel(
             pos.append(keep.tile([P, T // PER_COLUMN], U16, name=f"pos_sb{r}"))
             nc.sync.dma_start(pos[r][:], source)
         gates = {}
-        for r0, r1 in ((2, 3), (0, 1)):
+        for r0, r1 in ((0, 1), (2, 3)):
             tile = sb(f"gate{r0}", [P, 2, T], F32)
             nc.sync.dma_start(tile[:], gate[r0 : r1 + 1 : r1 - r0, :P, :].rearrange("r p t -> p r t"))
             gates[r0], gates[r1] = tile[:, 0, :], tile[:, 1, :]
 
         x_bytes = sb("x_bytes", [P, T], U8)
         nc.vector.memset(x_bytes[:].bitcast(I32), 0)
-        y = [sb(f"y{half}", [P, S + PAD], F32) for half in range(2)]
+        y = [sb("y0", [P, S + PAD], F32)]
+        products = [by_expert(sb(f"products{half}", [P, TOP, T], F32)) for half in range(2)]
+        y.append(sb("y1", [P, S + PAD], F32))
         nc.vector.memset(y[1][:, S:], 0.0)
         nc.scalar.activation(y[0][:, S:], y[1][:, S:], GELU)
         ident = sb("ident", [P, P], F32)
@@ -271,7 +273,6 @@ def tile_moe_ecr_mlp_gelu_kernel(
         second_layer(0, 7, 8, on_scalar)
         second_layer(1, 3, 7, on_vector)
 
-        products = [by_expert(sb(f"products{half}", [P, TOP, T], F32)) for half in range(2)]
         fetched = {}
 
         def entries(r, a, b):
@@ -316,43 +317,43 @@ def tile_moe_ecr_mlp_gelu_kernel(
 
         def store_half0(part):
             a, b = TOKEN_PARTS[0][part]
-            nc.scalar.copy(result0[:, a:b], backs[0, part][:, : b - a])
+            result = sb(f"result0{part}", [P, b - a], F32)
+            nc.scalar.copy(result[:], backs[0, part][:, : b - a])
+            nc.sync.dma_start(out[:P, a:b], result[:])
 
-        fetch(0, 0)
-        fetch(0, 1)
         second_layer(1, 0, 3, on_scalar)
         second_layer(1, 7, 8, on_scalar)
-        fetch_times_gate(0, 3)
-        add_up(0, 3, first=True)
-        fetch_times_gate(0, 2)
-        add_up(0, 2)
-        times_gate(0, 0)
-        add_up(0, 0)
-        times_gate(0, 1)
-        add_up(0, 1, final=True)
-        fetch(1, 0)
-        fetch_times_gate(1, 3)
+        fetch(1, 3)
+        fetch(1, 2)
+        fetch(0, 3)
+        for a, b in TOKEN_PARTS[0]:
+            fetch(0, 2, a, b)
+        fetch_times_gate(0, 0)
+        add_up(0, 0, first=True)
+        fetch_times_gate(0, 1)
+        add_up(0, 1)
+        times_gate(1, 3)
         add_up(1, 3, first=True)
-        times_gate(1, 0)
-        add_up(1, 0, final=True)
+        times_gate(1, 2)
+        add_up(1, 2)
+        fetch_times_gate(1, 1)
+        add_up(1, 1, final=True)
+        times_gate(0, 3)
+        add_up(0, 3)
+        for part, (a, b) in enumerate(TOKEN_PARTS[0]):
+            times_gate(0, 2, a, b)
+            add_up(0, 2, final=True, only=part)
+        for a, b in TOKEN_PARTS[1]:
+            fetch_times_gate(1, 0, a, b)
+        turn_back(1, 0)
         turn_back(0, 0)
         turn_back(0, 1)
-        for a, b in TOKEN_PARTS[1]:
-            fetch(1, 1, a, b)
-        fetch_times_gate(1, 2)
-        turn_back(1, 0)
         turn_back(1, 1)
-        result0 = sb("result0", [P, T], F32)
-        store_half0(0)
-        store_half0(1)
-        nc.sync.dma_start(out[:P, :], result0[:])
-        pair = sb("pair", [P, T], F32)
-        for a, b in TOKEN_PARTS[1]:
-            times_gate(1, 1, a, b)
-        for a, b in TOKEN_PARTS[1]:
-            nc.vector.tensor_tensor(pair[:, a:b], products[1][1][:, a:b], products[1][2][:, a:b], ADD)
+        turn_back(0, 2)
+        for part in range(3):
+            store_half0(part)
         for part, a, b in STORE_PARTS:
             first = TOKEN_PARTS[1][part][0]
             result = sb(f"result1_{a}", [P, b - a], F32)
-            nc.vector.tensor_tensor(result[:], backs[1, part][:, a - first : b - first], pair[:, a:b], ADD)
+            nc.vector.tensor_tensor(result[:], backs[1, part][:, a - first : b - first], products[1][0][:, a:b], ADD)
             nc.sync.dma_start(out[P:, a:b], result[:])

@@ -29,8 +29,8 @@ ADD = mybir.AluOpType.add
 X_CHUNKS = [(0, 256), (256, 512), (512, 640)]
 X_EIGHTHS_ON_VECTOR = 5
 GATHER_GROUPS = [(3, 4), (4, 5), (5, 7), (7, 8), (0, 1), (1, 3)]
-TOKEN_PARTS = [[(0, 2 * P), (2 * P, 4 * P), (4 * P, T)], [(0, 4 * P), (4 * P, T)]]
-STORE_PARTS = [(0, 0, 2 * P), (0, 2 * P, 4 * P), (1, 4 * P, T)]
+TOKEN_PARTS = [(0, 3 * P), (3 * P, T)]
+STORE_PARTS = [(0, 0, 3 * P), (1, 3 * P, 4 * P), (1, 4 * P, T)]
 
 
 def tile_moe_ecr_mlp_gelu_kernel(
@@ -89,17 +89,13 @@ def tile_moe_ecr_mlp_gelu_kernel(
         for r, source in enumerate((pos1, pos2, pos3, pos4)):
             pos.append(keep.tile([P, T // PER_COLUMN], U16, name=f"pos_sb{r}"))
             nc.sync.dma_start(pos[r][:], source)
-        gates = {}
-        for r0, r1 in ((0, 1), (2, 3)):
-            tile = sb(f"gate{r0}", [P, 2, T], F32)
-            nc.sync.dma_start(tile[:], gate[r0 : r1 + 1 : r1 - r0, :P, :].rearrange("r p t -> p r t"))
-            gates[r0], gates[r1] = tile[:, 0, :], tile[:, 1, :]
+        gate_sb = sb("gate_sb", [P, TOP, T], F32)
+        nc.sync.dma_start(gate_sb[:], gate[:, :P, :].rearrange("r p t -> p r t"))
+        gates = by_expert(gate_sb)
 
         x_bytes = sb("x_bytes", [P, T], U8)
         nc.vector.memset(x_bytes[:].bitcast(I32), 0)
-        y = [sb("y0", [P, S + PAD], F32)]
-        products = [by_expert(sb(f"products{half}", [P, TOP, T], F32)) for half in range(2)]
-        y.append(sb("y1", [P, S + PAD], F32))
+        y = [sb(f"y{half}", [P, S + PAD], F32) for half in range(2)]
         nc.vector.memset(y[1][:, S:], 0.0)
         nc.scalar.activation(y[0][:, S:], y[1][:, S:], GELU)
         ident = sb("ident", [P, P], F32)
@@ -273,6 +269,7 @@ def tile_moe_ecr_mlp_gelu_kernel(
         second_layer(0, 7, 8, on_scalar)
         second_layer(1, 3, 7, on_vector)
 
+        products = [[sb(f"products{half}{r}", [P, T], F32) for r in range(TOP)] for half in range(2)]
         fetched = {}
 
         def entries(r, a, b):
@@ -283,17 +280,17 @@ def tile_moe_ecr_mlp_gelu_kernel(
                 products[half][r][:, a:b], y[half][:].indirect(entries(r, a, b)), gates[r][:, a:b], MULT
             )
 
-        def fetch(half, r, a=0, b=T):
-            fetched[half, r, a] = sb(f"fetched{half}{r}_{a}", [P, b - a], F32)
+        def fetch(half, r, a=0, b=T, place=None):
+            fetched[half, r, a] = sb(f"fetched{half}{r}_{a}", [P, b - a], F32, place)
             nc.scalar.activation(fetched[half, r, a][:], y[half][:].indirect(entries(r, a, b)), COPY)
 
         def times_gate(half, r, a=0, b=T):
             nc.vector.tensor_tensor(products[half][r][:, a:b], fetched[half, r, a][:], gates[r][:, a:b], MULT)
 
-        sums = [[bank() for part in TOKEN_PARTS[half]] for half in range(2)]
+        sums = [[bank() for part in TOKEN_PARTS] for half in range(2)]
 
         def add_up(half, r, first=False, final=False, only=None):
-            for part, (a, b) in enumerate(TOKEN_PARTS[half]):
+            for part, (a, b) in enumerate(TOKEN_PARTS):
                 if only is None or part == only:
                     for t0 in range(a, b, P):
                         nc.tensor.matmul(
@@ -307,53 +304,61 @@ def tile_moe_ecr_mlp_gelu_kernel(
 
         backs = {}
 
+        flipped = {}
+
+        def empty(half, part):
+            a, b = TOKEN_PARTS[part]
+            flipped[half, part] = sb(f"flipped{half}_{a}", [P, b - a], F32)
+            nc.scalar.copy(flipped[half, part][:], sums[half][part][:, : b - a])
+
         def turn_back(half, part):
-            a, b = TOKEN_PARTS[half][part]
-            flipped = sb(f"flipped{half}_{a}", [P, b - a], F32)
-            nc.scalar.copy(flipped[:], sums[half][part][:, : b - a])
+            a, b = TOKEN_PARTS[part]
             backs[half, part] = bank()
             for t0 in range(0, b - a, P):
-                nc.tensor.transpose(backs[half, part][:, t0 : t0 + P], flipped[:, t0 : t0 + P], ident[:])
+                nc.tensor.transpose(backs[half, part][:, t0 : t0 + P], flipped[half, part][:, t0 : t0 + P], ident[:])
 
         def store_half0(part):
-            a, b = TOKEN_PARTS[0][part]
+            a, b = TOKEN_PARTS[part]
             result = sb(f"result0{part}", [P, b - a], F32)
             nc.scalar.copy(result[:], backs[0, part][:, : b - a])
             nc.sync.dma_start(out[:P, a:b], result[:])
 
+        early, late = TOKEN_PARTS
+        fetch(0, 0)
         second_layer(1, 0, 3, on_scalar)
         second_layer(1, 7, 8, on_scalar)
-        fetch(1, 3)
-        fetch(1, 2)
-        fetch(0, 3)
-        for a, b in TOKEN_PARTS[0]:
-            fetch(0, 2, a, b)
-        fetch_times_gate(0, 0)
-        add_up(0, 0, first=True)
-        fetch_times_gate(0, 1)
-        add_up(0, 1)
-        times_gate(1, 3)
-        add_up(1, 3, first=True)
-        times_gate(1, 2)
-        add_up(1, 2)
-        fetch_times_gate(1, 1)
-        add_up(1, 1, final=True)
-        times_gate(0, 3)
-        add_up(0, 3)
-        for part, (a, b) in enumerate(TOKEN_PARTS[0]):
-            times_gate(0, 2, a, b)
-            add_up(0, 2, final=True, only=part)
-        for a, b in TOKEN_PARTS[1]:
-            fetch_times_gate(1, 0, a, b)
-        turn_back(1, 0)
+        fetch(1, 0)
+        fetch(1, 1, *early)
+        fetch(1, 1, *late)
+        for r in (3, 2, 1):
+            fetch_times_gate(0, r)
+            add_up(0, r, first=(r == 3))
+        times_gate(0, 0)
+        add_up(0, 0, final=True)
+        times_gate(1, 0)
+        add_up(1, 0, first=True)
+        times_gate(1, 1, *early)
+        add_up(1, 1, only=0)
+        empty(0, 0)
+        empty(0, 1)
         turn_back(0, 0)
+        fetch_times_gate(1, 3, *early)
+        add_up(1, 3, final=True, only=0)
+        fetch_times_gate(1, 3, *late)
+        add_up(1, 3, only=1)
+        times_gate(1, 1, *late)
+        add_up(1, 1, final=True, only=1)
         turn_back(0, 1)
+        store_half0(0)
+        empty(1, 0)
+        turn_back(1, 0)
+        empty(1, 1)
         turn_back(1, 1)
-        turn_back(0, 2)
-        for part in range(3):
-            store_half0(part)
+        store_half0(1)
+        fetch_times_gate(1, 2, *early)
+        fetch_times_gate(1, 2, *late)
         for part, a, b in STORE_PARTS:
-            first = TOKEN_PARTS[1][part][0]
+            first = TOKEN_PARTS[part][0]
             result = sb(f"result1_{a}", [P, b - a], F32)
-            nc.vector.tensor_tensor(result[:], backs[1, part][:, a - first : b - first], products[1][0][:, a:b], ADD)
+            nc.vector.tensor_tensor(result[:], backs[1, part][:, a - first : b - first], products[1][2][:, a:b], ADD)
             nc.sync.dma_start(out[P:, a:b], result[:])

@@ -10,7 +10,7 @@ P = 128
 BANK = 512
 PACK = 4
 PER_COLUMN = 16
-SORTED = 3
+SORTED = [2, 6, 7]
 FLOPS = 2 * S * (K * H + H * N)
 
 F32 = mybir.dt.float32
@@ -28,7 +28,7 @@ ADD = mybir.AluOpType.add
 
 X_CHUNKS = [(0, 256), (256, 512), (512, 640)]
 X_EIGHTHS_ON_VECTOR = 5
-GATHER_GROUPS = [(3, 4), (4, 5), (5, 7), (7, 8), (0, 1), (1, 3)]
+GATHER_GROUPS = [(0, 1), (1, 2), (2, 3), (3, 5), (5, 6), (6, 8)]
 TOKEN_PARTS = [(0, 3 * P), (3 * P, T)]
 STORE_PARTS = [(0, 0, 3 * P), (1, 3 * P, 4 * P), (1, 4 * P, T)]
 
@@ -75,14 +75,15 @@ def tile_moe_ecr_mlp_gelu_kernel(
         def by_expert(*tiles):
             return [tile[:, e, :] for tile in tiles for e in range(tile.shape[1])]
 
-        plane_first = load_plane("w1_plane", w1_scales, 0, 5)
-        words_3_4 = load_words("w1_from3", w1_words, 3, 5)
-        words_5_6 = load_words("w1_from5", w1_words, 5, 7)
-        plane_rest = load_plane("w1_plane_rest", w1_scales, 5, E)
-        words_to_sort = load_words("w1_from0", w1_words, 0, SORTED)
-        words_7 = load_words("w1_from7", w1_words, 7, E)
+        plane_first = load_plane("w1_plane", w1_scales, 0, 3)
+        words_0_2 = load_words("w1_from0", w1_words, 0, 3)
+        plane_rest = load_plane("w1_plane_rest", w1_scales, 3, E)
+        words_3 = load_words("w1_from3", w1_words, 3, 4)
+        words_4 = load_words("w1_from4", w1_words, 4, 5)
+        words_6_7 = load_words("w1_from6", w1_words, 6, E)
+        words_5 = load_words("w1_from5", w1_words, 5, 6)
         w1_plane = by_expert(plane_first, plane_rest)
-        w1 = by_expert(words_to_sort, words_3_4, words_5_6, words_7)
+        w1 = by_expert(words_0_2, words_3, words_4, words_5, words_6_7)
         w2_plane = by_expert(load_plane("w2_plane", w2_scales, 0, E))
         w2 = by_expert(load_words("w2_all", w2_words, 0, E))
         pos = []
@@ -101,17 +102,18 @@ def tile_moe_ecr_mlp_gelu_kernel(
         ident = sb("ident", [P, P], F32)
         make_identity(nc, ident[:])
 
-        w1_sorted = sb("w1_sorted", [P, SORTED, H], U16)
-        plane_sorted = sb("plane_sorted", [P, SORTED, H], U8)
-        nc.gpsimd.tensor_copy(
-            plane_sorted[:].rearrange("p e (t m) -> p e t m", t=PACK),
-            plane_first[:, :SORTED].rearrange("p e (m t) -> p e t m", t=PACK),
-        )
-        for e0, e1 in ((0, 1), (1, SORTED)):
+        w1_sorted = sb("w1_sorted", [P, len(SORTED), H], U16)
+        plane_sorted = sb("plane_sorted", [P, len(SORTED), H], U8)
+        for s0, s1, plane in ((0, 1, plane_first[:, 2:]), (1, 3, plane_rest[:, 3:])):
             nc.gpsimd.tensor_copy(
-                w1_sorted[:, e0:e1].rearrange("p e (t m) -> p e t m", t=PACK),
-                words_to_sort[:, e0:e1].bitcast(U16).rearrange("p e (m t) -> p e t m", t=PACK),
+                plane_sorted[:, s0:s1].rearrange("p e (t m) -> p e t m", t=PACK),
+                plane.rearrange("p e (m t) -> p e t m", t=PACK),
             )
+            for s in range(s0, s1):
+                nc.gpsimd.tensor_copy(
+                    w1_sorted[:, s].rearrange("p (t m) -> p t m", t=PACK),
+                    w1[SORTED[s]].bitcast(U16).rearrange("p (m t) -> p t m", t=PACK),
+                )
 
         x_words = sb("x_words", [P, T], U32)
         x_bf = [sb(f"x_bf{chunk}", [P, b - a, PACK], BF16) for chunk, (a, b) in enumerate(X_CHUNKS)]
@@ -187,8 +189,8 @@ def tile_moe_ecr_mlp_gelu_kernel(
             for t in range(PACK):
                 nc.tensor.matmul_mx(
                     out=acc[:, t * C : (t + 1) * C],
-                    lhsT=w1_sorted[:, e, t * P : (t + 1) * P].bitcast(FP4X4),
-                    lhsT_scale=plane_sorted[:, e, t * P : (t + 1) * P],
+                    lhsT=w1_sorted[:, SORTED.index(e), t * P : (t + 1) * P].bitcast(FP4X4),
+                    lhsT_scale=plane_sorted[:, SORTED.index(e), t * P : (t + 1) * P],
                     rhs=slot_words[:, slots].bitcast(FP8X4),
                     rhs_scale=slot_bytes[:, slots],
                     start=True,
@@ -238,36 +240,38 @@ def tile_moe_ecr_mlp_gelu_kernel(
             copy(y[half][:, e0 * C : e1 * C], acc[:, : (e1 - e0) * C])
 
         on_vector, on_scalar = nc.vector.tensor_copy, nc.scalar.copy
-        for e0, e1 in ((0, 1), (1, 3), (3, 5), (5, 7)):
+        for e0, e1 in ((0, 2), (2, 3), (3, 5), (6, 8)):
             group(e0, e1)
-        for e in range(3, 7):
-            first_layer(e)
-        turn(3, 3)
-        first_layer(7)
-        turn(4, 4)
-        first_layer_sorted(0)
-        interleave(3, 4, on_scalar)
-        turn(5, 5)
-        turn(6, 5)
-        first_layer_sorted(1)
+        first_layer(0)
+        first_layer(1)
         first_layer_sorted(2)
-        turn(7, 7)
-        group(7, 8, "w1_sorted")
-        interleave(4, 5, on_vector)
-        interleave(5, 7, on_vector)
-        interleave(7, 8, on_scalar)
-        quantise_h(3, 5, "h_bf6")
-        quantise_h(0, 1)
-        quantise_h(5, 7)
-        quantise_h(1, 3)
-        quantise_h(7, 8)
+        first_layer(3)
+        first_layer(4)
+        turn(0, 0)
+        first_layer(5)
+        turn(1, 1)
+        interleave(0, 1, on_scalar)
+        turn(3, 3)
+        turn(4, 3)
+        first_layer_sorted(6)
+        first_layer_sorted(7)
+        turn(5, 5)
+        group(5, 6, "w1_sorted")
+        interleave(1, 2, on_vector)
+        interleave(3, 5, on_vector)
+        interleave(5, 6, on_scalar)
+        quantise_h(0, 2, "h_bf4")
+        quantise_h(2, 3)
+        quantise_h(3, 5)
+        quantise_h(6, 8)
+        quantise_h(5, 6)
+        second_layer(0, 0, 2, on_scalar)
+        second_layer(0, 2, 3, on_vector)
         second_layer(0, 3, 5, on_scalar)
-        second_layer(0, 0, 1, on_vector)
-        second_layer(0, 5, 7, on_scalar)
-        second_layer(0, 1, 2, on_vector)
-        second_layer(0, 2, 3, on_scalar)
+        second_layer(0, 6, 7, on_vector)
         second_layer(0, 7, 8, on_scalar)
-        second_layer(1, 3, 7, on_vector)
+        second_layer(0, 5, 6, on_scalar)
+        second_layer(1, 0, 4, on_vector)
 
         products = [[sb(f"products{half}{r}", [P, T], F32) for r in range(TOP)] for half in range(2)]
         fetched = {}
@@ -325,8 +329,7 @@ def tile_moe_ecr_mlp_gelu_kernel(
 
         early, late = TOKEN_PARTS
         fetch(0, 0)
-        second_layer(1, 0, 3, on_scalar)
-        second_layer(1, 7, 8, on_scalar)
+        second_layer(1, 4, 8, on_scalar)
         fetch(1, 0)
         fetch(1, 1, *early)
         fetch(1, 1, *late)

@@ -10,7 +10,7 @@ P = 128
 BANK = 512
 PACK = 4
 PER_COLUMN = 16
-SORTED = [2, 6, 7]
+SORTED = [1, 3, 6, 7]
 FLOPS = 2 * S * (K * H + H * N)
 
 F32 = mybir.dt.float32
@@ -28,9 +28,8 @@ ADD = mybir.AluOpType.add
 
 X_CHUNKS = [(0, 256), (256, 512), (512, 640)]
 X_EIGHTHS_ON_VECTOR = 5
-GATHER_GROUPS = [(0, 1), (1, 2), (2, 3), (3, 5), (5, 6), (6, 8)]
-TOKEN_PARTS = [(0, 3 * P), (3 * P, T)]
-STORE_PARTS = [(0, 0, 3 * P), (1, 3 * P, 4 * P), (1, 4 * P, T)]
+GATHER_GROUPS = [(0, 1), (1, 2), (2, 4), (4, 5), (5, 6), (6, 8)]
+TOKEN_PARTS = [[(0, 3 * P), (3 * P, T)], [(0, 2 * P), (2 * P, 4 * P), (4 * P, T)]]
 
 
 def tile_moe_ecr_mlp_gelu_kernel(
@@ -75,21 +74,23 @@ def tile_moe_ecr_mlp_gelu_kernel(
         def by_expert(*tiles):
             return [tile[:, e, :] for tile in tiles for e in range(tile.shape[1])]
 
-        plane_first = load_plane("w1_plane", w1_scales, 0, 3)
-        words_0_2 = load_words("w1_from0", w1_words, 0, 3)
-        plane_rest = load_plane("w1_plane_rest", w1_scales, 3, E)
-        words_3 = load_words("w1_from3", w1_words, 3, 4)
+        plane_first = load_plane("w1_plane", w1_scales, 0, 4)
+        words_0_1 = load_words("w1_from0", w1_words, 0, 2)
+        words_2_3 = load_words("w1_from2", w1_words, 2, 4)
+        plane_rest = load_plane("w1_plane_rest", w1_scales, 4, E)
         words_4 = load_words("w1_from4", w1_words, 4, 5)
         words_6_7 = load_words("w1_from6", w1_words, 6, E)
         words_5 = load_words("w1_from5", w1_words, 5, 6)
         w1_plane = by_expert(plane_first, plane_rest)
-        w1 = by_expert(words_0_2, words_3, words_4, words_5, words_6_7)
+        w1 = by_expert(words_0_1, words_2_3, words_4, words_5, words_6_7)
         w2_plane = by_expert(load_plane("w2_plane", w2_scales, 0, E))
         w2 = by_expert(load_words("w2_all", w2_words, 0, E))
         pos = []
         for r, source in enumerate((pos1, pos2, pos3, pos4)):
             pos.append(keep.tile([P, T // PER_COLUMN], U16, name=f"pos_sb{r}"))
             nc.sync.dma_start(pos[r][:], source)
+        gate_columns = sb("gate_columns", [P, 2, 2 * PACK], F32)
+        nc.sync.dma_start(gate_columns[:, :, :PACK], gate[:2, 0, :BANK].rearrange("r (p c) -> p r c", c=PACK))
         gate_sb = sb("gate_sb", [P, TOP, T], F32)
         nc.sync.dma_start(gate_sb[:], gate[:, :P, :].rearrange("r p t -> p r t"))
         gates = by_expert(gate_sb)
@@ -104,16 +105,24 @@ def tile_moe_ecr_mlp_gelu_kernel(
 
         w1_sorted = sb("w1_sorted", [P, len(SORTED), H], U16)
         plane_sorted = sb("plane_sorted", [P, len(SORTED), H], U8)
-        for s0, s1, plane in ((0, 1, plane_first[:, 2:]), (1, 3, plane_rest[:, 3:])):
+        def regroup_plane(s0, s1, plane):
             nc.gpsimd.tensor_copy(
                 plane_sorted[:, s0:s1].rearrange("p e (t m) -> p e t m", t=PACK),
                 plane.rearrange("p e (m t) -> p e t m", t=PACK),
             )
-            for s in range(s0, s1):
-                nc.gpsimd.tensor_copy(
-                    w1_sorted[:, s].rearrange("p (t m) -> p t m", t=PACK),
-                    w1[SORTED[s]].bitcast(U16).rearrange("p (m t) -> p t m", t=PACK),
-                )
+
+        def regroup_words(s, copy):
+            copy(
+                w1_sorted[:, s].rearrange("p (t m) -> p t m", t=PACK),
+                w1[SORTED[s]].bitcast(U16).rearrange("p (m t) -> p t m", t=PACK),
+            )
+
+        regroup_plane(0, 1, plane_first[:, 1:2])
+        regroup_plane(1, 2, plane_first[:, 3:4])
+        regroup_words(1, nc.gpsimd.tensor_copy)
+        regroup_plane(2, 4, plane_rest[:, 2:])
+        regroup_words(2, nc.gpsimd.tensor_copy)
+        regroup_words(3, nc.gpsimd.tensor_copy)
 
         x_words = sb("x_words", [P, T], U32)
         x_bf = [sb(f"x_bf{chunk}", [P, b - a, PACK], BF16) for chunk, (a, b) in enumerate(X_CHUNKS)]
@@ -140,6 +149,7 @@ def tile_moe_ecr_mlp_gelu_kernel(
         round_x(2)
         quantise_x(1)
         quantise_x(2)
+        regroup_words(0, nc.scalar.copy)
         slot_words = sb("slot_words", [P, S], U32)
         slot_bytes = sb("slot_bytes", [P, S], U8)
 
@@ -240,128 +250,140 @@ def tile_moe_ecr_mlp_gelu_kernel(
             copy(y[half][:, e0 * C : e1 * C], acc[:, : (e1 - e0) * C])
 
         on_vector, on_scalar = nc.vector.tensor_copy, nc.scalar.copy
-        for e0, e1 in ((0, 2), (2, 3), (3, 5), (6, 8)):
+        for e0, e1 in ((0, 2), (2, 4), (4, 5), (6, 8)):
             group(e0, e1)
         first_layer(0)
-        first_layer(1)
-        first_layer_sorted(2)
-        first_layer(3)
+        first_layer_sorted(1)
+        first_layer(2)
+        first_layer_sorted(3)
         first_layer(4)
         turn(0, 0)
         first_layer(5)
-        turn(1, 1)
-        interleave(0, 1, on_scalar)
-        turn(3, 3)
-        turn(4, 3)
+        turn(2, 2)
+        turn(4, 4)
         first_layer_sorted(6)
         first_layer_sorted(7)
         turn(5, 5)
         group(5, 6, "w1_sorted")
-        interleave(1, 2, on_vector)
-        interleave(3, 5, on_vector)
+        interleave(0, 1, on_vector)
+        interleave(2, 3, on_vector)
+        interleave(4, 5, on_vector)
         interleave(5, 6, on_scalar)
         quantise_h(0, 2, "h_bf4")
-        quantise_h(2, 3)
-        quantise_h(3, 5)
+        quantise_h(2, 4)
+        quantise_h(4, 5)
         quantise_h(6, 8)
         quantise_h(5, 6)
         second_layer(0, 0, 2, on_scalar)
-        second_layer(0, 2, 3, on_vector)
-        second_layer(0, 3, 5, on_scalar)
+        second_layer(0, 2, 4, on_scalar)
+        second_layer(0, 4, 5, on_vector)
         second_layer(0, 6, 7, on_vector)
         second_layer(0, 7, 8, on_scalar)
         second_layer(0, 5, 6, on_scalar)
         second_layer(1, 0, 4, on_vector)
 
-        products = [[sb(f"products{half}{r}", [P, T], F32) for r in range(TOP)] for half in range(2)]
-        fetched = {}
+        products, tails, fetched, spread = {}, {}, {}, {}
 
         def entries(r, a, b):
             return pos[r][:, a // PER_COLUMN : b // PER_COLUMN]
 
-        def fetch_times_gate(half, r, a=0, b=T):
-            nc.vector.tensor_tensor(
-                products[half][r][:, a:b], y[half][:].indirect(entries(r, a, b)), gates[r][:, a:b], MULT
-            )
+        def fetch_times_gate(half, r, place=None):
+            products[half, r] = sb(f"products{half}{r}", [P, T], F32, place)
+            tails[half, r] = products[half, r][:, BANK:]
+            nc.vector.tensor_tensor(products[half, r][:], y[half][:].indirect(pos[r][:]), gates[r], MULT)
 
         def fetch(half, r, a=0, b=T, place=None):
             fetched[half, r, a] = sb(f"fetched{half}{r}_{a}", [P, b - a], F32, place)
             nc.scalar.activation(fetched[half, r, a][:], y[half][:].indirect(entries(r, a, b)), COPY)
 
-        def times_gate(half, r, a=0, b=T):
-            nc.vector.tensor_tensor(products[half][r][:, a:b], fetched[half, r, a][:], gates[r][:, a:b], MULT)
+        def spread_gate(r):
+            spread[r] = bank()
+            for c in range(PACK):
+                nc.tensor.transpose(
+                    spread[r][:, c * P : (c + 1) * P], gate_columns[:, r, c : c + 1].to_broadcast([P, P]), ident[:]
+                )
 
-        sums = [[bank() for part in TOKEN_PARTS] for half in range(2)]
+        def times_gate(half, r):
+            nc.vector.tensor_tensor(
+                products[half, r][:, :BANK].rearrange("n (p c) -> n p c", c=PACK),
+                fetched[half, r, 0][:, :BANK].rearrange("n (p c) -> n p c", c=PACK),
+                spread[r][:].rearrange("n (c p) -> n p c", c=PACK),
+                MULT,
+            )
+            nc.gpsimd.tensor_tensor(tails[half, r], fetched[half, r, 0][:, BANK:], gates[r][:, BANK:], MULT)
 
-        def add_up(half, r, first=False, final=False, only=None):
-            for part, (a, b) in enumerate(TOKEN_PARTS):
-                if only is None or part == only:
-                    for t0 in range(a, b, P):
-                        nc.tensor.matmul(
-                            sums[half][part][:, t0 - a : t0 - a + P],
-                            products[half][r][:, t0 : t0 + P],
-                            ident[:],
-                            start=(first and t0 == a),
-                            stop=(final and t0 == b - P),
-                            is_transpose=True,
-                        )
+        sums = {}
+
+        def add_up(half, r, first=False, final=False):
+            for part, (a, b) in enumerate(TOKEN_PARTS[half]):
+                for t0 in range(a, b, P):
+                    nc.tensor.matmul(
+                        sums[half][part][:, t0 - a : t0 - a + P],
+                        products[half, r][:, t0 : t0 + P] if t0 < BANK else tails[half, r],
+                        ident[:],
+                        start=(first and t0 == a),
+                        stop=(final and t0 == b - P),
+                        is_transpose=True,
+                    )
 
         backs = {}
 
         flipped = {}
 
         def empty(half, part):
-            a, b = TOKEN_PARTS[part]
+            a, b = TOKEN_PARTS[half][part]
             flipped[half, part] = sb(f"flipped{half}_{a}", [P, b - a], F32)
             nc.scalar.copy(flipped[half, part][:], sums[half][part][:, : b - a])
 
         def turn_back(half, part):
-            a, b = TOKEN_PARTS[part]
+            a, b = TOKEN_PARTS[half][part]
             backs[half, part] = bank()
             for t0 in range(0, b - a, P):
                 nc.tensor.transpose(backs[half, part][:, t0 : t0 + P], flipped[half, part][:, t0 : t0 + P], ident[:])
 
-        def store_half0(part):
-            a, b = TOKEN_PARTS[part]
-            result = sb(f"result0{part}", [P, b - a], F32)
-            nc.scalar.copy(result[:], backs[0, part][:, : b - a])
-            nc.sync.dma_start(out[:P, a:b], result[:])
-
-        early, late = TOKEN_PARTS
+        EARLY = 3 * P
         fetch(0, 0)
         second_layer(1, 4, 8, on_scalar)
-        fetch(1, 0)
-        fetch(1, 1, *early)
-        fetch(1, 1, *late)
+        fetch(1, 1)
+        fetch(1, 2, 0, EARLY)
+        for half in range(2):
+            sums[half] = [bank() for part in range(2)]
+        for r in range(2):
+            spread_gate(r)
+        sums[1].append(bank())
         for r in (3, 2, 1):
             fetch_times_gate(0, r)
             add_up(0, r, first=(r == 3))
+        products[0, 0] = sb("products00", [P, BANK], F32, "products03")
+        products[1, 1] = sb("products11", [P, BANK + 2 * P], F32, "products02")
+        products[1, 2] = sb("products12", [P, T], F32, "products01")
+        tails[0, 0] = products[1, 1][:, BANK : BANK + P]
+        tails[1, 1] = products[1, 1][:, BANK + P :]
+        tails[1, 2] = products[1, 2][:, BANK:]
         times_gate(0, 0)
         add_up(0, 0, final=True)
-        times_gate(1, 0)
-        add_up(1, 0, first=True)
-        times_gate(1, 1, *early)
-        add_up(1, 1, only=0)
-        empty(0, 0)
-        empty(0, 1)
-        turn_back(0, 0)
-        fetch_times_gate(1, 3, *early)
-        add_up(1, 3, final=True, only=0)
-        fetch_times_gate(1, 3, *late)
-        add_up(1, 3, only=1)
-        times_gate(1, 1, *late)
-        add_up(1, 1, final=True, only=1)
-        turn_back(0, 1)
-        store_half0(0)
-        empty(1, 0)
-        turn_back(1, 0)
-        empty(1, 1)
-        turn_back(1, 1)
-        store_half0(1)
-        fetch_times_gate(1, 2, *early)
-        fetch_times_gate(1, 2, *late)
-        for part, a, b in STORE_PARTS:
-            first = TOKEN_PARTS[part][0]
+        times_gate(1, 1)
+        add_up(1, 1, first=True)
+        for part in range(2):
+            empty(0, part)
+        fetch(1, 2, EARLY, T, "products02")
+        result0 = sb("result0", [P, T], F32)
+        for part, (a, b) in enumerate(TOKEN_PARTS[0]):
+            turn_back(0, part)
+            nc.scalar.copy(result0[:, a:b], backs[0, part][:, : b - a])
+        nc.sync.dma_start(out[:P], result0[:])
+        fetch_times_gate(1, 3, "fetched00_0")
+        add_up(1, 3)
+        last = {}
+        for (a, b), (c, d), place in (((0, EARLY), (BANK, T), "fetched11_0"), ((EARLY, T), (0, BANK), "flipped0_384")):
+            nc.vector.tensor_tensor(products[1, 2][:, a:b], fetched[1, 2, a][:], gates[2][:, a:b], MULT)
+            last[c] = sb(f"last{c}", [P, T], F32, place)
+            nc.vector.tensor_tensor(last[c][:, c:d], y[1][:].indirect(entries(0, c, d)), gates[0][:, c:d], MULT)
+        add_up(1, 2, final=True)
+        for part in range(3):
+            empty(1, part)
+            turn_back(1, part)
+        for part, (a, b) in enumerate(TOKEN_PARTS[1]):
             result = sb(f"result1_{a}", [P, b - a], F32)
-            nc.vector.tensor_tensor(result[:], backs[1, part][:, a - first : b - first], products[1][2][:, a:b], ADD)
+            nc.vector.tensor_tensor(result[:], backs[1, part][:, : b - a], last[BANK if a == BANK else 0][:, a:b], ADD)
             nc.sync.dma_start(out[P:, a:b], result[:])

@@ -75,14 +75,14 @@ def tile_moe_ecr_mlp_gelu_kernel(
             return [tile[:, e, :] for tile in tiles for e in range(tile.shape[1])]
 
         plane_first = load_plane("w1_plane", w1_scales, 0, 4)
-        words_0_1 = load_words("w1_from0", w1_words, 0, 2)
+        words_0 = load_words("w1_from0", w1_words, 0, 1)
+        words_1 = load_words("w1_from1", w1_words, 1, 2)
         words_2_3 = load_words("w1_from2", w1_words, 2, 4)
         plane_rest = load_plane("w1_plane_rest", w1_scales, 4, E)
-        words_4 = load_words("w1_from4", w1_words, 4, 5)
+        words_4_5 = load_words("w1_from4", w1_words, 4, 6)
         words_6_7 = load_words("w1_from6", w1_words, 6, E)
-        words_5 = load_words("w1_from5", w1_words, 5, 6)
         w1_plane = by_expert(plane_first, plane_rest)
-        w1 = by_expert(words_0_1, words_2_3, words_4, words_5, words_6_7)
+        w1 = by_expert(words_0, words_1, words_2_3, words_4_5, words_6_7)
         w2_plane = by_expert(load_plane("w2_plane", w2_scales, 0, E))
         w2 = by_expert(load_words("w2_all", w2_words, 0, E))
         pos = []
@@ -103,26 +103,26 @@ def tile_moe_ecr_mlp_gelu_kernel(
         ident = sb("ident", [P, P], F32)
         make_identity(nc, ident[:])
 
-        w1_sorted = sb("w1_sorted", [P, len(SORTED), H], U16)
-        plane_sorted = sb("plane_sorted", [P, len(SORTED), H], U8)
-        def regroup_plane(s0, s1, plane):
+        words_early = sb("words_early", [P, 2, H], U16)
+        w1_sorted = by_expert(words_early)
+        plane_1 = sb("plane_1", [P, 1, H], U8)
+        plane_3 = sb("plane_3", [P, 1, H], U8)
+        def regroup_plane(regrouped, plane):
             nc.gpsimd.tensor_copy(
-                plane_sorted[:, s0:s1].rearrange("p e (t m) -> p e t m", t=PACK),
+                regrouped.rearrange("p e (t m) -> p e t m", t=PACK),
                 plane.rearrange("p e (m t) -> p e t m", t=PACK),
             )
 
         def regroup_words(s, copy):
             copy(
-                w1_sorted[:, s].rearrange("p (t m) -> p t m", t=PACK),
+                w1_sorted[s].rearrange("p (t m) -> p t m", t=PACK),
                 w1[SORTED[s]].bitcast(U16).rearrange("p (m t) -> p t m", t=PACK),
             )
 
-        regroup_plane(0, 1, plane_first[:, 1:2])
-        regroup_plane(1, 2, plane_first[:, 3:4])
+        regroup_plane(plane_1[:], plane_first[:, 1:2])
+        regroup_plane(plane_3[:], plane_first[:, 3:4])
         regroup_words(1, nc.gpsimd.tensor_copy)
-        regroup_plane(2, 4, plane_rest[:, 2:])
-        regroup_words(2, nc.gpsimd.tensor_copy)
-        regroup_words(3, nc.gpsimd.tensor_copy)
+        plane_sorted = by_expert(plane_1, plane_3)
 
         x_words = sb("x_words", [P, T], U32)
         x_bf = [sb(f"x_bf{chunk}", [P, b - a, PACK], BF16) for chunk, (a, b) in enumerate(X_CHUNKS)]
@@ -174,7 +174,7 @@ def tile_moe_ecr_mlp_gelu_kernel(
             tile, first = h_grouped[e0]
             return tile[:, first : first + e1 - e0].rearrange("p e w -> p (e w)")
 
-        def first_layer(e):
+        def first_layer(e, place=None):
             slots = slice(e * C, (e + 1) * C)
             acc = bank()
             nc.tensor.matmul_mx(
@@ -186,7 +186,7 @@ def tile_moe_ecr_mlp_gelu_kernel(
                 start=True,
                 stop=True,
             )
-            h_bf[e] = sb(f"h_bf{e}", [P, H], BF16)
+            h_bf[e] = sb(f"h_bf{e}", [P, H], BF16, place)
             nc.scalar.activation(
                 h_bf[e][:].rearrange("s (u p d) -> s u p d", u=2, d=2),
                 acc[:].rearrange("s (p u d) -> s u p d", u=2, d=2),
@@ -199,8 +199,8 @@ def tile_moe_ecr_mlp_gelu_kernel(
             for t in range(PACK):
                 nc.tensor.matmul_mx(
                     out=acc[:, t * C : (t + 1) * C],
-                    lhsT=w1_sorted[:, SORTED.index(e), t * P : (t + 1) * P].bitcast(FP4X4),
-                    lhsT_scale=plane_sorted[:, SORTED.index(e), t * P : (t + 1) * P],
+                    lhsT=w1_sorted[SORTED.index(e)][:, t * P : (t + 1) * P].bitcast(FP4X4),
+                    lhsT_scale=plane_sorted[SORTED.index(e)][:, t * P : (t + 1) * P],
                     rhs=slot_words[:, slots].bitcast(FP8X4),
                     rhs_scale=slot_bytes[:, slots],
                     start=True,
@@ -252,9 +252,16 @@ def tile_moe_ecr_mlp_gelu_kernel(
         on_vector, on_scalar = nc.vector.tensor_copy, nc.scalar.copy
         for e0, e1 in ((0, 2), (2, 4), (4, 5), (6, 8)):
             group(e0, e1)
-        first_layer(0)
+        first_layer(0, "w1_from1")
         first_layer_sorted(1)
         first_layer(2)
+        late = sb("late", [P, 2, 3 * H], U8, "plane_1")
+        planes_late = late[:, :, :H]
+        w1_sorted.extend(by_expert(late[:, :, H:].bitcast(U16)))
+        regroup_plane(planes_late, plane_rest[:, 2:])
+        regroup_words(2, nc.gpsimd.tensor_copy)
+        regroup_words(3, nc.gpsimd.tensor_copy)
+        plane_sorted.extend(by_expert(planes_late))
         first_layer_sorted(3)
         first_layer(4)
         turn(0, 0)
@@ -264,7 +271,7 @@ def tile_moe_ecr_mlp_gelu_kernel(
         first_layer_sorted(6)
         first_layer_sorted(7)
         turn(5, 5)
-        group(5, 6, "w1_sorted")
+        group(5, 6, "plane_1")
         interleave(0, 1, on_vector)
         interleave(2, 3, on_vector)
         interleave(4, 5, on_vector)

@@ -89,8 +89,8 @@ def tile_moe_ecr_mlp_gelu_kernel(
         for r, source in enumerate((pos1, pos2, pos3, pos4)):
             pos.append(keep.tile([P, T // PER_COLUMN], U16, name=f"pos_sb{r}"))
             nc.sync.dma_start(pos[r][:], source)
-        gate_columns = sb("gate_columns", [P, 2, 2 * PACK], F32)
-        nc.sync.dma_start(gate_columns[:, :, :PACK], gate[:2, 0, :BANK].rearrange("r (p c) -> p r c", c=PACK))
+        gate_columns = sb("gate_columns", [P, 3, 2 * PACK], F32)
+        nc.sync.dma_start(gate_columns[:, :, :PACK], gate[:3, 0, :BANK].rearrange("r (p c) -> p r c", c=PACK))
         gate_sb = sb("gate_sb", [P, TOP, T], F32)
         nc.sync.dma_start(gate_sb[:], gate[:, :P, :].rearrange("r p t -> p r t"))
         gates = by_expert(gate_sb)
@@ -299,9 +299,9 @@ def tile_moe_ecr_mlp_gelu_kernel(
             tails[half, r] = products[half, r][:, BANK:]
             nc.vector.tensor_tensor(products[half, r][:], y[half][:].indirect(pos[r][:]), gates[r], MULT)
 
-        def fetch(half, r, a=0, b=T, place=None):
-            fetched[half, r, a] = sb(f"fetched{half}{r}_{a}", [P, b - a], F32, place)
-            nc.scalar.activation(fetched[half, r, a][:], y[half][:].indirect(entries(r, a, b)), COPY)
+        def fetch(half, r):
+            fetched[half, r] = sb(f"fetched{half}{r}", [P, T], F32)
+            nc.scalar.activation(fetched[half, r][:], y[half][:].indirect(pos[r][:]), COPY)
 
         def spread_gate(r):
             spread[r] = bank()
@@ -313,11 +313,11 @@ def tile_moe_ecr_mlp_gelu_kernel(
         def times_gate(half, r):
             nc.vector.tensor_tensor(
                 products[half, r][:, :BANK].rearrange("n (p c) -> n p c", c=PACK),
-                fetched[half, r, 0][:, :BANK].rearrange("n (p c) -> n p c", c=PACK),
+                fetched[half, r][:, :BANK].rearrange("n (p c) -> n p c", c=PACK),
                 spread[r][:].rearrange("n (c p) -> n p c", c=PACK),
                 MULT,
             )
-            nc.gpsimd.tensor_tensor(tails[half, r], fetched[half, r, 0][:, BANK:], gates[r][:, BANK:], MULT)
+            nc.gpsimd.tensor_tensor(tails[half, r], fetched[half, r][:, BANK:], gates[r][:, BANK:], MULT)
 
         sums = {}
 
@@ -348,14 +348,13 @@ def tile_moe_ecr_mlp_gelu_kernel(
             for t0 in range(0, b - a, P):
                 nc.tensor.transpose(backs[half, part][:, t0 : t0 + P], flipped[half, part][:, t0 : t0 + P], ident[:])
 
-        EARLY = 3 * P
         fetch(0, 0)
         second_layer(1, 4, 8, on_scalar)
         fetch(1, 1)
-        fetch(1, 2, 0, EARLY)
+        fetch(1, 2)
         for half in range(2):
             sums[half] = [bank() for part in range(2)]
-        for r in range(2):
+        for r in range(3):
             spread_gate(r)
         sums[1].append(bank())
         for r in (3, 2, 1):
@@ -373,24 +372,20 @@ def tile_moe_ecr_mlp_gelu_kernel(
         add_up(1, 1, first=True)
         for part in range(2):
             empty(0, part)
-        fetch(1, 2, EARLY, T, "products02")
         result0 = sb("result0", [P, T], F32)
         for part, (a, b) in enumerate(TOKEN_PARTS[0]):
             turn_back(0, part)
             nc.scalar.copy(result0[:, a:b], backs[0, part][:, : b - a])
         nc.sync.dma_start(out[:P], result0[:])
-        fetch_times_gate(1, 3, "fetched00_0")
+        fetch_times_gate(1, 3, "fetched00")
         add_up(1, 3)
-        last = {}
-        for (a, b), (c, d), place in (((0, EARLY), (BANK, T), "fetched11_0"), ((EARLY, T), (0, BANK), "flipped0_384")):
-            nc.vector.tensor_tensor(products[1, 2][:, a:b], fetched[1, 2, a][:], gates[2][:, a:b], MULT)
-            last[c] = sb(f"last{c}", [P, T], F32, place)
-            nc.vector.tensor_tensor(last[c][:, c:d], y[1][:].indirect(entries(0, c, d)), gates[0][:, c:d], MULT)
+        times_gate(1, 2)
         add_up(1, 2, final=True)
         for part in range(3):
             empty(1, part)
             turn_back(1, part)
+        fetch_times_gate(1, 0, "fetched11")
         for part, (a, b) in enumerate(TOKEN_PARTS[1]):
             result = sb(f"result1_{a}", [P, b - a], F32)
-            nc.vector.tensor_tensor(result[:], backs[1, part][:, : b - a], last[BANK if a == BANK else 0][:, a:b], ADD)
+            nc.vector.tensor_tensor(result[:], backs[1, part][:, : b - a], products[1, 0][:, a:b], ADD)
             nc.sync.dma_start(out[P:, a:b], result[:])

@@ -285,9 +285,8 @@ def tile_moe_ecr_mlp_gelu_kernel(
         second_layer(0, 2, 4, on_scalar)
         second_layer(0, 4, 5, on_vector)
         second_layer(0, 6, 7, on_vector)
-        second_layer(0, 7, 8, on_scalar)
+        second_layer(0, 7, 8, on_vector)
         second_layer(0, 5, 6, on_scalar)
-        second_layer(1, 0, 4, on_vector)
 
         products, tails, fetched, spread = {}, {}, {}, {}
 
@@ -310,13 +309,15 @@ def tile_moe_ecr_mlp_gelu_kernel(
                     spread[r][:, c * P : (c + 1) * P], gate_columns[:, r, c : c + 1].to_broadcast([P, P]), ident[:]
                 )
 
-        def times_gate(half, r):
-            nc.vector.tensor_tensor(
-                products[half, r][:, :BANK].rearrange("n (p c) -> n p c", c=PACK),
-                fetched[half, r][:, :BANK].rearrange("n (p c) -> n p c", c=PACK),
-                spread[r][:].rearrange("n (c p) -> n p c", c=PACK),
-                MULT,
-            )
+        def times_gate(half, r, pieces=1):
+            step = P // pieces
+            for p0 in range(0, P, step):
+                nc.vector.tensor_tensor(
+                    products[half, r][:, :BANK].rearrange("n (p c) -> n p c", c=PACK)[:, p0 : p0 + step],
+                    fetched[half, r][:, :BANK].rearrange("n (p c) -> n p c", c=PACK)[:, p0 : p0 + step],
+                    spread[r][:].rearrange("n (c p) -> n p c", c=PACK)[:, p0 : p0 + step],
+                    MULT,
+                )
             nc.gpsimd.tensor_tensor(tails[half, r], fetched[half, r][:, BANK:], gates[r][:, BANK:], MULT)
 
         sums = {}
@@ -349,6 +350,7 @@ def tile_moe_ecr_mlp_gelu_kernel(
                 nc.tensor.transpose(backs[half, part][:, t0 : t0 + P], flipped[half, part][:, t0 : t0 + P], ident[:])
 
         fetch(0, 0)
+        second_layer(1, 0, 4, on_scalar)
         second_layer(1, 4, 8, on_scalar)
         fetch(1, 1)
         fetch(1, 2)
@@ -379,7 +381,7 @@ def tile_moe_ecr_mlp_gelu_kernel(
         nc.sync.dma_start(out[:P], result0[:])
         fetch_times_gate(1, 3, "fetched00")
         add_up(1, 3)
-        times_gate(1, 2)
+        times_gate(1, 2, pieces=2)
         add_up(1, 2, final=True)
         for part in range(3):
             empty(1, part)

@@ -250,7 +250,7 @@ def tile_moe_ecr_mlp_gelu_kernel(
             copy(y[half][:, e0 * C : e1 * C], acc[:, : (e1 - e0) * C])
 
         on_vector, on_scalar = nc.vector.tensor_copy, nc.scalar.copy
-        for e0, e1 in ((0, 2), (2, 4), (4, 5), (6, 8)):
+        for e0, e1 in ((0, 2), (2, 4), (4, 5), (5, 6), (6, 8)):
             group(e0, e1)
         first_layer(0, "w1_from1")
         first_layer_sorted(1)
@@ -271,22 +271,22 @@ def tile_moe_ecr_mlp_gelu_kernel(
         first_layer_sorted(6)
         first_layer_sorted(7)
         turn(5, 5)
-        group(5, 6, "plane_1")
         interleave(0, 1, on_vector)
         interleave(2, 3, on_vector)
         interleave(4, 5, on_vector)
-        interleave(5, 6, on_scalar)
         quantise_h(0, 2, "h_bf4")
         quantise_h(2, 4)
         quantise_h(4, 5)
-        quantise_h(6, 8)
+        interleave(5, 6, on_vector)
+        quantise_h(6, 7)
         quantise_h(5, 6)
+        quantise_h(7, 8)
         second_layer(0, 0, 2, on_scalar)
         second_layer(0, 2, 4, on_scalar)
         second_layer(0, 4, 5, on_vector)
         second_layer(0, 6, 7, on_vector)
-        second_layer(0, 7, 8, on_vector)
-        second_layer(0, 5, 6, on_scalar)
+        second_layer(0, 5, 6, on_vector)
+        second_layer(0, 7, 8, on_scalar)
 
         products, tails, fetched, spread = {}, {}, {}, {}
 

@@ -28,7 +28,7 @@ ADD = mybir.AluOpType.add
 
 X_CHUNKS = [(0, 256), (256, 512), (512, 640)]
 X_EIGHTHS_ON_VECTOR = 5
-GATHER_GROUPS = [(0, 1), (1, 2), (2, 4), (4, 5), (5, 6), (6, 8)]
+GATHER_GROUPS = [(0, 1), (1, 2), (2, 4), (4, 5), (5, 6), (6, 7), (7, 8)]
 TOKEN_PARTS = [[(0, 3 * P), (3 * P, T)], [(0, 2 * P), (2 * P, 4 * P), (4 * P, T)]]
 
 
@@ -293,10 +293,12 @@ def tile_moe_ecr_mlp_gelu_kernel(
         def entries(r, a, b):
             return pos[r][:, a // PER_COLUMN : b // PER_COLUMN]
 
-        def fetch_times_gate(half, r, place=None):
+        def fetch_times_gate(half, r, place=None, end=T):
             products[half, r] = sb(f"products{half}{r}", [P, T], F32, place)
             tails[half, r] = products[half, r][:, BANK:]
-            nc.vector.tensor_tensor(products[half, r][:], y[half][:].indirect(pos[r][:]), gates[r], MULT)
+            nc.vector.tensor_tensor(
+                products[half, r][:, :end], y[half][:].indirect(entries(r, 0, end)), gates[r][:, :end], MULT
+            )
 
         def fetch(half, r):
             fetched[half, r] = sb(f"fetched{half}{r}", [P, T], F32)
@@ -322,9 +324,9 @@ def tile_moe_ecr_mlp_gelu_kernel(
 
         sums = {}
 
-        def add_up(half, r, first=False, final=False):
+        def add_up(half, r, first=False, final=False, parts=None):
             for part, (a, b) in enumerate(TOKEN_PARTS[half]):
-                for t0 in range(a, b, P):
+                for t0 in range(a, b, P) if parts is None or part in parts else ():
                     nc.tensor.matmul(
                         sums[half][part][:, t0 - a : t0 - a + P],
                         products[half, r][:, t0 : t0 + P] if t0 < BANK else tails[half, r],
@@ -379,10 +381,14 @@ def tile_moe_ecr_mlp_gelu_kernel(
             turn_back(0, part)
             nc.scalar.copy(result0[:, a:b], backs[0, part][:, : b - a])
         nc.sync.dma_start(out[:P], result0[:])
-        fetch_times_gate(1, 3, "fetched00")
-        add_up(1, 3)
+        fetch_times_gate(1, 3, "fetched00", end=BANK)
+        add_up(1, 3, parts=(0, 1))
         times_gate(1, 2, pieces=2)
-        add_up(1, 2, final=True)
+        add_up(1, 2, final=True, parts=(0, 1))
+        tails[1, 3] = sb("tail13", [P, T - BANK], F32)[:]
+        nc.vector.tensor_tensor(tails[1, 3], y[1][:].indirect(entries(3, BANK, T)), gates[3][:, BANK:], MULT)
+        add_up(1, 2, parts=(2,))
+        add_up(1, 3, final=True, parts=(2,))
         for part in range(3):
             empty(1, part)
             turn_back(1, part)

@@ -105,8 +105,6 @@ def tile_moe_ecr_mlp_gelu_kernel(
 
         words_early = sb("words_early", [P, 2, H], U16)
         w1_sorted = by_expert(words_early)
-        plane_1 = sb("plane_1", [P, 1, H], U8)
-        plane_3 = sb("plane_3", [P, 1, H], U8)
         def regroup_plane(regrouped, plane):
             nc.gpsimd.tensor_copy(
                 regrouped.rearrange("p e (t m) -> p e t m", t=PACK),
@@ -119,10 +117,6 @@ def tile_moe_ecr_mlp_gelu_kernel(
                 w1[SORTED[s]].bitcast(U16).rearrange("p (m t) -> p t m", t=PACK),
             )
 
-        regroup_plane(plane_1[:], plane_first[:, 1:2])
-        regroup_plane(plane_3[:], plane_first[:, 3:4])
-        regroup_words(1, nc.gpsimd.tensor_copy)
-        plane_sorted = by_expert(plane_1, plane_3)
 
         x_words = sb("x_words", [P, T], U32)
         x_bf = [sb(f"x_bf{chunk}", [P, b - a, PACK], BF16) for chunk, (a, b) in enumerate(X_CHUNKS)]
@@ -150,6 +144,11 @@ def tile_moe_ecr_mlp_gelu_kernel(
         quantise_x(1)
         quantise_x(2)
         regroup_words(0, nc.scalar.copy)
+        planes_early = sb("planes_early", [P, 2, H], U8, "x_bf2")
+        regroup_plane(planes_early[:, :1], plane_first[:, 1:2])
+        regroup_plane(planes_early[:, 1:], plane_first[:, 3:4])
+        regroup_words(1, nc.gpsimd.tensor_copy)
+        plane_sorted = by_expert(planes_early)
         slot_words = sb("slot_words", [P, S], U32)
         slot_bytes = sb("slot_bytes", [P, S], U8)
 
@@ -255,7 +254,7 @@ def tile_moe_ecr_mlp_gelu_kernel(
         first_layer(0, "w1_from1")
         first_layer_sorted(1)
         first_layer(2)
-        late = sb("late", [P, 2, 3 * H], U8, "plane_1")
+        late = sb("late", [P, 2, 3 * H], U8, "w1_from0")
         planes_late = late[:, :, :H]
         w1_sorted.extend(by_expert(late[:, :, H:].bitcast(U16)))
         regroup_plane(planes_late, plane_rest[:, 2:])

@@ -27,7 +27,7 @@ MULT = mybir.AluOpType.mult
 ADD = mybir.AluOpType.add
 
 X_CHUNKS = [(0, 256), (256, 512), (512, 640)]
-X_EIGHTHS_ON_VECTOR = 5
+X_SIXTEENTHS_ON_VECTOR = 9
 GATHER_GROUPS = [(0, 1), (1, 2), (2, 4), (4, 5), (5, 6), (6, 7), (7, 8)]
 TOKEN_PARTS = [[(0, 3 * P), (3 * P, T)], [(0, 2 * P), (2 * P, 4 * P), (4 * P, T)]]
 
@@ -47,10 +47,11 @@ def tile_moe_ecr_mlp_gelu_kernel(
             return keep.tile(shape, dtype, name=name, tag=place or name, align_bytes=64)
 
         x_rows = xT.rearrange("(p j) t -> p j t", j=PACK)
-        x_raw = []
-        for chunk, (a, b) in enumerate(X_CHUNKS):
-            x_raw.append(sb(f"x_raw{chunk}", [P, PACK, b - a], F32))
-            nc.sync.dma_start(x_raw[chunk][:], x_rows[:, :, a:b])
+        x_all = sb("x_raw", [P, PACK, T], F32)
+        nc.sync.dma_start(x_all[:, :2, :], x_rows[:, :2, :])
+        for a, b in X_CHUNKS:
+            nc.sync.dma_start(x_all[:, 2:, a:b], x_rows[:, 2:, a:b])
+        x_raw = [x_all[:, :, a:b] for a, b in X_CHUNKS]
         offs_sb = keep.tile([P, S // PER_COLUMN], U16, name="offs_sb")
         nc.sync.dma_start(offs_sb[:], offs)
 
@@ -79,10 +80,9 @@ def tile_moe_ecr_mlp_gelu_kernel(
         words_1 = load_words("w1_from1", w1_words, 1, 2)
         words_2_3 = load_words("w1_from2", w1_words, 2, 4)
         plane_rest = load_plane("w1_plane_rest", w1_scales, 4, E)
-        words_4_5 = load_words("w1_from4", w1_words, 4, 6)
-        words_6_7 = load_words("w1_from6", w1_words, 6, E)
+        words_4_7 = load_words("w1_from4", w1_words, 4, E)
         w1_plane = by_expert(plane_first, plane_rest)
-        w1 = by_expert(words_0, words_1, words_2_3, words_4_5, words_6_7)
+        w1 = by_expert(words_0, words_1, words_2_3, words_4_7)
         w2_plane = by_expert(load_plane("w2_plane", w2_scales, 0, E))
         w2 = by_expert(load_words("w2_all", w2_words, 0, E))
         pos = []
@@ -123,9 +123,9 @@ def tile_moe_ecr_mlp_gelu_kernel(
 
         def round_x(chunk):
             a, b = X_CHUNKS[chunk]
-            runs_on_vector = (b - a) * X_EIGHTHS_ON_VECTOR // 8 // 4
+            runs_on_vector = (b - a) * X_SIXTEENTHS_ON_VECTOR // 16 // 4
             dst = x_bf[chunk][:].rearrange("p (c i) j -> p c j i", i=4)
-            src = x_raw[chunk][:].rearrange("p j (c i) -> p c j i", i=4)
+            src = x_raw[chunk].rearrange("p j (c i) -> p c j i", i=4)
             nc.vector.tensor_copy(dst[:, :runs_on_vector], src[:, :runs_on_vector])
             nc.scalar.activation(dst[:, runs_on_vector:], src[:, runs_on_vector:], COPY)
 
@@ -138,8 +138,8 @@ def tile_moe_ecr_mlp_gelu_kernel(
             )
 
         round_x(0)
-        quantise_x(0)
         round_x(1)
+        quantise_x(0)
         round_x(2)
         quantise_x(1)
         quantise_x(2)

@@ -284,6 +284,7 @@ def tile_moe_ecr_mlp_gelu_kernel(
         second_layer(0, 2, 4, on_scalar)
         second_layer(0, 4, 5, on_vector)
         second_layer(0, 6, 7, on_vector)
+        second_layer(1, 0, 2, on_scalar)
         second_layer(0, 5, 6, on_vector)
         second_layer(0, 7, 8, on_scalar)
 
@@ -351,8 +352,8 @@ def tile_moe_ecr_mlp_gelu_kernel(
                 nc.tensor.transpose(backs[half, part][:, t0 : t0 + P], flipped[half, part][:, t0 : t0 + P], ident[:])
 
         fetch(0, 0)
-        second_layer(1, 0, 4, on_scalar)
-        second_layer(1, 4, 8, on_scalar)
+        second_layer(1, 2, 5, on_scalar)
+        second_layer(1, 5, 8, on_scalar)
         fetch(1, 1)
         fetch(1, 2)
         for half in range(2):
@@ -391,7 +392,8 @@ def tile_moe_ecr_mlp_gelu_kernel(
         for part in range(3):
             empty(1, part)
             turn_back(1, part)
-        fetch_times_gate(1, 0, "fetched11")
+        fetch_times_gate(1, 0, "fetched11", end=BANK)
+        nc.vector.tensor_tensor(tails[1, 0], y[1][:].indirect(entries(0, BANK, T)), gates[0][:, BANK:], MULT)
         for part, (a, b) in enumerate(TOKEN_PARTS[1]):
             result = sb(f"result1_{a}", [P, b - a], F32)
             nc.vector.tensor_tensor(result[:], backs[1, part][:, : b - a], products[1, 0][:, a:b], ADD)

@@ -27,7 +27,6 @@ MULT = mybir.AluOpType.mult
 ADD = mybir.AluOpType.add
 
 X_CHUNKS = [(0, 256), (256, 512), (512, 640)]
-X_SIXTEENTHS_ON_VECTOR = 9
 GATHER_GROUPS = [(0, 1), (1, 2), (2, 4), (4, 5), (5, 6), (6, 7), (7, 8)]
 TOKEN_PARTS = [[(0, 3 * P), (3 * P, T)], [(0, 2 * P), (2 * P, 4 * P), (4 * P, T)]]
 
@@ -48,8 +47,11 @@ def tile_moe_ecr_mlp_gelu_kernel(
 
         x_rows = xT.rearrange("(p j) t -> p j t", j=PACK)
         x_all = sb("x_raw", [P, PACK, T], F32)
-        nc.sync.dma_start(x_all[:, :2, :], x_rows[:, :2, :])
-        for a, b in X_CHUNKS:
+        first = X_CHUNKS[0][1]
+        x_run, x_all_run = xT.rearrange("(p j) t -> p (j t)", j=PACK), x_all[:].rearrange("p j t -> p (j t)")
+        nc.sync.dma_start(x_all_run[:, : 2 * T + first], x_run[:, : 2 * T + first])
+        nc.sync.dma_start(x_all[:, 3, :first], x_rows[:, 3, :first])
+        for a, b in X_CHUNKS[1:]:
             nc.sync.dma_start(x_all[:, 2:, a:b], x_rows[:, 2:, a:b])
         x_raw = [x_all[:, :, a:b] for a, b in X_CHUNKS]
         offs_sb = keep.tile([P, S // PER_COLUMN], U16, name="offs_sb")
@@ -121,28 +123,28 @@ def tile_moe_ecr_mlp_gelu_kernel(
         x_words = sb("x_words", [P, T], U32)
         x_bf = [sb(f"x_bf{chunk}", [P, b - a, PACK], BF16) for chunk, (a, b) in enumerate(X_CHUNKS)]
 
-        def round_x(chunk):
-            a, b = X_CHUNKS[chunk]
-            runs_on_vector = (b - a) * X_SIXTEENTHS_ON_VECTOR // 16 // 4
+        def round_x(chunk, cuts):
             dst = x_bf[chunk][:].rearrange("p (c i) j -> p c j i", i=4)
             src = x_raw[chunk].rearrange("p j (c i) -> p c j i", i=4)
-            nc.vector.tensor_copy(dst[:, :runs_on_vector], src[:, :runs_on_vector])
-            nc.scalar.activation(dst[:, runs_on_vector:], src[:, runs_on_vector:], COPY)
+            for a, b in zip([0] + cuts, cuts):
+                nc.vector.tensor_copy(dst[:, a // 4 : b // 4], src[:, a // 4 : b // 4])
+            nc.scalar.activation(dst[:, cuts[-1] // 4 :], src[:, cuts[-1] // 4 :], COPY)
 
-        def quantise_x(chunk):
-            a, b = X_CHUNKS[chunk]
+        def quantise_x(chunk, a, b):
+            first = X_CHUNKS[chunk][0]
             nc.vector.quantize_mx(
-                out=x_words[:, a:b].bitcast(FP8X4),
-                scales=x_bytes[:, a:b],
-                in_=x_bf[chunk][:].rearrange("p t j -> p (t j)"),
+                out=x_words[:, first + a : first + b].bitcast(FP8X4),
+                scales=x_bytes[:, first + a : first + b],
+                in_=x_bf[chunk][:, a:b].rearrange("p t j -> p (t j)"),
             )
 
-        round_x(0)
-        round_x(1)
-        quantise_x(0)
-        round_x(2)
-        quantise_x(1)
-        quantise_x(2)
+        round_x(0, [128, 192])
+        quantise_x(0, 0, 128)
+        round_x(1, [144])
+        quantise_x(0, 128, 256)
+        round_x(2, [64])
+        quantise_x(1, 0, 256)
+        quantise_x(2, 0, 128)
         regroup_words(0, nc.scalar.copy)
         planes_early = sb("planes_early", [P, 2, H], U8, "x_bf2")
         regroup_plane(planes_early[:, :1], plane_first[:, 1:2])
@@ -356,6 +358,8 @@ def tile_moe_ecr_mlp_gelu_kernel(
         second_layer(1, 5, 8, on_scalar)
         fetch(1, 1)
         fetch(1, 2)
+        fetched_tail = sb("fetched_tail", [P, T - BANK], F32)
+        nc.scalar.activation(fetched_tail[:], y[1][:].indirect(entries(3, BANK, T)), COPY)
         for half in range(2):
             sums[half] = [bank() for part in range(2)]
         for r in range(3):
@@ -386,7 +390,7 @@ def tile_moe_ecr_mlp_gelu_kernel(
         times_gate(1, 2, pieces=2)
         add_up(1, 2, final=True, parts=(0, 1))
         tails[1, 3] = sb("tail13", [P, T - BANK], F32)[:]
-        nc.vector.tensor_tensor(tails[1, 3], y[1][:].indirect(entries(3, BANK, T)), gates[3][:, BANK:], MULT)
+        nc.vector.tensor_tensor(tails[1, 3], fetched_tail[:], gates[3][:, BANK:], MULT)
         add_up(1, 2, parts=(2,))
         add_up(1, 3, final=True, parts=(2,))
         for part in range(3):

@@ -78,13 +78,12 @@ def tile_moe_ecr_mlp_gelu_kernel(
             return [tile[:, e, :] for tile in tiles for e in range(tile.shape[1])]
 
         plane_first = load_plane("w1_plane", w1_scales, 0, 4)
-        words_0 = load_words("w1_from0", w1_words, 0, 1)
-        words_1 = load_words("w1_from1", w1_words, 1, 2)
+        words_0_1 = load_words("w1_from0", w1_words, 0, 2)
         words_2_3 = load_words("w1_from2", w1_words, 2, 4)
         plane_rest = load_plane("w1_plane_rest", w1_scales, 4, E)
         words_4_7 = load_words("w1_from4", w1_words, 4, E)
         w1_plane = by_expert(plane_first, plane_rest)
-        w1 = by_expert(words_0, words_1, words_2_3, words_4_7)
+        w1 = by_expert(words_0_1, words_2_3, words_4_7)
         w2_plane = by_expert(load_plane("w2_plane", w2_scales, 0, E))
         w2 = by_expert(load_words("w2_all", w2_words, 0, E))
         pos = []
@@ -93,9 +92,10 @@ def tile_moe_ecr_mlp_gelu_kernel(
             nc.sync.dma_start(pos[r][:], source)
         gate_columns = sb("gate_columns", [P, 3, 2 * PACK], F32)
         nc.sync.dma_start(gate_columns[:, :, :PACK], gate[:3, 0, :BANK].rearrange("r (p c) -> p r c", c=PACK))
-        gate_sb = sb("gate_sb", [P, TOP, T], F32)
-        nc.sync.dma_start(gate_sb[:], gate[:, :P, :].rearrange("r p t -> p r t"))
-        gates = by_expert(gate_sb)
+        gate_first, gate_last = sb("gate_first", [P, TOP - 1, T], F32), sb("gate_last", [P, 1, T], F32)
+        nc.sync.dma_start(gate_first[:], gate[1:, :P, :].rearrange("r p t -> p r t"))
+        nc.sync.dma_start(gate_last[:], gate[:1, :P, :].rearrange("r p t -> p r t"))
+        gates = by_expert(gate_last, gate_first)
 
         x_bytes = sb("x_bytes", [P, T], U8)
         nc.vector.memset(x_bytes[:].bitcast(I32), 0)
@@ -253,7 +253,7 @@ def tile_moe_ecr_mlp_gelu_kernel(
         on_vector, on_scalar = nc.vector.tensor_copy, nc.scalar.copy
         for e0, e1 in ((0, 2), (2, 4), (4, 5), (5, 6), (6, 8)):
             group(e0, e1)
-        first_layer(0, "w1_from1")
+        first_layer(0)
         first_layer_sorted(1)
         first_layer(2)
         late = sb("late", [P, 2, 3 * H], U8, "w1_from0")

from contextlib import ExitStack

import concourse.mybir as mybir
from concourse.masks import make_identity

K, T, E, C, H, N = 512, 640, 8, 128, 512, 256
TOP, PAD = 4, 64
S = E * C
P = 128
BANK = 512
PACK = 4
PER_COLUMN = 16
SORTED = [1, 3, 6, 7]
FLOPS = 2 * S * (K * H + H * N)

F32 = mybir.dt.float32
BF16 = mybir.dt.bfloat16
I32 = mybir.dt.int32
U32 = mybir.dt.uint32
U16 = mybir.dt.uint16
U8 = mybir.dt.uint8
FP8X4 = mybir.dt.float8_e4m3fn_x4
FP4X4 = mybir.dt.float4_e2m1fn_x4
GELU = mybir.ActivationFunctionType.Gelu_apprx_tanh
COPY = mybir.ActivationFunctionType.Copy
MULT = mybir.AluOpType.mult
ADD = mybir.AluOpType.add

X_CHUNKS = [(0, 256), (256, 512), (512, 640)]
GATHER_GROUPS = [(0, 1), (1, 2), (2, 4), (4, 5), (5, 6), (6, 7), (7, 8)]
TOKEN_PARTS = [[(0, 3 * P), (3 * P, T)], [(0, 2 * P), (2 * P, 4 * P), (4 * P, T)]]


def tile_moe_ecr_mlp_gelu_kernel(
    tc, xT, w1_words, w1_scales, w2_words, w2_scales, gate, offs, pos1, pos2, pos3, pos4, out
):
    nc = tc.nc
    with ExitStack() as ctx:
        keep = ctx.enter_context(tc.tile_pool(name="keep", bufs=1))
        psum = ctx.enter_context(tc.psum_pool(name="psum", bufs=8))

        def bank():
            return psum.tile([P, BANK], F32, name="bank")

        def sb(name, shape, dtype, place=None):
            return keep.tile(shape, dtype, name=name, tag=place or name, align_bytes=64)

        x_rows = xT.rearrange("(p j) t -> p j t", j=PACK)
        x_all = sb("x_raw", [P, PACK, T], F32)
        first = X_CHUNKS[0][1]
        x_run, x_all_run = xT.rearrange("(p j) t -> p (j t)", j=PACK), x_all[:].rearrange("p j t -> p (j t)")
        nc.sync.dma_start(x_all_run[:, : 2 * T + first], x_run[:, : 2 * T + first])
        nc.sync.dma_start(x_all[:, 3, :first], x_rows[:, 3, :first])
        for a, b in X_CHUNKS[1:]:
            nc.sync.dma_start(x_all[:, 2:, a:b], x_rows[:, 2:, a:b])
        x_raw = [x_all[:, :, a:b] for a, b in X_CHUNKS]
        offs_sb = keep.tile([P, S // PER_COLUMN], U16, name="offs_sb")
        nc.sync.dma_start(offs_sb[:], offs)

        def load_plane(name, source, e0, e1):
            tile = sb(name, [P, e1 - e0, source.shape[3]], U8)
            nc.vector.memset(tile[:].bitcast(I32), 0)
            for row in range(4):
                nc.sync.dma_start(
                    tile[row:P:32].bitcast(I32),
                    source[e0:e1, 0, row:16:4, :].bitcast(I32).rearrange("e q w -> q e w"),
                )
            return tile

        def load_words(name, source, e0, e1):
            tile = sb(name, [P, e1 - e0, source.shape[3]], U8)
            nc.sync.dma_start(
                tile[:].bitcast(I32), source[e0:e1, 0].bitcast(I32).rearrange("e p w -> p e w")
            )
            return tile

        def by_expert(*tiles):
            return [tile[:, e, :] for tile in tiles for e in range(tile.shape[1])]

        plane_first = load_plane("w1_plane", w1_scales, 0, 4)
        words_0_1 = load_words("w1_from0", w1_words, 0, 2)
        words_2_3 = load_words("w1_from2", w1_words, 2, 4)
        plane_rest = load_plane("w1_plane_rest", w1_scales, 4, E)
        words_4_7 = load_words("w1_from4", w1_words, 4, E)
        w1_plane = by_expert(plane_first, plane_rest)
        w1 = by_expert(words_0_1, words_2_3, words_4_7)
        w2_plane = by_expert(load_plane("w2_plane", w2_scales, 0, E))
        w2 = by_expert(load_words("w2_all", w2_words, 0, E))
        pos = []
        for r, source in enumerate((pos1, pos2, pos3, pos4)):
            pos.append(keep.tile([P, T // PER_COLUMN], U16, name=f"pos_sb{r}"))
            nc.sync.dma_start(pos[r][:], source)
        gate_columns = sb("gate_columns", [P, 3, 2 * PACK], F32)
        nc.sync.dma_start(gate_columns[:, :, :PACK], gate[:3, 0, :BANK].rearrange("r (p c) -> p r c", c=PACK))
        gate_first, gate_last = sb("gate_first", [P, TOP - 1, T], F32), sb("gate_last", [P, 1, T], F32)
        nc.sync.dma_start(gate_first[:], gate[1:, :P, :].rearrange("r p t -> p r t"))
        nc.sync.dma_start(gate_last[:], gate[:1, :P, :].rearrange("r p t -> p r t"))
        gates = by_expert(gate_last, gate_first)

        x_bytes = sb("x_bytes", [P, T], U8)
        nc.vector.memset(x_bytes[:].bitcast(I32), 0)
        y = [sb(f"y{half}", [P, S + PAD], F32) for half in range(2)]
        nc.vector.memset(y[1][:, S:], 0.0)
        nc.scalar.activation(y[0][:, S:], y[1][:, S:], GELU)
        ident = sb("ident", [P, P], F32)
        make_identity(nc, ident[:])

        words_early = sb("words_early", [P, 2, H], U16)
        w1_sorted = by_expert(words_early)
        def regroup_plane(regrouped, plane):
            nc.gpsimd.tensor_copy(
                regrouped.rearrange("p e (t m) -> p e t m", t=PACK),
                plane.rearrange("p e (m t) -> p e t m", t=PACK),
            )

        def regroup_words(s, copy):
            copy(
                w1_sorted[s].rearrange("p (t m) -> p t m", t=PACK),
                w1[SORTED[s]].bitcast(U16).rearrange("p (m t) -> p t m", t=PACK),
            )


        x_words = sb("x_words", [P, T], U32)
        x_bf = [sb(f"x_bf{chunk}", [P, b - a, PACK], BF16) for chunk, (a, b) in enumerate(X_CHUNKS)]

        def round_x(chunk, cuts):
            dst = x_bf[chunk][:].rearrange("p (c i) j -> p c j i", i=4)
            src = x_raw[chunk].rearrange("p j (c i) -> p c j i", i=4)
            for a, b in zip([0] + cuts, cuts):
                nc.vector.tensor_copy(dst[:, a // 4 : b // 4], src[:, a // 4 : b // 4])
            nc.scalar.activation(dst[:, cuts[-1] // 4 :], src[:, cuts[-1] // 4 :], COPY)

        def quantise_x(chunk, a, b):
            first = X_CHUNKS[chunk][0]
            nc.vector.quantize_mx(
                out=x_words[:, first + a : first + b].bitcast(FP8X4),
                scales=x_bytes[:, first + a : first + b],
                in_=x_bf[chunk][:, a:b].rearrange("p t j -> p (t j)"),
            )

        round_x(0, [128, 192])
        quantise_x(0, 0, 128)
        round_x(1, [144])
        quantise_x(0, 128, 256)
        round_x(2, [64])
        quantise_x(1, 0, 256)
        quantise_x(2, 0, 128)
        regroup_words(0, nc.scalar.copy)
        planes_early = sb("planes_early", [P, 2, H], U8, "x_bf2")
        regroup_plane(planes_early[:, :1], plane_first[:, 1:2])
        regroup_plane(planes_early[:, 1:], plane_first[:, 3:4])
        regroup_words(1, nc.gpsimd.tensor_copy)
        plane_sorted = by_expert(planes_early)
        slot_words = sb("slot_words", [P, S], U32)
        slot_bytes = sb("slot_bytes", [P, S], U8)

        def gather(slots, tokens, e0, e1):
            entries = offs_sb[:, e0 * C // PER_COLUMN : e1 * C // PER_COLUMN]
            nc.vector.tensor_copy(slots[:, e0 * C : e1 * C], tokens[:].indirect(entries))

        for e0, e1 in GATHER_GROUPS:
            gather(slot_bytes, x_bytes, e0, e1)
            for e in range(e0, e1):
                gather(slot_words, x_words, e, e + 1)

        h_bf, turned, h_grouped, h_words = {}, {}, {}, {}
        h_bytes = sb("h_bytes", [P, S], U8)

        def group(e0, e1, place=None):
            tile = sb(f"h_grouped{e0}", [P, e1 - e0, C * PACK], BF16, place)
            for e in range(e0, e1):
                h_grouped[e] = (tile, e - e0)

        def grouped(e0, e1):
            tile, first = h_grouped[e0]
            return tile[:, first : first + e1 - e0].rearrange("p e w -> p (e w)")

        def first_layer(e, place=None):
            slots = slice(e * C, (e + 1) * C)
            acc = bank()
            nc.tensor.matmul_mx(
                out=acc[:],
                lhsT=slot_words[:, slots].bitcast(FP8X4),
                lhsT_scale=slot_bytes[:, slots],
                rhs=w1[e].bitcast(FP4X4),
                rhs_scale=w1_plane[e],
                start=True,
                stop=True,
            )
            h_bf[e] = sb(f"h_bf{e}", [P, H], BF16, place)
            nc.scalar.activation(
                h_bf[e][:].rearrange("s (u p d) -> s u p d", u=2, d=2),
                acc[:].rearrange("s (p u d) -> s u p d", u=2, d=2),
                GELU,
            )

        def first_layer_sorted(e):
            slots = slice(e * C, (e + 1) * C)
            acc = bank()
            for t in range(PACK):
                nc.tensor.matmul_mx(
                    out=acc[:, t * C : (t + 1) * C],
                    lhsT=w1_sorted[SORTED.index(e)][:, t * P : (t + 1) * P].bitcast(FP4X4),
                    lhsT_scale=plane_sorted[SORTED.index(e)][:, t * P : (t + 1) * P],
                    rhs=slot_words[:, slots].bitcast(FP8X4),
                    rhs_scale=slot_bytes[:, slots],
                    start=True,
                    stop=True,
                )
            nc.scalar.activation(
                grouped(e, e + 1).rearrange("p (s t) -> p s t", t=PACK),
                acc[:].rearrange("p (t s) -> p s t", t=PACK),
                GELU,
            )

        def turn(e, e0):
            if e == e0:
                turned[e0] = bank()
            pairs = h_bf[e][:].bitcast(F32)
            for u in range(2):
                col = (2 * (e - e0) + u) * C
                nc.tensor.transpose(turned[e0][:, col : col + C], pairs[:, u * P : (u + 1) * P], ident[:])

        def interleave(e0, e1, copy):
            copy(
                grouped(e0, e1).bitcast(F32).rearrange("p (e s u) -> p e s u", s=C, u=2),
                turned[e0][:, : (e1 - e0) * 2 * C].rearrange("p (e u s) -> p e s u", s=C, u=2),
            )

        def quantise_h(e0, e1, place=None):
            words = sb(f"h_words{e0}", [P, (e1 - e0) * C], U32, place)
            nc.vector.quantize_mx(
                out=words[:].bitcast(FP8X4), scales=h_bytes[:, e0 * C : e1 * C], in_=grouped(e0, e1)
            )
            for e in range(e0, e1):
                h_words[e] = words[:, (e - e0) * C : (e - e0 + 1) * C]

        def second_layer(half, e0, e1, copy):
            acc = bank()
            for e in range(e0, e1):
                slots = slice(e * C, (e + 1) * C)
                nc.tensor.matmul_mx(
                    out=acc[:, (e - e0) * C : (e - e0 + 1) * C],
                    lhsT=w2[e][:, 2 * half * P : 2 * (half + 1) * P].bitcast(FP4X4),
                    lhsT_scale=w2_plane[e][:, half * P : (half + 1) * P],
                    rhs=h_words[e].bitcast(FP8X4),
                    rhs_scale=h_bytes[:, slots],
                    start=True,
                    stop=True,
                )
            copy(y[half][:, e0 * C : e1 * C], acc[:, : (e1 - e0) * C])

        on_vector, on_scalar = nc.vector.tensor_copy, nc.scalar.copy
        for e0, e1 in ((0, 2), (2, 4), (4, 5), (5, 6), (6, 8)):
            group(e0, e1)
        first_layer(0)
        first_layer_sorted(1)
        first_layer(2)
        late = sb("late", [P, 2, 3 * H], U8, "w1_from0")
        planes_late = late[:, :, :H]
        w1_sorted.extend(by_expert(late[:, :, H:].bitcast(U16)))
        regroup_plane(planes_late, plane_rest[:, 2:])
        regroup_words(2, nc.gpsimd.tensor_copy)
        regroup_words(3, nc.gpsimd.tensor_copy)
        plane_sorted.extend(by_expert(planes_late))
        first_layer_sorted(3)
        first_layer(4)
        turn(0, 0)
        first_layer(5)
        turn(2, 2)
        turn(4, 4)
        first_layer_sorted(6)
        first_layer_sorted(7)
        turn(5, 5)
        interleave(0, 1, on_vector)
        interleave(2, 3, on_vector)
        interleave(4, 5, on_vector)
        quantise_h(0, 2, "h_bf4")
        quantise_h(2, 4)
        quantise_h(4, 5)
        interleave(5, 6, on_vector)
        quantise_h(6, 7)
        quantise_h(5, 6)
        quantise_h(7, 8)
        second_layer(0, 0, 2, on_scalar)
        second_layer(0, 2, 4, on_scalar)
        second_layer(0, 4, 5, on_vector)
        second_layer(0, 6, 7, on_vector)
        second_layer(1, 0, 2, on_scalar)
        second_layer(0, 5, 6, on_vector)
        second_layer(0, 7, 8, on_scalar)

        products, tails, fetched, spread = {}, {}, {}, {}

        def entries(r, a, b):
            return pos[r][:, a // PER_COLUMN : b // PER_COLUMN]

        def fetch_times_gate(half, r, place=None, end=T):
            products[half, r] = sb(f"products{half}{r}", [P, T], F32, place)
            tails[half, r] = products[half, r][:, BANK:]
            nc.vector.tensor_tensor(
                products[half, r][:, :end], y[half][:].indirect(entries(r, 0, end)), gates[r][:, :end], MULT
            )

        def fetch(half, r):
            fetched[half, r] = sb(f"fetched{half}{r}", [P, T], F32)
            nc.scalar.activation(fetched[half, r][:], y[half][:].indirect(pos[r][:]), COPY)

        def spread_gate(r):
            spread[r] = bank()
            for c in range(PACK):
                nc.tensor.transpose(
                    spread[r][:, c * P : (c + 1) * P], gate_columns[:, r, c : c + 1].to_broadcast([P, P]), ident[:]
                )

        def times_gate(half, r, pieces=1):
            step = P // pieces
            for p0 in range(0, P, step):
                nc.vector.tensor_tensor(
                    products[half, r][:, :BANK].rearrange("n (p c) -> n p c", c=PACK)[:, p0 : p0 + step],
                    fetched[half, r][:, :BANK].rearrange("n (p c) -> n p c", c=PACK)[:, p0 : p0 + step],
                    spread[r][:].rearrange("n (c p) -> n p c", c=PACK)[:, p0 : p0 + step],
                    MULT,
                )
            nc.gpsimd.tensor_tensor(tails[half, r], fetched[half, r][:, BANK:], gates[r][:, BANK:], MULT)

        sums = {}

        def add_up(half, r, first=False, final=False, parts=None):
            for part, (a, b) in enumerate(TOKEN_PARTS[half]):
                for t0 in range(a, b, P) if parts is None or part in parts else ():
                    nc.tensor.matmul(
                        sums[half][part][:, t0 - a : t0 - a + P],
                        products[half, r][:, t0 : t0 + P] if t0 < BANK else tails[half, r],
                        ident[:],
                        start=(first and t0 == a),
                        stop=(final and t0 == b - P),
                        is_transpose=True,
                    )

        backs = {}

        flipped = {}

        def empty(half, part):
            a, b = TOKEN_PARTS[half][part]
            flipped[half, part] = sb(f"flipped{half}_{a}", [P, b - a], F32)
            nc.scalar.copy(flipped[half, part][:], sums[half][part][:, : b - a])

        def turn_back(half, part):
            a, b = TOKEN_PARTS[half][part]
            backs[half, part] = bank()
            for t0 in range(0, b - a, P):
                nc.tensor.transpose(backs[half, part][:, t0 : t0 + P], flipped[half, part][:, t0 : t0 + P], ident[:])

        fetch(0, 0)
        second_layer(1, 2, 5, on_scalar)
        second_layer(1, 5, 8, on_scalar)
        fetch(1, 1)
        fetch(1, 2)
        fetched_tail = sb("fetched_tail", [P, T - BANK], F32)
        nc.scalar.activation(fetched_tail[:], y[1][:].indirect(entries(3, BANK, T)), COPY)
        for half in range(2):
            sums[half] = [bank() for part in range(2)]
        for r in range(3):
            spread_gate(r)
        sums[1].append(bank())
        for r in (3, 2, 1):
            fetch_times_gate(0, r)
            add_up(0, r, first=(r == 3))
        products[0, 0] = sb("products00", [P, BANK], F32, "products03")
        products[1, 1] = sb("products11", [P, BANK + 2 * P], F32, "products02")
        products[1, 2] = sb("products12", [P, T], F32, "products01")
        tails[0, 0] = products[1, 1][:, BANK : BANK + P]
        tails[1, 1] = products[1, 1][:, BANK + P :]
        tails[1, 2] = products[1, 2][:, BANK:]
        times_gate(0, 0)
        add_up(0, 0, final=True)
        times_gate(1, 1)
        add_up(1, 1, first=True)
        for part in range(2):
            empty(0, part)
        result0 = sb("result0", [P, T], F32)
        for part, (a, b) in enumerate(TOKEN_PARTS[0]):
            turn_back(0, part)
            nc.scalar.copy(result0[:, a:b], backs[0, part][:, : b - a])
        nc.sync.dma_start(out[:P], result0[:])
        fetch_times_gate(1, 3, "fetched00", end=BANK)
        add_up(1, 3, parts=(0, 1))
        times_gate(1, 2, pieces=2)
        add_up(1, 2, final=True, parts=(0, 1))
        tails[1, 3] = sb("tail13", [P, T - BANK], F32)[:]
        nc.vector.tensor_tensor(tails[1, 3], fetched_tail[:], gates[3][:, BANK:], MULT)
        add_up(1, 2, parts=(2,))
        add_up(1, 3, final=True, parts=(2,))
        for part in range(3):
            empty(1, part)
            turn_back(1, part)
        fetch_times_gate(1, 0, "fetched11", end=BANK)
        nc.vector.tensor_tensor(tails[1, 0], y[1][:].indirect(entries(0, BANK, T)), gates[0][:, BANK:], MULT)
        for part, (a, b) in enumerate(TOKEN_PARTS[1]):
            result = sb(f"result1_{a}", [P, b - a], F32)
            nc.vector.tensor_tensor(result[:], backs[1, part][:, : b - a], products[1, 0][:, a:b], ADD)
            nc.sync.dma_start(out[P:, a:b], result[:])
